import numpy as np, ml_dtypes
CORES = [66,74,82,90,194,202,210,218]
N = 8
import mx_ref
BF = ml_dtypes.bfloat16
def gentries(a):
    return np.ascontiguousarray(a.reshape(8, 16, -1).transpose(0, 2, 1)).reshape(8, -1)
def gtable(e):
    e = np.asarray(e); return np.ascontiguousarray(e.reshape(8, -1, 16).transpose(0, 2, 1)).reshape(128, -1).astype(np.int32)
def gcols(t, e):
    v = np.concatenate([t.reshape(8, 16, -1, 4), np.zeros((8, 16, 1, 4), BF)], axis=2)
    return np.ascontiguousarray(np.stack([v[g][:, e[g]] for g in range(8)])).reshape(128, -1)
def tile(rs):
    return np.stack(rs, axis=2).reshape(128, -1).astype(BF)
def pick(q, e):
    c = np.concatenate([q[0].reshape(128, -1, 4), np.zeros((128, 1, 4), np.uint8)], axis=1); s = np.concatenate([q[1], np.ones((16, 1), np.uint8)], axis=1)
    return (np.ascontiguousarray(c[:, e].reshape(128, -1)), np.ascontiguousarray(s[:, e]))
def join(*qs):
    return (np.concatenate([q[0] for q in qs], axis=1), np.concatenate([q[1] for q in qs], axis=1))
def put(q, e, v):
    c, s = q[0].reshape(128, -1, 4).copy(), q[1].copy(); c[:, e] = v[0].reshape(128, -1, 4); s[:, e] = v[1]
    return (c.reshape(128, -1), s)
def pk(c, s):
    return (np.ascontiguousarray(c), mx_ref.live(s))
def emit(q):
    return q[0], q[1]
def packed(v, rng):
    q = [mx_ref.quantize(np.ascontiguousarray(v[r])) for r in range(N)]
    return np.stack([a for a, b in q]), np.stack([mx_ref.plane(b, rng) for a, b in q])
def values_of_codes():
    e, c = np.zeros((128, 128, 4), np.float32), np.zeros((128, 2, 4), np.uint8)
    e[np.arange(128), np.arange(128), 0] = 1
    c[:127, :, 0] = np.arange(256).reshape(2, 128).T[:127]
    return mx_ref.matmul(mx_ref.quantize(e.reshape(128, 512).astype(BF)), (c.reshape(128, 8), np.full((16, 2), 127, np.uint8))).T.reshape(-1).astype(np.float64)
CODE_VALUE, SCALE_VALUE = values_of_codes(), 2.0 ** (np.arange(256) - 127.0)
def decode(q):
    return (CODE_VALUE[q[0]].reshape(16, 8, -1, 4) * SCALE_VALUE[q[1]][:, None, :, None] + 0.0).reshape(128, -1).astype(np.float32)
def f(rng, *shape):
    return mx_ref.flush((rng.standard_normal(shape, dtype=np.float32) * np.exp2(rng.integers(-2, 3, shape[:-1] + (1,)))).astype(BF))
def wide(rng, *shape, cols=0):
    v = rng.standard_normal(shape, dtype=np.float32) * np.exp2(rng.integers(-12, 13, shape)).astype(np.float32)
    if cols: v *= np.repeat(np.exp2(rng.integers(-cols, cols + 1, shape[:-2] + (1, shape[-1] // 4))) * (rng.random(shape[:-2] + (1, shape[-1] // 4)) > 0.0625), 4, axis=-1).astype(np.float32)
    return mx_ref.flush(v.astype(BF))
C, E, B, R = 192, 12, 80, 2
L = C + B
M = L - 2 * E - 15
S = np.arange(16)
AT = np.arange(0, E, E // 4)
G = np.arange(8)[:, None, None]
def choose(s, b):
    p, n = b.copy(), b.copy()
    for k in range(1, 16):
        n[:, k] = p[:, k - 1] + E
        c = b[:, k:k + 1] + S
        d = np.max(np.abs(s[G, n[:, k, None, None] + AT] - s[G, c[:, :, None] + AT]), axis=2)
        d[c == n[:, k:k + 1]] = np.inf
        p[:, k] = b[:, k] + np.argmin(d, axis=1)
    return p, n
def places(e):
    return (e[:, :, None] + np.arange(E)).reshape(8, C)
def big(v):
    v = v.astype(np.float32)
    v[np.abs(v) < np.float32(2.0 ** -16)] = 0
    return v.astype(BF)
def numbers_of(rng):
    return {"x": big(f(rng, N, 128, 4 * C)), "u": np.array(f(rng, N, 128, 512)), "v": np.array(f(rng, N, 128, 512))}
def lists_of(rng):
    hop = rng.integers(E - E // 4, E + E // 4 + 1, (N, 8, R, 1))
    return (hop * S + rng.integers(0, M - 15 * (E + E // 4) + 1, (N, 8, R, 16))).reshape(N, 8, 16 * R)
def even(rng, k):
    return (rng.integers(0, M - 15 * E + 1, (k, R, 1)) + E * S).reshape(k, 16 * R)
def halves(rng, k):
    return rng.integers(0, C // 2 - 15 - 2 * E + 1, (k, 16)) + C // 2 * (S % 2)
def stored(l):
    return np.stack([gtable(e) for e in l])
def weights(rng, w):
    c, p = packed(w, rng)
    return {"wc": c, "ws": p}
def layers(rng):
    return weights(rng, f(rng, N, 128, 2048))
def unit(rng, a):
    w = np.zeros((N, 128, 4, 128, 4), np.float32)
    i = np.arange(128)
    for b in range(4): w[:, i, b, i, b] = a
    return weights(rng, w.reshape(N, 128, 2048).astype(BF))
def setup_inputs(rng):
    return {**numbers_of(rng), "st": stored(lists_of(rng)), **layers(rng)}
def setup_inputs_ties(rng):
    d, l = numbers_of(rng), lists_of(rng)
    o = rng.permutation(N)
    x = d["x"].reshape(N, 8, 16, C, 4)
    for r in range(N):
        k = np.zeros(C, int) if r == o[0] else rng.permutation(C) % 3
        a = x[r][:, :8, :3].copy()
        a[:, :, 2] = 0
        x[r][:, :8] = a[:, :, k]
    x[o[1]] = 0
    l[o[0], :2] = even(rng, 2)
    l[o[1], 0] = rng.integers(C, M + 1, 16 * R)
    u = d["u"].reshape(N, 8, 16, 128, 4)
    u[:, :, 8:, ::16] = 0
    return {"x": x.reshape(N, 128, 4 * C), "u": u.reshape(N, 128, 512), "v": d["v"], "st": stored(l), **layers(rng)}
def setup_inputs_near(rng):
    d, l = numbers_of(rng), lists_of(rng)
    o = rng.permutation(N)
    h, j = C // 2, np.arange(C)
    sign, t, tiny = np.ones((N, 8, C)), np.zeros((N, C), int), []
    for r in range(N):
        t[r] = np.where(j < h, h - 1 - j, j - h) if o[r] % 4 < 2 else rng.integers(0, 256, C)
        far = rng.permutation(8) % 2 == 1
        sign[r] = np.where(far[:, None] & (j >= h), -1.0, 1.0)
        l[r, far, :16] = halves(rng, 4)
        if o[r] % 4 == 1:
            e = rng.permutation(np.flatnonzero(~far))[:2]
            l[r, e, :16] = halves(rng, 2)
            tiny += [(r, int(i)) for i in e]
    g = ((t[:, :, None] >> np.arange(8)) & 1) * np.exp2(np.arange(8) - 23.0)
    x = d["x"].astype(np.float32).reshape(N, 8, 16, C, 4)
    x[:, :, 0] = 0
    x[:, :, 0, :, 0] = sign
    x[:, :, 8] = g[:, None, :, :4]
    x[:, :, 9] = g[:, None, :, 4:]
    x[:, :, 10:] = rng.integers(4, 8, (N, 8, 6, C, 4)) * rng.choice([-1.0, 1.0], (N, 8, 6, C, 4)) * 2.0 ** -20
    x *= np.where(o % 2, 2.0 ** -4, 1.0).astype(np.float32)[:, None, None, None, None]
    u = d["u"].reshape(N, 128, 128, 4)
    k = np.where(o % 2, 2.0 ** -30, 1.0).astype(np.float32).astype(BF)
    u[:, :, ::16] = 0
    for i in range(0, 128, 16):
        u[:, i, i, 0] = k
        u[:, i + 8:i + 10, i] = k[:, None, None]
    for r, i in tiny:
        w = t[r] // 8 + 32 * (j < h)
        x[r, i, :8] = 0
        x[r, i, 1, :, 0] = (8 + w % 8) * 2.0 ** -32
        x[r, i, 2, :, 0] = (8 + w % 8) * 2.0 ** -32
        x[r, i, 3, :, 0] = (8 + w // 8) * 2.0 ** -32
        u[r, :, 16 * i] = 0
        u[r, 16 * i + 1:16 * i + 4, 16 * i, 0] = (np.array([-1.0, 1.125, 1.0]) * 2.0 ** -30).astype(np.float32).astype(BF)
    return {"x": x.reshape(N, 128, 4 * C).astype(BF), "u": u.reshape(N, 128, 512), "v": d["v"], "st": stored(l), **unit(rng, 32)}
def setup_inputs_huge(rng):
    d, l = numbers_of(rng), lists_of(rng)
    o = rng.permutation(N)
    a = np.zeros((N, C))
    m = 0.9 + 0.1 * rng.random((N, 128, C, 4))
    k = 0.9 + 0.1 * rng.random((N, 128, 8, 4))
    for r in range(N):
        if o[r] % 2:
            l[r, :, :16] = even(rng, 8)[:, :16]
            if o[r] % 4 == 1:
                i = int(l[r, 0, 1])
                a[r] = rng.choice([-1.0, 1.0], C)
                a[r, i] = 1
                a[r, i + 1:i + 16] = -1
                m[r, :, i:i + 16] = 1
                k[r] = 1
            else:
                a[r] = rng.uniform(-1, 1, C)
        else:
            a[r] = np.where(np.arange(C) < C // 2, 1.0, -1.0)
            l[r, :, :16] = halves(rng, 8)
    x = 2.0 ** 30 * m * a[:, None, :, None]
    g = np.stack([rng.permutation(8) % 2 * 2.0 - 1.0 for r in range(N)])
    u = d["u"].reshape(N, 128, 128, 4)
    u[:, :, ::16] = (2.0 ** 30 * k * g[:, None, :, None]).astype(np.float32).astype(BF)
    return {"x": x.astype(np.float32).reshape(N, 128, 4 * C).astype(BF), "u": u.reshape(N, 128, 512), "v": d["v"], "st": stored(l), **unit(rng, -16)}
def setup_inputs_lists(rng):
    d, l = numbers_of(rng), lists_of(rng)
    for r in range(N):
        g = rng.permutation(8)
        l[r, g[:2]] = rng.integers(0, M + 1, (2, 16 * R))
        l[r, g[2:4]] = M
        l[r, g[4]] = np.sort(rng.integers(0, M + 1, (R, 16)), axis=1)[:, ::-1].reshape(-1)
        l[r, g[5]] = even(rng, 1)[0]
        l[r, g[6]] = rng.integers(C, M + 1, 16 * R)
        l[r, g[7]] = 0
    return {**d, "st": stored(l), **layers(rng)}
def setup_inputs_spread(rng):
    d = setup_inputs(rng)
    d["x"] = big(wide(rng, N, 128, 4 * C, cols=6))
    return d
def check_inputs(d):
    b = []
    for k in ("x", "u", "v"):
        a = np.abs(d[k].astype(np.float32))
        if not (np.isfinite(a).all() and ((a == 0) | (a >= 2.0 ** -30) & (a <= 2.0 ** 30)).all()): b.append("a value of " + k)
    if ((d["st"] < 0) | (d["st"] > M)).any(): b.append("an entry of st")
    return b
def reference(x, u, v, st, wc, ws):
    qu = [mx_ref.quantize(u[r]) for r in range(N)]
    lay = [pk(wc[r], ws[r]) for r in range(N)]
    first = [gentries(st[r]).astype(np.int64) for r in range(N)]
    now = [x[r] for r in range(N)]
    y, ol = np.zeros((N, 128, C), np.float32), np.zeros((N, 8, 16 * R), np.float32)
    oc, osc = np.zeros((N, 128, 4 * C), np.uint8), np.zeros((N, 16, C), np.uint8)
    for t in range(R):
        q = [mx_ref.quantize(now[r]) for r in range(N)]
        now = []
        for r in range(N):
            window = join(q[r], pick(q[(r + 1) % N], np.arange(B)))
            p, n = choose(mx_ref.matmul(qu[r], window)[::16], first[r][:, 16 * t:16 * t + 16])
            ol[r, :, 16 * t:16 * t + 16] = p
            d = decode(window).astype(BF)
            z = (gcols(d, places(n)).astype(np.float32) + gcols(d, places(p)).astype(np.float32)) * np.float32(0.5)
            qz = mx_ref.quantize(z.astype(BF))
            w = lay[(r + 1 + t) % N]
            h = tile([mx_ref.matmul(pick(w, np.arange(128 * b, 128 * b + 128)), qz) * np.float32(0.03125) for b in range(4)])
            now.append((decode(qz) + decode(mx_ref.quantize(h))).astype(BF))
    for r in range(N):
        q = mx_ref.quantize(now[r])
        y[r] = mx_ref.matmul(mx_ref.quantize(v[r]), q)
        oc[r], osc[r] = emit(q)
    return {"y": y, "ol": ol, "oc": oc, "osc": osc}

@@ -1,0 +1,665 @@
+from concourse.bass import DstId, RemoteDMATransfer
+from concourse.mybir import dt, AluOpType, ActivationFunctionType
+
+F32, BF, I32, U16, CODE, U8 = "float32", "bfloat16", "int32", "uint16", "float8_e4m3fn_x4", "uint8"
+SPLIT = (7, 7)
+NA, NB, NH = 84, 108, 80
+ZB = 136
+BIG = 5.0e29
+EXCL = 1.0e29
+BIAS = 176
+HC = 128
+WS0 = 128
+PLANS = ({"cyc": 0.00104, "gat": 0.00125, "wake": 0.08, "halo0": 4.5, "halo1": 3.6, "w0": 12.5, "w1": 22.0},
+         {"cyc": 0.00090, "gat": 0.00100, "wake": 0.05, "halo0": 3.5, "halo1": 2.8, "w0": 10.5, "w1": 18.0},
+         {"cyc": 0.00115, "gat": 0.00155, "wake": 0.14, "halo0": 5.5, "halo1": 4.4, "w0": 14.5, "w1": 25.0})
+TRIES = 5000
+STORE = 2.4
+
+SCRATCH = {
+    "xa": ("sbuf", [128, 528], BF), "xb": ("sbuf", [128, 512], BF),
+    "za": ("sbuf", [128, 528], BF), "zb": ("sbuf", [128, 512], BF),
+    "ha": ("sbuf", [128, 528], BF), "hb": ("sbuf", [128, 512], BF),
+    "ut": ("sbuf", [128, 512], BF), "vt": ("sbuf", [128, 512], BF),
+    "et": ("sbuf", [128, 516], BF),
+    "eq": ("sbuf", [128, 512], CODE), "es": ("sbuf", [128, 512], U8),
+    "uq": ("sbuf", [128, 128], CODE), "us": ("sbuf", [128, 128], U8),
+    "urq": ("sbuf", [128, 128], CODE), "urs": ("sbuf", [128, 128], U8),
+    "vq": ("sbuf", [128, 128], CODE), "vs": ("sbuf", [128, 128], U8),
+    "qv0": ("sbuf", [128, 336], CODE), "sv0": ("sbuf", [128, 336], U8),
+    "qv1": ("sbuf", [128, 336], CODE), "sv1": ("sbuf", [128, 336], U8),
+    "qv2": ("sbuf", [128, 264], CODE), "sv2": ("sbuf", [128, 264], U8),
+    "qz": ("sbuf", [128, 264], CODE), "sz": ("sbuf", [128, 264], U8),
+    "qh": ("sbuf", [128, 264], CODE), "sh": ("sbuf", [128, 264], U8),
+    "wlc": ("sbuf", [128, 512], CODE), "wls": ("sbuf", [128, 512], U8),
+    "whc": ("sbuf", [128, 256], CODE), "whs": ("sbuf", [128, 256], U8),
+    "w0c": ("sbuf", [128, 512], CODE), "w0s": ("sbuf", [128, 512], U8),
+    "w1c": ("sbuf", [128, 512], CODE), "w1s": ("sbuf", [128, 512], U8),
+    "sti": ("sbuf", [128, 2], I32), "stu": ("sbuf", [128, 2], U16),
+    "pi": ("sbuf", [128, 1], I32), "ci": ("sbuf", [128, 8], I32), "cf": ("sbuf", [128, 8], F32),
+    "cx": ("sbuf", [128, 16], F32), "cr": ("sbuf", [128, 48], F32),
+    "iw": ("sbuf", [128, 256], F32), "i8": ("sbuf", [128, 320], F32), "i40": ("sbuf", [128, 40], F32),
+    "m2": ("sbuf", [128, 320], F32), "rs8": ("sbuf", [128, 320], F32),
+    "d1": ("sbuf", [128, 344], F32), "rr": ("sbuf", [128, 160], F32), "p1": ("sbuf", [128, 480], F32),
+    "ex": ("sbuf", [128, 960], BF), "win": ("sbuf", [128, 32], F32),
+    "kb": ("sbuf", [128, 32], F32), "kk": ("sbuf", [128, 32], F32), "bf": ("sbuf", [128, 32], F32),
+    "nd": ("sbuf", [128, 32], F32), "ne": ("sbuf", [128, 32], F32),
+    "ou": ("sbuf", [128, 8], U16), "ob": ("sbuf", [128, 40], U16), "ocd": ("sbuf", [128, 128], U16),
+    "o2": ("sbuf", [128, 64], U16), "oe": ("sbuf", [128, 32], U16), "oz": ("sbuf", [128, 8], U16),
+    "op": ("sbuf", [128, 16], U16), "ch": ("sbuf", [128, 64], U16), "og": ("sbuf", [128, 50], U16),
+    "i1": ("sbuf", [128, 524], F32), "t1": ("sbuf", [128, 524], F32),
+    "g2": ("sbuf", [128, 480], F32), "tt": ("sbuf", [128, 480], F32),
+    "cc": ("sbuf", [128, 960], F32), "df": ("sbuf", [128, 960], F32), "ab": ("sbuf", [128, 960], F32),
+    "mx": ("sbuf", [128, 964], F32), "mm": ("sbuf", [128, 240], F32), "nn": ("sbuf", [128, 240], F32),
+    "pt": ("sbuf", [128, 240], F32), "tb1": ("sbuf", [128, 352], F32), "tb2": ("sbuf", [128, 352], F32),
+    "pf": ("sbuf", [128, 16], F32), "pp": ("sbuf", [128, 32], F32),
+    "dv": ("sbuf", [128, 1088], BF), "tn": ("sbuf", [128, 768], BF), "yb": ("sbuf", [128, 192], F32),
+}
+for _b in range(8):
+    SCRATCH["ps%d" % _b] = ("psum", [128, 512], F32)
+
+SEMAPHORES = ["cv", "cs", "cp", "cg", "sent", "halo0", "halo1", "w0", "w1", "hp0", "hp1", "hp2", "hp3",
+              "lxa", "lxb", "lst", "lu", "lv", "lwh", "lws0", "lws", "lwd", "sta", "stb", "stc"]
+
+ADD, SUB, MUL, MAX, MIN = AluOpType.add, AluOpType.subtract, AluOpType.mult, AluOpType.max, AluOpType.min
+COPY, IDENT, ABS = ActivationFunctionType.Copy, ActivationFunctionType.Identity, ActivationFunctionType.Abs
+SIGN = ActivationFunctionType.Sign
+PLANNED = {}
+
+
+def mask_of(engines):
+    m = 0
+    for e in engines:
+        m |= 1 << e
+    return m
+
+
+def helpers_of(T, topo, r):
+    c, n = T.cores[r], len(T.cores)
+    prev = T.cores[(r - 1) % n]
+    return [h for h in topo.cores_of(c) if topo.die(h) != topo.die(c) and topo.may_write(h, prev) and T.rank_of(h) is None][:2]
+
+
+def bytes_of(view):
+    return view.bitcast(dt.uint8)
+
+
+def helper_columns(i):
+    rest = 256 - HC
+    return (512 - 2 * HC + HC * i, HC), (rest * i, rest)
+
+
+def helper_program(g, core, T, topo, r, i):
+    n = len(T.cores)
+    d1, d2 = T.cores[(r - 1) % n], T.cores[(r - 2) % n]
+    total = [0]
+
+    def send(out, src, sem, dst):
+        rid, pid = topo.addr(dst, core)
+        g.remote_dma(out, src, sem, T.sem.sent, pid, rid, topo.mask(core, dst))
+        total[0] += len(topo.engines(core, dst))
+
+    got = len(spare_engines(T, topo, r)) // 2
+    (a, c), (b, d) = helper_columns(i)
+    first, rest = WS0 // 2, 256 - WS0 // 2
+    g.wait_ge(T.sem.hp0, got)
+    send(T.w1s[:, first * i:first * i + first], T.whs[:, 0:first], T.sem.w1, d2)
+    g.wait_ge(T.sem.hp1, got)
+    send(bytes_of(T.w0c[:, a:a + c]), bytes_of(T.whc[:, 0:c]), T.sem.w0, d1)
+    send(bytes_of(T.w1c[:, a:a + c]), bytes_of(T.whc[:, 0:c]), T.sem.w1, d2)
+    g.wait_ge(T.sem.hp2, got)
+    send(bytes_of(T.w1c[:, b:b + d]), bytes_of(T.whc[:, c:c + d]), T.sem.w1, d2)
+    g.wait_ge(T.sem.hp3, got)
+    send(T.w1s[:, WS0 + rest * i:WS0 + rest * i + rest], T.whs[:, first:256], T.sem.w1, d2)
+    g.wait_ge(T.sem.sent, total[0])
+
+
+def spare_engines(T, topo, r):
+    c = T.cores[r]
+    off = topo.engines(c, T.cores[(r - 1) % len(T.cores)])
+    return [e for e in topo.engines(c, helpers_of(T, topo, r)[0]) if e not in off]
+
+
+def cyc(c):
+    return (0.0, max(64, c), 0)
+
+
+def gat(c):
+    return (0.06, 0, c)
+
+
+def fixed(c):
+    return (c, 0, 0)
+
+
+def priced(nodes, plan):
+    cost = [nd["cost"][0] + nd["cost"][1] * plan["cyc"] + nd["cost"][2] * plan["gat"] for nd in nodes]
+    return cost, [plan.get(nd["lat"], nd["lat"]) for nd in nodes], plan["wake"]
+
+
+def replay(nodes, queue, seq, price):
+    cost, lat, wake = price
+    issued, end, free = {}, {}, {}
+    for i in seq:
+        t = free.get(queue[i], 0.0)
+        for j in nodes[i]["hard"]:
+            t = max(t, end[j] + wake)
+        for j in nodes[i]["soft"]:
+            t = max(t, issued[j])
+        issued[i] = t + cost[i]
+        end[i] = issued[i] + lat[i]
+        if queue[i]:
+            free[queue[i]] = issued[i]
+    return max(end.values())
+
+
+def lay_out(nodes, after, queue, rank, look, price):
+    cost, lat, wake = price
+    left = [len(nd["hard"]) + len(nd["soft"]) for nd in nodes]
+    avail = [0.0] * len(nodes)
+    ready = [i for i in range(len(nodes)) if left[i] == 0]
+    free, seq = {q: 0.0 for q in queue}, []
+    while ready:
+        first = min(ready, key=lambda i: max(avail[i], free[queue[i]]))
+        q = queue[first]
+        i = first
+        if q:
+            limit = max(avail[first], free[q]) + look * cost[first]
+            i = max([k for k in ready if queue[k] == q and avail[k] <= limit], key=lambda k: rank[k])
+        t = max(avail[i], free[q]) + cost[i]
+        if q:
+            free[q] = t
+        seq.append(i)
+        ready.remove(i)
+        for j, hard in after[i]:
+            avail[j] = max(avail[j], t + lat[i] + wake if hard else t)
+            left[j] -= 1
+            if left[j] == 0:
+                ready.append(j)
+    return seq
+
+
+def schedule(nodes):
+    after = [[] for _ in nodes]
+    for i, nd in enumerate(nodes):
+        for j in nd["hard"]:
+            after[j].append((i, True))
+        for j in nd["soft"]:
+            after[j].append((i, False))
+    prices = [priced(nodes, p) for p in PLANS]
+    cost, lat, wake = prices[0]
+    rank = [0.0] * len(nodes)
+    for i in range(len(nodes) - 1, -1, -1):
+        rank[i] = cost[i] + max([lat[i]] + [rank[j] + (lat[i] + wake if hard else 0.0) for j, hard in after[i]])
+    groups = {}
+    for i, nd in enumerate(nodes):
+        if nd["group"]:
+            groups.setdefault(nd["group"], []).append(i)
+    names = sorted(groups)
+    seed = [12345]
+
+    def rnd():
+        seed[0] = (seed[0] * 1103515245 + 12345) % 2147483648
+        return seed[0] / 2147483648.0
+
+    def attempt(queue, rank, look):
+        seq = lay_out(nodes, after, queue, rank, look, prices[0])
+        return (sum(replay(nodes, queue, seq, p) for p in prices), seq, queue, rank, look)
+
+    best = min([attempt([nd["q"] for nd in nodes], rank, look) for look in (0.0, 0.2, 0.4)], key=lambda b: b[0])
+    for _ in range(TRIES):
+        queue, rank, look = list(best[2]), list(best[3]), best[4]
+        kind = rnd()
+        if kind < 0.4:
+            for _k in range(1 + int(rnd() * 2)):
+                for i in groups[names[int(rnd() * len(names))]]:
+                    queue[i] = "s" if queue[i] == "v" else "v"
+        elif kind < 0.95:
+            a = int(rnd() * len(nodes))
+            d = (rnd() - 0.5) * 3.0
+            for i in range(a, min(len(nodes), a + 1 + int(rnd() * 14))):
+                rank[i] += d
+        else:
+            look = rnd() * 0.5
+        new = attempt(queue, rank, look)
+        if new[0] <= best[0]:
+            best = new
+    return best[1], best[2], best[0]
+
+
+def rank_program(g, core, T, topo):
+    rank = T.rank_of(core)
+    n = len(T.cores)
+    if rank is None:
+        for r in range(n):
+            hs = helpers_of(T, topo, r)
+            if core in hs:
+                helper_program(g, core, T, topo, r, hs.index(core))
+        return
+
+    Q = {"v": g.vector, "s": g.scalar, "p": g.tensor, "g": g, "y": g.sync}
+    own = {"v": "cv", "s": "cs", "p": "cp", "g": "cg"}
+    nodes, wrote, readers = [], {}, {}
+
+    def node(q, reads, writes, call, cost, lat=0.0, sem=None, inc=1, loose=(), behind=(), group=None):
+        hard, soft = set(), set()
+        for k in list(reads) + list(writes):
+            if k in wrote:
+                (soft if k in loose else hard).add(wrote[k])
+            if k in writes:
+                hard.update(readers.get(k, []))
+        for k in behind:
+            if k in wrote:
+                soft.add(wrote[k])
+        i = len(nodes)
+        nodes.append({"q": q, "hard": sorted(hard), "soft": sorted(soft - hard), "call": call, "cost": cost, "lat": lat,
+                      "sem": sem, "inc": inc, "group": group})
+        for k in reads:
+            readers.setdefault(k, []).append(i)
+        for k in list(writes) + list(behind):
+            wrote[k] = i
+            readers[k] = []
+
+    def op(q, reads, writes, call, cost, loose=(), behind=()):
+        node(q, reads, writes, lambda _q: call(), cost, sem="own", loose=loose, behind=behind)
+
+    def dma(q, s, reads, writes, out, src, lat):
+        node(q, reads, writes, lambda _q: Q[q].dma_start(out, src), fixed(0.06), lat, s, 16, behind=["dma" + q])
+
+    def arrives(key, c, behind=()):
+        node(None, [], [key], None, fixed(0.0), key, key, c, behind=behind)
+
+    sent = [0]
+
+    def send(reads, out, src, sem, dst, mark=()):
+        rid, pid = topo.addr(dst, core)
+        node("g", reads, [], lambda _q: g.remote_dma(out, src, sem, T.sem.sent, pid, rid, topo.mask(core, dst)), fixed(0.3),
+             behind=["g"] + list(mark))
+        sent[0] += len(topo.engines(core, dst))
+
+    V, S, P = g.vector, g.scalar, g.tensor
+    prev, nxt = T.cores[(rank - 1) % n], T.cores[(rank + 1) % n]
+    hs = helpers_of(T, topo, rank)
+    spare = spare_engines(T, topo, rank)
+    ps = [T["ps%d" % b] for b in range(8)]
+    qv, sv = [T.qv0, T.qv1, T.qv2], [T.sv0, T.sv1, T.sv2]
+    wc, wsc = [T.w0c, T.w1c], [T.w0s, T.w1s]
+    e1 = len(topo.engines(nxt, core))
+    arrives("w0", 2 * e1 + sum(len(topo.engines(h, core)) for h in helpers_of(T, topo, (rank + 1) % n)))
+    arrives("w1", 4 * sum(len(topo.engines(h, core)) for h in helpers_of(T, topo, (rank + 2) % n)))
+
+    def ts(reads, writes, c, out, in0, s1, s2, op0, op1=None):
+        if op1 is None:
+            op("v", reads, writes, lambda: V.tensor_scalar(out, in0, s1, None, op0), cyc(c))
+        else:
+            op("v", reads, writes, lambda: V.tensor_scalar(out, in0, s1, s2, op0, op1), cyc(c))
+
+    def cp(reads, writes, cost, out, src):
+        op("v", reads, writes, lambda: V.tensor_copy(out, src), cost)
+
+    def tt(reads, writes, cost, out, a, b, o):
+        op("v", reads, writes, lambda: V.tensor_tensor(out, a, b, o), cost)
+
+    def scan(reads, writes, c, out, d0, d1, o0, o1):
+        op("v", reads, writes, lambda: V.tensor_tensor_scan(out, d0, d1, 0.0, o0, o1), cyc(c))
+
+    def fill(key, c, out, value):
+        op("v", [], [key], lambda: V.memset(out, value), cyc(c))
+
+    def act(reads, writes, cost, out, src, func, **kw):
+        op("s", reads, writes, lambda: S.activation(out, src, func, **kw), cost)
+
+    def move(q, group, reads, writes, cost, out, src, scale=None, bias=None):
+        def call(on):
+            if on == "v":
+                if scale is not None:
+                    return V.tensor_scalar(out, src, scale, None, MUL)
+                if bias is not None:
+                    return V.tensor_scalar(out, src, bias, None, ADD)
+                return V.tensor_copy(out, src)
+            if scale is not None:
+                return S.activation(out, src, IDENT, scale=scale)
+            if bias is not None:
+                return S.activation(out, src, IDENT, bias=bias)
+            return S.activation(out, src, COPY)
+        node(q, reads, writes, call, cost, sem="own", group=group)
+
+    def quant(reads, writes, q, s, a, tile, c=128):
+        op("v", reads, writes, lambda: V.quantize_mx(q[:, a:a + c], s[:, a:a + c], tile), fixed(0.125))
+
+    def mm(reads, bank, lq, ls, la, rq, rs, ra, cols, start=True, stop=True):
+        key = "ps%d" % bank
+        op("p", reads, [key], lambda: P.matmul_mx(ps[bank][:, 0:cols], lq[:, la:la + 128], ls[:, la:la + 128],
+                                                  rq[:, ra:ra + cols], rs[:, ra:ra + cols], start, stop),
+           fixed((cols + 16) * 0.0006), loose=() if start else (key,))
+
+    def send_halo(t):
+        name = "halo%d" % t
+        send(["qvA%d" % t], bytes_of(qv[t][:, 256:336]), bytes_of(qv[t][:, 0:NH]), T.sem[name], prev)
+        send(["qvA%d" % t], sv[t][:, 256:336], sv[t][:, 0:NH], T.sem[name], prev, ["left" + name])
+        arrives(name, 2 * e1, ["left" + name])
+
+    def to_helpers(reads, srcs, dst, sem):
+        half = len(spare) // 2
+        trs = []
+        for i in range(2):
+            rid, pid = topo.addr(hs[i], core)
+            trs.append(RemoteDMATransfer(dst_ids=[DstId(rid=rid, pnc=pid)], dma_engine_mask=mask_of(spare[half * i:half * i + half]),
+                                         remote_sem=sem, src=srcs[i], dst=dst))
+        node("g", reads, [], lambda _q: g.remote_dma_fused(trs, local_sem=T.sem.sent), fixed(0.3), behind=["g"])
+        sent[0] += 2 * half
+
+    WD = 512 - 2 * HC
+    dma("s", "lws0", [], ["ws0"], T.wls[:, 0:WS0], T.ws[:, 0:WS0], 1.9)
+    dma("y", "lxa", [], ["xa"], T.xa[:, 0:4 * NA], T.x[:, 0:4 * NA], 2.6)
+    dma("s", "lst", [], ["sti"], T.sti[:], T.st[:], 2.9)
+    dma("y", "lwh", [], ["wlh"], bytes_of(T.wlc[:, WD:512]), T.wc[:, 4 * WD:2048], 3.7)
+    dma("y", "lu", [], ["ut"], T.ut[:], T.u[:], 4.6)
+    dma("y", "lxb", [], ["xb"], T.xb[:, 0:4 * NB], T.x[:, 4 * NA:768], 5.4)
+    dma("y", "lws", ["ut"], ["wls"], T.wls[:, WS0:512], T.ws[:, WS0:512], 2.5)
+    dma("y", "lwd", [], ["wld"], bytes_of(T.wlc[:, 0:WD]), T.wc[:, 0:4 * WD], 3.5)
+
+    EQ = AluOpType.is_equal
+    s0 = WS0 // 2
+    op("g", [], ["pi"], lambda: g.iota(T.pi[:], [[0, 1]], 0, 1), fixed(0.13), behind=["g"])
+    op("g", [], ["iw"], lambda: g.iota(T.iw[:], [[1, 256]], 0, 0, allow_small_or_imprecise_dtypes=True), fixed(0.66), behind=["g"])
+    op("g", [], ["i8"], lambda: g.iota(T.i8[:], [[0, 40], [1, 8]], 0, 0, allow_small_or_imprecise_dtypes=True), fixed(0.8), behind=["g"])
+    to_helpers(["ws0"], [T.wls[:, 0:s0], T.wls[:, s0:WS0]], T.whs[:, 0:s0], T.sem.hp0)
+    op("g", [], ["i40"], lambda: g.iota(T.i40[:], [[32, 10], [0, 4]], 7, 0, allow_small_or_imprecise_dtypes=True), fixed(0.2), behind=["g"])
+    fill("xapad", 88, T.xa[:, 4 * NA:512], 0.0)
+    fill("xbpad", 40, T.xb[:, 4 * NB:512], 0.0)
+    fill("et", 258, T.et[:], 0.0)
+    SHR, AND = AluOpType.logical_shift_right, AluOpType.bitwise_and
+    ts(["pi"], ["ci0"], 1, T.ci[:, 0:1], T.pi[:], 15, None, AND)
+    ts(["pi"], ["ci1"], 1, T.ci[:, 1:2], T.pi[:], 2, 3, SHR, AND)
+    ts(["pi"], ["ci2"], 1, T.ci[:, 2:3], T.pi[:], 3, None, AND)
+    ts(["pi"], ["ci3"], 1, T.ci[:, 3:4], T.pi[:], 3, 1, SHR, AND)
+    ts(["pi"], ["ci4"], 1, T.ci[:, 4:5], T.pi[:], 7, None, AND)
+    ts(["pi"], ["ci5"], 1, T.ci[:, 5:6], T.pi[:], 127, None, AND)
+    fill("exa", 120, T.ex[:, 0:960:4], -BIG)
+    cp(["ci0", "ci1", "ci2", "ci3", "ci4", "ci5"], ["cf"], cyc(6), T.cf[:, 0:6], T.ci[:, 0:6])
+    fill("exc", 120, T.ex[:, 2:960:4], 0.0)
+    fill("exd", 120, T.ex[:, 3:960:4], 0.0)
+    c_r, c_r4, c_m4, c_hi, c_m8, c_p = [T.cf[:, i:i + 1] for i in range(6)]
+    c_lo, c_8m4, c_rho, c_sig, c_bias = [T.cx[:, i:i + 1] for i in range(5)]
+    cp(["iw"], ["ou"], cyc(8), T.ou[:], T.iw[:, 0:128:16])
+    ts(["iw", "cf"], ["et"], 128, T.et[:, 3:515:4], T.iw[:, 0:128], c_p, None, EQ)
+    ts(["cf"], ["c_rho"], 1, c_rho, c_m4, 3.0, c_r4, MUL, ADD)
+    ts(["cf"], ["c_sig"], 1, c_sig, c_hi, 3.0, c_m8, MUL, ADD)
+    ts(["cf"], ["c_bias"], 1, c_bias, c_r, 1.0, float(BIAS), AluOpType.is_ge, MUL)
+    for b in range(4):
+        quant(["et"], ["eq%d" % b], T.eq, T.es, 128 * b, T.et[:, 3 - b:515 - b])
+
+    quant(["xa", "xapad"], ["qvA0"], T.qv0, T.sv0, 0, T.xa[:, 0:512])
+    send_halo(0)
+    quant(["ut"], ["uq"], T.uq, T.us, 0, T.ut[:])
+    quant(["xb", "xbpad"], ["qvB0"], T.qv0, T.sv0, 128, T.xb[:])
+    cp(["uq", "ou"], ["urq"], gat(128), T.urq[:].bitcast(dt.uint32), T.uq[:].bitcast(dt.uint32).indirect(T.ou[:]))
+    act(["uq", "ou"], ["urs"], gat(128), T.urs[:], T.us[:].indirect(T.ou[:]), COPY)
+    UR = ["urq", "urs"]
+    dma("y", "lv", ["halo0"], ["vt"], T.vt[:], T.v[:], 3.0)
+    (a0, c0), (b0, d0) = helper_columns(0)
+    (a1, _), (b1, _) = helper_columns(1)
+    to_helpers(["wlh"], [bytes_of(T.wlc[:, a0:a0 + c0]), bytes_of(T.wlc[:, a1:a1 + c0])], bytes_of(T.whc[:, 0:c0]), T.sem.hp1)
+    send(["ws0", "wls"], T.w0s[:], T.wls[:], T.sem.w0, prev)
+    send(["wld"], bytes_of(T.w0c[:, 0:WD]), bytes_of(T.wlc[:, 0:WD]), T.sem.w0, prev)
+    to_helpers(["wld"], [bytes_of(T.wlc[:, b0:b0 + d0]), bytes_of(T.wlc[:, b1:b1 + d0])], bytes_of(T.whc[:, c0:c0 + d0]), T.sem.hp2)
+    to_helpers(["wls"], [T.wls[:, WS0:256 + s0], T.wls[:, 256 + s0:512]], T.whs[:, s0:256], T.sem.hp3)
+    quant(["vt"], ["vq"], T.vq, T.vs, 0, T.vt[:])
+
+    act(["cf"], ["c_lo"], cyc(1), c_lo, c_hi, IDENT, scale=-1.0, bias=1.0)
+    act(["cf"], ["c_8m4"], cyc(1), c_8m4, c_m4, COPY, scale=8.0)
+    act(["cf", "iw"], ["cr"], cyc(48), T.cr[:], T.iw[:, 0:48], IDENT, bias=c_r)
+    act(["iw"], ["d1e"], cyc(172), T.d1[:, 0:344:2], T.iw[:, 0:172], COPY, scale=0.0)
+    act(["iw", "c_lo"], ["d1o"], cyc(172), T.d1[:, 1:344:2], T.iw[:, 0:172], IDENT, scale=0.0, bias=c_lo)
+    act(["iw"], ["rr"], cyc(160), T.rr[:], T.iw[:, 0:160], COPY, scale=0.0)
+    act(["iw"], ["rr"], cyc(10), T.rr[:, 0:160:16], T.iw[:, 0:10], IDENT, scale=0.0, bias=BIG)
+    act(["iw"], ["mxpad"], cyc(4), T.mx[:, 0:4], T.iw[:, 0:4], COPY)
+    act(["i8"], ["rs8"], cyc(320), T.rs8[:], T.i8[:], SIGN)
+    for t in range(2):
+        e, key = SPLIT[t] - 1, "p1%d" % t
+        act(["iw"], ["kb0%d" % t], cyc(6), T.kb[:, 16 * t:16 * t + e], T.iw[:, 0:16 * e:16], COPY, scale=-1.0)
+        act(["iw"], ["kb1%d" % t], cyc(10), T.kb[:, 16 * t + e:16 * t + 16], T.iw[:, 0:16 * (16 - e):16], COPY, scale=-1.0)
+        p1 = 240 * t
+        act(["iw"], [key], cyc(240), T.p1[:, p1:p1 + 240], T.iw[:, 0:240], IDENT, scale=0.0, bias=-1.0)
+        act(["iw"], [key], cyc(5), T.p1[:, p1 + 15:p1 + 16 * (e - 1):16], T.iw[:, 31:16 * e:16], COPY)
+        act(["iw"], [key], cyc(10), T.p1[:, p1 + 16 * e - 1:p1 + 240:16], T.iw[:, 15:16 * (16 - e):16], COPY)
+    for h, tb in ((1, T.tb1), (2, T.tb2)):
+        act(["iw"], ["tb%df" % h], cyc(BIAS), tb[:, 0:BIAS], T.iw[:, 0:BIAS], COPY, scale=0.0)
+        act(["iw"], ["tb%dg" % h], cyc(BIAS), tb[:, BIAS:2 * BIAS], T.iw[:, 0:BIAS], COPY, scale=0.0)
+    for tile, key, c in ((T.za, "zApad", NA), (T.ha, "hApad", NA), (T.zb, "zBpad", NB), (T.hb, "hBpad", NB)):
+        fill(key, 256 - 2 * c, tile[:, 4 * c:512], 0.0)
+
+    cp(["sti"], ["stu"], cyc(2), T.stu[:], T.sti[:])
+    ts(["iw", "c_rho"], ["c_q"], 4, T.cx[:, 8:12], T.iw[:, 0:16:4], c_rho, None, ADD)
+    cp(["iw", "stu"], ["bf"], gat(32), T.bf[:], T.iw[:].indirect(T.stu[:]))
+    ts(["iw", "c_sig"], ["c_2"], 2, T.cx[:, 12:14], T.iw[:, 1:14:12], c_sig, c_sig, ADD, ADD)
+    tt(["bf"], ["nd"], cyc(62), T.nd[:, 0:31], T.bf[:, 1:32], T.bf[:, 0:31], SUB)
+    for q in range(2):
+        ts(["bf", "c_2"], ["o2%d" % q], 32, T.o2[:, q:64:2], T.bf[:], 2.0, T.cx[:, 12 + q:13 + q], MUL, ADD)
+    ts(["nd", "cf"], ["ne"], 31, T.ne[:, 0:31], T.nd[:, 0:31], c_r, 0.0, ADD, MAX)
+    for q in range(4):
+        ts(["bf", "c_q"], ["oc%d" % q], 32, T.ocd[:, q:128:4], T.bf[:], T.cx[:, 8 + q:9 + q], 2.0, ADD, MUL)
+    ts(["ne"], ["oe"], 31, T.oe[:, 0:31], T.ne[:, 0:31], 28.0, None, MIN)
+    ts(["iw", "cr"], ["win"], 32, T.win[:], T.iw[:, 0:32], T.cr[:, 12:13], EXCL, EQ, MUL)
+    ts(["i8", "cf"], ["m2"], 320, T.m2[:], T.i8[:], c_m8, None, EQ)
+    ts(["i40", "c_8m4"], ["ob"], 40, T.ob[:], T.i40[:], c_8m4, None, ADD)
+    KB = ["kb00", "kb10", "kb01", "kb11"]
+    ts(KB + ["c_bias"], KB, 16, T.kb[:, 0:32:2], T.kb[:, 0:32:2], c_bias, None, SUB)
+    cp(["c_bias"], ["ch0"], cyc(1), T.ch[:, 0:1], c_bias)
+    for m in range(3):
+        ts(["bf", "cr"], ["oz%d" % m], 2, T.oz[:, m:8:4], T.bf[:, 0:32:16], 4.0, T.cr[:, 16 * m:16 * m + 1], MUL, ADD)
+    tt(["bf"] + KB, ["kk"], cyc(64), T.kk[:], T.bf[:], T.kb[:], ADD)
+
+    piece = {"A": (0, NA, 0, 0), "B": (NA, NB, 128, 0), "H": (NA + NB, NH, 208, 48)}
+
+    def scores(t, k, bank):
+        keys = ["qvB%d" % t, "halo%d" % t] if k == "H" else ["qv%s%d" % (k, t)]
+        mm(UR + keys, bank, T.urq, T.urs, 0, qv[t], sv[t], piece[k][2], 128)
+
+    def plain(k, bank, group):
+        j0, c, _, r0 = piece[k]
+        c = min(c, 262 - j0)
+        move("s", group, ["ps%d" % bank], ["n" + k], cyc(c), T.i1[:, 2 * j0:2 * (j0 + c):2], ps[bank][:, r0:r0 + c])
+
+    def masked(k, bank, q, group):
+        j0, c, _, r0 = piece[k]
+        a, b = max(j0, 8), min(j0 + c, 270)
+        move(q, group, ["cf", "ps%d" % bank], ["m" + k], cyc(b - a), T.i1[:, 2 * (a - 8) + 1:2 * (b - 8):2],
+             ps[bank][:, r0 + a - j0:r0 + b - j0], scale=c_hi)
+
+    def shift(a, b, reads, key):
+        scan(reads + ["d1e", "d1o"], [key], 2 * (b - a), T.t1[:, 2 * a:2 * b], T.d1[:, 0:2 * (b - a)], T.i1[:, 2 * a:2 * b], MUL, ADD)
+
+    def decode(t, reads, ra, cols, parts):
+        for b in range(4):
+            mm(["eq%d" % b] + reads, 4 + b, T.eq, T.es, 128 * b, qv[t], sv[t], ra, cols)
+            for k, r0 in parts:
+                j0, c = piece[k][0], piece[k][1]
+                move("s", "dv%d%d%d" % (t, ra, b), ["ps%d" % (4 + b)], ["dv%s%d" % (k, b)], cyc(c),
+                     T.dv[:, 4 * j0 + b:4 * (j0 + c):4], ps[4 + b][:, r0:r0 + c], scale=0.5)
+
+    DV = ["dv%s%d" % (k, b) for k in "ABH" for b in range(4)]
+    I1 = ["nA", "nB", "nH", "mA", "mB", "mH"]
+    T1 = ["t1a", "t1b", "t1c"]
+
+    def span(name, a, b):
+        return ["%s%d" % (name, i) for i in range(a, b)]
+
+    def search(t, h):
+        e = SPLIT[t] - 1
+        a, b = (0, e) if h == 1 else (e, 15)
+        c0, k, name = 64 * t + 4, b - a, "%d%d" % (t, h)
+        move("s", "ex" + name, ["win", "oe"], span("ex", a, b), gat(16 * k), T.ex[:, 64 * a + 1:64 * b:4],
+             T.win[:].indirect(T.oe[:, 16 * t + a:16 * t + b]))
+        tt(T1 + ["o20", "o21", "m2"], span("g2", a, b), gat(32 * k), T.g2[:, 32 * a:32 * b],
+           T.t1[:, 24:524].indirect(T.o2[:, 32 * t + 2 * a:32 * t + 2 * b]), T.m2[:, 0:32 * k], MUL)
+        scan(span("g2", a, b) + ["rs8"], span("tt", a, b), 32 * k, T.tt[:, 32 * a:32 * b], T.rs8[:, 0:32 * k], T.g2[:, 32 * a:32 * b], MUL, ADD)
+        parts = -(-k // 3)
+        for x in range(parts):
+            i, j = a + k * x // parts, a + k * (x + 1) // parts
+            c = 64 * (j - i)
+            move("s", "cc%s%d" % (name, x), I1 + span("oc", 0, 4), span("cc", i, j), gat(c), T.cc[:, 64 * i:64 * j],
+                 T.i1[:].indirect(T.ocd[:, c0 + 4 * i:c0 + 4 * j]))
+            tt(span("tt", a, b) + ["ob"] + span("cc", i, j), span("df", i, j), gat(c), T.df[:, 64 * i:64 * j],
+               T.tt[:, 32 * a:32 * b].indirect(T.ob[:, 4 * (i - a):4 * (j - a)]), T.cc[:, 64 * i:64 * j], SUB)
+            act(span("df", i, j), span("ab", i, j), cyc(c), T.ab[:, 64 * i:64 * j], T.df[:, 64 * i:64 * j], ABS)
+            scan(span("ab", i, j) + span("ex", i, j) + ["exa", "exc", "exd"], span("mx", i, j), c,
+                 T.mx[:, 4 + 64 * i:4 + 64 * j], T.ex[:, 64 * i:64 * j], T.ab[:, 64 * i:64 * j], ADD, MAX)
+        scan(["mxpad", "rr"] + span("mx", max(a - 1, 0), b), span("mm", a, b), 16 * k, T.mm[:, 16 * a:16 * b],
+             T.mx[:, 3 + 64 * a:64 * b:4], T.rr[:, 0:16 * k], MIN, MAX)
+        tt(span("mx", a, b) + span("mm", a, b), span("nn", a, b), cyc(32 * k), T.nn[:, 16 * a:16 * b], T.mx[:, 7 + 64 * a:4 + 64 * b:4],
+           T.mm[:, 16 * a:16 * b], AluOpType.is_ge)
+        p1 = 240 * t
+        scan(span("nn", a, b) + ["p1%d" % t], span("pt", a, b), 16 * k, T.pt[:, 16 * a:16 * b], T.nn[:, 16 * a:16 * b],
+             T.p1[:, p1 + 16 * a:p1 + 16 * b], MUL, ADD)
+        cp(span("pt", a, b), span("op", a, b), cyc(k), T.op[:, a:b], T.pt[:, 16 * a + 15:16 * b:16])
+        tb, c = (T.tb1, T.tb2)[h - 1], 16 * k
+        move("s", "tf" + name, ["iw"] + span("op", a, b), ["tb%df" % h], gat(c), tb[:, 0:c], T.iw[:].indirect(T.op[:, a:b]))
+        move("s", "tg" + name, ["tb%df" % h, "c_bias"] + span("op", a, b), ["tb%dg" % h], gat(c - 16), tb[:, BIAS:BIAS + c - 16],
+             tb[:, 0:c].indirect(T.op[:, a:b - 1]), bias=c_bias)
+        for s in range(a // 2, (b + 1) // 2):
+            cp(["tb%df" % h, "tb%dg" % h, "ch0", "ch"], ["ch"], gat(16), T.ch[:, 4 * s + 2:4 * s + 34:2], tb[:].indirect(T.ch[:, 4 * s:4 * s + 1]))
+        a, b = (0, e + 1) if h == 1 else (e + 1, 16)
+        c = 3 * a + (h - 1)
+        cp(["ch", "ch0"], span("pf", a, b), cyc(9), T.pf[:, a:b], T.ch[:, 2 * a:2 * b:2])
+        tt(span("pf", a, b) + ["kk"], ["pp" + name], cyc(22), T.pp[:, 16 * t + a:16 * t + b], T.pf[:, a:b], T.kk[:, 16 * t + a:16 * t + b], ADD)
+        for m in range(3):
+            ts(["pp" + name, "cr"], span("og%d_" % m, a, b + 1) if h == 1 else span("og%d_" % m, a + 1, 17), 9,
+               T.og[:, c + m:c + 3 * (b - a):3], T.pp[:, 16 * t + a:16 * t + b], 4.0, T.cr[:, 16 * m:16 * m + 1], MUL, ADD)
+
+    def overlap(t, h):
+        s = SPLIT[t]
+        og = [x for m in range(3) for x in (span("og%d_" % m, 0, s + 1) if h == 1 else span("og%d_" % m, s + 1, 17))]
+        if h == 1:
+            move("s", "tz%d" % t, DV + span("oz", 0, 3), span("tn", 0, 3), gat(48), T.tn[:, 0:48], T.dv[:].indirect(T.oz[:, 4 * t:4 * t + 3]))
+            o0, u0, cols, ncols = 0, 0, 3 * s, 3 * s
+        else:
+            o0, u0, cols, ncols = 3 * s + 1, 3 * s, 48 - 3 * s, 45 - 3 * s
+        z, k = ((T.za, "A"), (T.zb, "B"))[h - 1]
+        m = ncols // 4 * 2
+        for i, (a, b) in enumerate(((0, m), (m, ncols))):
+            move("s", "tn%d%d%d" % (t, h, i), DV + og, span("tn", u0 + 3 + a, u0 + 3 + b), gat(16 * (b - a)),
+                 T.tn[:, 16 * (u0 + 3 + a):16 * (u0 + 3 + b)], T.dv[:, 48:1088].indirect(T.og[:, o0 + a:o0 + b]))
+        for i, (a, b) in enumerate(((0, m + 2), (m + 2, cols))):
+            tt(DV + og + span("tn", u0 + a, u0 + b), ["z%s%d" % (k, i)] + ["z%spad" % k] * (t * i), gat(16 * (b - a)), z[:, 16 * a:16 * b],
+               T.dv[:].indirect(T.og[:, o0 + a:o0 + b]), T.tn[:, 16 * (u0 + a):16 * (u0 + b)], ADD)
+
+    tiles = {"A": (T.za, T.ha, T.xa), "B": (T.zb, T.hb, T.xb)}
+
+    def made(t, k):
+        c = 12 * SPLIT[t] if k == "A" else 192 - 12 * SPLIT[t]
+        return c, max(c, 128), (0 if k == "A" else ZB)
+
+    def unload(tile, key, t, c, bank0, scale):
+        for b in range(4):
+            move("sv"[b % 2], "%s%d%d" % (key, t, b), ["ps%d" % (bank0 + b)], ["%s%d" % (key, b)], cyc(c),
+                 tile[:, b:4 * c:4], ps[bank0 + b][:, 0:c], scale=scale)
+
+    def layer(t, k):
+        z, h, _ = tiles[k]
+        c, w, a = made(t, k)
+        quant(["z%s0" % k, "z%s1" % k, "z%spad" % k], ["qz" + k], T.qz, T.sz, a, z[:, 0:4 * w], w)
+        for b in range(4):
+            mm(["qz" + k, "w%d" % t], b, wc[t], wsc[t], 128 * b, T.qz, T.sz, a, w)
+        for b in range(4):
+            mm(["qz" + k, "eq%d" % b], 4 + b, T.eq, T.es, 128 * b, T.qz, T.sz, a, w, True, False)
+        unload(h, "h" + k, t, c, 0, 0.03125)
+        quant(span("h" + k, 0, 4) + ["h%spad" % k], ["qh" + k], T.qh, T.sh, a, h[:, 0:4 * w], w)
+
+    def new_state(t, k):
+        x = tiles[k][2]
+        c, w, a = made(t, k)
+        for b in range(4):
+            mm(["qh" + k, "eq%d" % b], 4 + b, T.eq, T.es, 128 * b, T.qh, T.sh, a, w, False, True)
+        name = "x" + k.lower()
+        keys = span(name, 0, 4)
+        if t == 0:
+            for key in keys:
+                readers[key] = list(readers[name])
+            a = piece[k][2]
+        unload(x, name, t, c, 4, None)
+        quant(keys + [name + "pad"], ["qv%s%d" % (k, t + 1)], qv[t + 1], sv[t + 1], a, x[:, 0:4 * w], w)
+
+    def store(k, sem, queues):
+        c, w, a = made(1, k)
+        j0 = 0 if k == "A" else 192 - c
+        key = ["qv%s2" % k]
+        mm(key + ["vq"], 0, T.vq, T.vs, 0, T.qv2, T.sv2, a, w)
+        dma(queues[0], sem[0], key, [], T.oc[:, 4 * j0:4 * (j0 + c)], bytes_of(T.qv2[:, a:a + c]), STORE)
+        for i in range(4):
+            j = i // 2
+            dma(queues[j], sem[j], key, [], T.osc[4 * i:4 * i + 4, j0:j0 + c], T.sv2[32 * i:32 * i + 4, a:a + c], STORE)
+        move("s" if k == "A" else "v", "y" + k, ["ps0"], ["y" + k], cyc(c), T.yb[:, j0:j0 + c], ps[0][:, 0:c])
+        dma(queues[1], sem[1], ["y" + k], [], T.y[:, j0:j0 + c], T.yb[:, j0:j0 + c], STORE)
+
+    def early(t, k, bank):
+        scores(t, k, bank)
+        plain(k, bank, "e%d%s" % (t, k))
+        masked(k, bank, "s", "e%d%s" % (t, k))
+
+    def late(t, k):
+        scores(t, k, 2)
+        scores(t, k, 3)
+        plain(k, 2, "n%d%s" % (t, k))
+        masked(k, 3, "v", "m%d%s" % (t, k))
+
+    early(0, "A", 0)
+    early(0, "B", 1)
+    shift(12, 184, ["nA", "nB", "mA", "mB"], "t1a")
+    decode(0, ["qvA0", "qvB0"], 0, 256, (("A", 0), ("B", 128)))
+    late(0, "H")
+    shift(184, 262, ["nB", "nH", "mH"], "t1b")
+    decode(0, ["qvB0", "halo0"], 208, 128, (("H", 48),))
+    for t in range(2):
+        search(t, 1)
+        overlap(t, 1)
+        layer(t, "A")
+        new_state(t, "A")
+        if t == 0:
+            send_halo(1)
+        search(t, 2)
+        overlap(t, 2)
+        if t == 1:
+            store("A", ("sta", "sta"), ("y", "y"))
+            dma("y", "sta", ["pp01", "pp02", "pp11", "pp12"], [], T.ol[:], T.pp[0:128:16, :], STORE)
+        layer(t, "B")
+        if t == 0:
+            early(1, "A", 0)
+            shift(12, 76, ["nA", "mA"], "t1a")
+        new_state(t, "B")
+        if t == 0:
+            early(1, "H", 1)
+            late(1, "B")
+            shift(192, 262, ["nH", "mH"], "t1c")
+            shift(76, 192, ["nA", "nB", "mB", "mH"], "t1b")
+            decode(1, ["qvA1", "qvB1", "halo1"], 0, 336, (("A", 0), ("B", 128), ("H", 256)))
+    store("B", ("stb", "stc"), ("y", "s"))
+
+    if "plan" not in PLANNED:
+        PLANNED["plan"] = schedule(nodes)
+    seq, queue, _ = PLANNED["plan"]
+    count, waited, token = {"sent": sent[0]}, {}, {}
+
+    def need(q, s, c):
+        if waited.get((q, s), 0) < c:
+            Q[q].wait_ge(T.sem[s], c)
+            waited[(q, s)] = c
+
+    for i in seq:
+        nd, q = nodes[i], queue[i]
+        s = own[q] if nd["sem"] == "own" else nd["sem"]
+        if q:
+            toks = {}
+            for j in nd["hard"]:
+                toks[token[j][0]] = max(toks.get(token[j][0], 0), token[j][1])
+            for k in sorted(toks):
+                need(q, k, toks[k])
+            call = nd["call"](q)
+            if s:
+                call.then_inc(T.sem[s], nd["inc"])
+        if s:
+            count[s] = count.get(s, 0) + nd["inc"]
+            token[i] = (s, count[s])
+    for s in sorted(count):
+        need("g", s, count[s])

@@ -2,59 +2,28 @@ from concourse.bass import DstId, RemoteDMATransfer
 from concourse.mybir import dt, AluOpType, ActivationFunctionType
 
 F32, BF, I32, U16, CODE, U8 = "float32", "bfloat16", "int32", "uint16", "float8_e4m3fn_x4", "uint8"
-SPLIT = (7, 7)
 NA, NB, NH = 84, 108, 80
-ZB = 136
 BIG = 5.0e29
 EXCL = 1.0e29
-BIAS = 176
+BIAS = 160
 HC = 128
 WS0 = 128
-PLANS = ({"cyc": 0.00104, "gat": 0.00125, "wake": 0.08, "halo0": 4.5, "halo1": 3.6, "w0": 12.5, "w1": 22.0},
-         {"cyc": 0.00090, "gat": 0.00100, "wake": 0.05, "halo0": 3.5, "halo1": 2.8, "w0": 10.5, "w1": 18.0},
-         {"cyc": 0.00115, "gat": 0.00155, "wake": 0.14, "halo0": 5.5, "halo1": 4.4, "w0": 14.5, "w1": 25.0})
-TRIES = 5000
+PLANS = ({"cyc": 0.00095, "gat": 0.00125, "wake": 0.18, "halo0": 6.0, "halo1": 4.2, "w0": 15.0, "w1": 24.0},
+         {"cyc": 0.00085, "gat": 0.00100, "wake": 0.11, "halo0": 4.8, "halo1": 3.4, "w0": 12.0, "w1": 20.0},
+         {"cyc": 0.00115, "gat": 0.00155, "wake": 0.27, "halo0": 7.5, "halo1": 5.2, "w0": 18.7, "w1": 28.0})
+TRIES = 10000
 STORE = 2.4
 
-SCRATCH = {
-    "xa": ("sbuf", [128, 528], BF), "xb": ("sbuf", [128, 512], BF),
-    "za": ("sbuf", [128, 528], BF), "zb": ("sbuf", [128, 512], BF),
-    "ha": ("sbuf", [128, 528], BF), "hb": ("sbuf", [128, 512], BF),
-    "ut": ("sbuf", [128, 512], BF), "vt": ("sbuf", [128, 512], BF),
-    "et": ("sbuf", [128, 516], BF),
-    "eq": ("sbuf", [128, 512], CODE), "es": ("sbuf", [128, 512], U8),
-    "uq": ("sbuf", [128, 128], CODE), "us": ("sbuf", [128, 128], U8),
-    "urq": ("sbuf", [128, 128], CODE), "urs": ("sbuf", [128, 128], U8),
-    "vq": ("sbuf", [128, 128], CODE), "vs": ("sbuf", [128, 128], U8),
-    "qv0": ("sbuf", [128, 336], CODE), "sv0": ("sbuf", [128, 336], U8),
-    "qv1": ("sbuf", [128, 336], CODE), "sv1": ("sbuf", [128, 336], U8),
-    "qv2": ("sbuf", [128, 264], CODE), "sv2": ("sbuf", [128, 264], U8),
-    "qz": ("sbuf", [128, 264], CODE), "sz": ("sbuf", [128, 264], U8),
-    "qh": ("sbuf", [128, 264], CODE), "sh": ("sbuf", [128, 264], U8),
-    "wlc": ("sbuf", [128, 512], CODE), "wls": ("sbuf", [128, 512], U8),
-    "whc": ("sbuf", [128, 256], CODE), "whs": ("sbuf", [128, 256], U8),
-    "w0c": ("sbuf", [128, 512], CODE), "w0s": ("sbuf", [128, 512], U8),
-    "w1c": ("sbuf", [128, 512], CODE), "w1s": ("sbuf", [128, 512], U8),
-    "sti": ("sbuf", [128, 2], I32), "stu": ("sbuf", [128, 2], U16),
-    "pi": ("sbuf", [128, 1], I32), "ci": ("sbuf", [128, 8], I32), "cf": ("sbuf", [128, 8], F32),
-    "cx": ("sbuf", [128, 16], F32), "cr": ("sbuf", [128, 48], F32),
-    "iw": ("sbuf", [128, 256], F32), "i8": ("sbuf", [128, 320], F32), "i40": ("sbuf", [128, 40], F32),
-    "m2": ("sbuf", [128, 320], F32), "rs8": ("sbuf", [128, 320], F32),
-    "d1": ("sbuf", [128, 344], F32), "rr": ("sbuf", [128, 160], F32), "p1": ("sbuf", [128, 480], F32),
-    "ex": ("sbuf", [128, 960], BF), "win": ("sbuf", [128, 32], F32),
-    "kb": ("sbuf", [128, 32], F32), "kk": ("sbuf", [128, 32], F32), "bf": ("sbuf", [128, 32], F32),
-    "nd": ("sbuf", [128, 32], F32), "ne": ("sbuf", [128, 32], F32),
-    "ou": ("sbuf", [128, 8], U16), "ob": ("sbuf", [128, 40], U16), "ocd": ("sbuf", [128, 128], U16),
-    "o2": ("sbuf", [128, 64], U16), "oe": ("sbuf", [128, 32], U16), "oz": ("sbuf", [128, 8], U16),
-    "op": ("sbuf", [128, 16], U16), "ch": ("sbuf", [128, 64], U16), "og": ("sbuf", [128, 50], U16),
-    "i1": ("sbuf", [128, 524], F32), "t1": ("sbuf", [128, 524], F32),
-    "g2": ("sbuf", [128, 480], F32), "tt": ("sbuf", [128, 480], F32),
-    "cc": ("sbuf", [128, 960], F32), "df": ("sbuf", [128, 960], F32), "ab": ("sbuf", [128, 960], F32),
-    "mx": ("sbuf", [128, 964], F32), "mm": ("sbuf", [128, 240], F32), "nn": ("sbuf", [128, 240], F32),
-    "pt": ("sbuf", [128, 240], F32), "tb1": ("sbuf", [128, 352], F32), "tb2": ("sbuf", [128, 352], F32),
-    "pf": ("sbuf", [128, 16], F32), "pp": ("sbuf", [128, 32], F32),
-    "dv": ("sbuf", [128, 1088], BF), "tn": ("sbuf", [128, 768], BF), "yb": ("sbuf", [128, 192], F32),
-}
+SCRATCH = {}
+for _dt, _list in ((BF, "xa512 xb512 za512 zb512 ha512 hb512 ut512 vt512 et516 ex960 dv1088 tn768"),
+                   (CODE, "eq512 uq128 ur128 vq128 qa336 qb336 qc256 qz256 qh256 wl512 wh256 wa512 wb512"),
+                   (U8, "es512 us128 ux128 vs128 sa336 sb336 sc256 sz256 sh256 ls512 hs256 sx512 sy512"),
+                   (I32, "si2 pi1 ci8"),
+                   (U16, "su2 ou8 ob36 od128 ot64 oe32 oz8 op16 ch64 og50"),
+                   (F32, "cf8 cx16 cr48 iw256 ie288 ib36 mk288 rs288 dd344 rr144 pa240 wn32 kb16 kk32 bf32 nd32 ne32 ia524 ta524 "
+                         "gg480 tt480 cc960 df960 ab960 mx964 mm240 nn240 pt240 tb480 tc480 pf16 pp32 yb192")):
+    for _n in _list.split():
+        SCRATCH[_n[:2]] = ("sbuf", [128, int(_n[2:])], _dt)
 for _b in range(8):
     SCRATCH["ps%d" % _b] = ("psum", [128, 512], F32)
 
@@ -103,14 +72,14 @@ def helper_program(g, core, T, topo, r, i):
     (a, c), (b, d) = helper_columns(i)
     first, rest = WS0 // 2, 256 - WS0 // 2
     g.wait_ge(T.sem.hp0, got)
-    send(T.w1s[:, first * i:first * i + first], T.whs[:, 0:first], T.sem.w1, d2)
+    send(T.sy[:, first * i:first * i + first], T.hs[:, 0:first], T.sem.w1, d2)
     g.wait_ge(T.sem.hp1, got)
-    send(bytes_of(T.w0c[:, a:a + c]), bytes_of(T.whc[:, 0:c]), T.sem.w0, d1)
-    send(bytes_of(T.w1c[:, a:a + c]), bytes_of(T.whc[:, 0:c]), T.sem.w1, d2)
+    send(bytes_of(T.wa[:, a:a + c]), bytes_of(T.wh[:, 0:c]), T.sem.w0, d1)
+    send(bytes_of(T.wb[:, a:a + c]), bytes_of(T.wh[:, 0:c]), T.sem.w1, d2)
     g.wait_ge(T.sem.hp2, got)
-    send(bytes_of(T.w1c[:, b:b + d]), bytes_of(T.whc[:, c:c + d]), T.sem.w1, d2)
+    send(bytes_of(T.wb[:, b:b + d]), bytes_of(T.wh[:, c:c + d]), T.sem.w1, d2)
     g.wait_ge(T.sem.hp3, got)
-    send(T.w1s[:, WS0 + rest * i:WS0 + rest * i + rest], T.whs[:, first:256], T.sem.w1, d2)
+    send(T.sy[:, WS0 + rest * i:WS0 + rest * i + rest], T.hs[:, first:256], T.sem.w1, d2)
     g.wait_ge(T.sem.sent, total[0])
 
 
@@ -282,8 +251,8 @@ def rank_program(g, core, T, topo):
     hs = helpers_of(T, topo, rank)
     spare = spare_engines(T, topo, rank)
     ps = [T["ps%d" % b] for b in range(8)]
-    qv, sv = [T.qv0, T.qv1, T.qv2], [T.sv0, T.sv1, T.sv2]
-    wc, wsc = [T.w0c, T.w1c], [T.w0s, T.w1s]
+    qv, sv = [T.qa, T.qb, T.qc], [T.sa, T.sb, T.sc]
+    wc, wsc = [T.wa, T.wb], [T.sx, T.sy]
     e1 = len(topo.engines(nxt, core))
     arrives("w0", 2 * e1 + sum(len(topo.engines(h, core)) for h in helpers_of(T, topo, (rank + 1) % n)))
     arrives("w1", 4 * sum(len(topo.engines(h, core)) for h in helpers_of(T, topo, (rank + 2) % n)))
@@ -324,8 +293,8 @@ def rank_program(g, core, T, topo):
             return S.activation(out, src, COPY)
         node(q, reads, writes, call, cost, sem="own", group=group)
 
-    def quant(reads, writes, q, s, a, tile, c=128):
-        op("v", reads, writes, lambda: V.quantize_mx(q[:, a:a + c], s[:, a:a + c], tile), fixed(0.125))
+    def quant(reads, writes, q, s, a, tile):
+        op("v", reads, writes, lambda: V.quantize_mx(q[:, a:a + 128], s[:, a:a + 128], tile), fixed(0.125))
 
     def mm(reads, bank, lq, ls, la, rq, rs, ra, cols, start=True, stop=True):
         key = "ps%d" % bank
@@ -349,23 +318,26 @@ def rank_program(g, core, T, topo):
         node("g", reads, [], lambda _q: g.remote_dma_fused(trs, local_sem=T.sem.sent), fixed(0.3), behind=["g"])
         sent[0] += 2 * half
 
+    def iota(key, out, pattern, base, cost):
+        op("g", [], [key], lambda: g.iota(out, pattern, base, 0, allow_small_or_imprecise_dtypes=True), fixed(cost), behind=["g"])
+
     WD = 512 - 2 * HC
-    dma("s", "lws0", [], ["ws0"], T.wls[:, 0:WS0], T.ws[:, 0:WS0], 1.9)
+    dma("s", "lws0", [], ["ws0"], T.ls[:, 0:WS0], T.ws[:, 0:WS0], 1.9)
     dma("y", "lxa", [], ["xa"], T.xa[:, 0:4 * NA], T.x[:, 0:4 * NA], 2.6)
-    dma("s", "lst", [], ["sti"], T.sti[:], T.st[:], 2.9)
-    dma("y", "lwh", [], ["wlh"], bytes_of(T.wlc[:, WD:512]), T.wc[:, 4 * WD:2048], 3.7)
+    dma("s", "lst", [], ["sti"], T.si[:], T.st[:], 2.9)
+    dma("y", "lwh", [], ["wlh"], bytes_of(T.wl[:, WD:512]), T.wc[:, 4 * WD:2048], 3.7)
     dma("y", "lu", [], ["ut"], T.ut[:], T.u[:], 4.6)
     dma("y", "lxb", [], ["xb"], T.xb[:, 0:4 * NB], T.x[:, 4 * NA:768], 5.4)
-    dma("y", "lws", ["ut"], ["wls"], T.wls[:, WS0:512], T.ws[:, WS0:512], 2.5)
-    dma("y", "lwd", [], ["wld"], bytes_of(T.wlc[:, 0:WD]), T.wc[:, 0:4 * WD], 3.5)
+    dma("y", "lws", ["ut"], ["wls"], T.ls[:, WS0:512], T.ws[:, WS0:512], 2.5)
+    dma("y", "lwd", [], ["wld"], bytes_of(T.wl[:, 0:WD]), T.wc[:, 0:4 * WD], 3.5)
 
     EQ = AluOpType.is_equal
     s0 = WS0 // 2
     op("g", [], ["pi"], lambda: g.iota(T.pi[:], [[0, 1]], 0, 1), fixed(0.13), behind=["g"])
-    op("g", [], ["iw"], lambda: g.iota(T.iw[:], [[1, 256]], 0, 0, allow_small_or_imprecise_dtypes=True), fixed(0.66), behind=["g"])
-    op("g", [], ["i8"], lambda: g.iota(T.i8[:], [[0, 40], [1, 8]], 0, 0, allow_small_or_imprecise_dtypes=True), fixed(0.8), behind=["g"])
-    to_helpers(["ws0"], [T.wls[:, 0:s0], T.wls[:, s0:WS0]], T.whs[:, 0:s0], T.sem.hp0)
-    op("g", [], ["i40"], lambda: g.iota(T.i40[:], [[32, 10], [0, 4]], 7, 0, allow_small_or_imprecise_dtypes=True), fixed(0.2), behind=["g"])
+    iota("iw", T.iw[:], [[1, 256]], 0, 0.66)
+    iota("i8", T.ie[:], [[0, 36], [1, 8]], 0, 0.73)
+    to_helpers(["ws0"], [T.ls[:, 0:s0], T.ls[:, s0:WS0]], T.hs[:, 0:s0], T.sem.hp0)
+    iota("i36", T.ib[:], [[32, 9], [0, 4]], 7, 0.2)
     fill("xapad", 88, T.xa[:, 4 * NA:512], 0.0)
     fill("xbpad", 40, T.xb[:, 4 * NB:512], 0.0)
     fill("et", 258, T.et[:], 0.0)
@@ -386,90 +358,89 @@ def rank_program(g, core, T, topo):
     ts(["iw", "cf"], ["et"], 128, T.et[:, 3:515:4], T.iw[:, 0:128], c_p, None, EQ)
     ts(["cf"], ["c_rho"], 1, c_rho, c_m4, 3.0, c_r4, MUL, ADD)
     ts(["cf"], ["c_sig"], 1, c_sig, c_hi, 3.0, c_m8, MUL, ADD)
-    ts(["cf"], ["c_bias"], 1, c_bias, c_r, 1.0, float(BIAS), AluOpType.is_ge, MUL)
+    ts(["cf"], ["c_bias"], 1, c_bias, c_r, 2.0, float(BIAS), MIN, MUL)
     for b in range(4):
         quant(["et"], ["eq%d" % b], T.eq, T.es, 128 * b, T.et[:, 3 - b:515 - b])
 
-    quant(["xa", "xapad"], ["qvA0"], T.qv0, T.sv0, 0, T.xa[:, 0:512])
+    quant(["xa", "xapad"], ["qvA0"], T.qa, T.sa, 0, T.xa[:])
     send_halo(0)
     quant(["ut"], ["uq"], T.uq, T.us, 0, T.ut[:])
-    quant(["xb", "xbpad"], ["qvB0"], T.qv0, T.sv0, 128, T.xb[:])
-    cp(["uq", "ou"], ["urq"], gat(128), T.urq[:].bitcast(dt.uint32), T.uq[:].bitcast(dt.uint32).indirect(T.ou[:]))
-    act(["uq", "ou"], ["urs"], gat(128), T.urs[:], T.us[:].indirect(T.ou[:]), COPY)
+    quant(["xb", "xbpad"], ["qvB0"], T.qa, T.sa, 128, T.xb[:])
+    cp(["uq", "ou"], ["urq"], gat(128), T.ur[:].bitcast(dt.uint32), T.uq[:].bitcast(dt.uint32).indirect(T.ou[:]))
+    act(["uq", "ou"], ["urs"], gat(128), T.ux[:], T.us[:].indirect(T.ou[:]), COPY)
     UR = ["urq", "urs"]
     dma("y", "lv", ["halo0"], ["vt"], T.vt[:], T.v[:], 3.0)
     (a0, c0), (b0, d0) = helper_columns(0)
     (a1, _), (b1, _) = helper_columns(1)
-    to_helpers(["wlh"], [bytes_of(T.wlc[:, a0:a0 + c0]), bytes_of(T.wlc[:, a1:a1 + c0])], bytes_of(T.whc[:, 0:c0]), T.sem.hp1)
-    send(["ws0", "wls"], T.w0s[:], T.wls[:], T.sem.w0, prev)
-    send(["wld"], bytes_of(T.w0c[:, 0:WD]), bytes_of(T.wlc[:, 0:WD]), T.sem.w0, prev)
-    to_helpers(["wld"], [bytes_of(T.wlc[:, b0:b0 + d0]), bytes_of(T.wlc[:, b1:b1 + d0])], bytes_of(T.whc[:, c0:c0 + d0]), T.sem.hp2)
-    to_helpers(["wls"], [T.wls[:, WS0:256 + s0], T.wls[:, 256 + s0:512]], T.whs[:, s0:256], T.sem.hp3)
+    to_helpers(["wlh"], [bytes_of(T.wl[:, a0:a0 + c0]), bytes_of(T.wl[:, a1:a1 + c0])], bytes_of(T.wh[:, 0:c0]), T.sem.hp1)
+    send(["ws0", "wls"], T.sx[:], T.ls[:], T.sem.w0, prev)
+    send(["wld"], bytes_of(T.wa[:, 0:WD]), bytes_of(T.wl[:, 0:WD]), T.sem.w0, prev)
+    to_helpers(["wld"], [bytes_of(T.wl[:, b0:b0 + d0]), bytes_of(T.wl[:, b1:b1 + d0])], bytes_of(T.wh[:, c0:c0 + d0]), T.sem.hp2)
+    to_helpers(["wls"], [T.ls[:, WS0:256 + s0], T.ls[:, 256 + s0:512]], T.hs[:, s0:256], T.sem.hp3)
     quant(["vt"], ["vq"], T.vq, T.vs, 0, T.vt[:])
 
     act(["cf"], ["c_lo"], cyc(1), c_lo, c_hi, IDENT, scale=-1.0, bias=1.0)
     act(["cf"], ["c_8m4"], cyc(1), c_8m4, c_m4, COPY, scale=8.0)
     act(["cf", "iw"], ["cr"], cyc(48), T.cr[:], T.iw[:, 0:48], IDENT, bias=c_r)
-    act(["iw"], ["d1e"], cyc(172), T.d1[:, 0:344:2], T.iw[:, 0:172], COPY, scale=0.0)
-    act(["iw", "c_lo"], ["d1o"], cyc(172), T.d1[:, 1:344:2], T.iw[:, 0:172], IDENT, scale=0.0, bias=c_lo)
-    act(["iw"], ["rr"], cyc(160), T.rr[:], T.iw[:, 0:160], COPY, scale=0.0)
-    act(["iw"], ["rr"], cyc(10), T.rr[:, 0:160:16], T.iw[:, 0:10], IDENT, scale=0.0, bias=BIG)
+    act(["iw"], ["d1e"], cyc(172), T.dd[:, 0:344:2], T.iw[:, 0:172], COPY, scale=0.0)
+    act(["iw", "c_lo"], ["d1o"], cyc(172), T.dd[:, 1:344:2], T.iw[:, 0:172], IDENT, scale=0.0, bias=c_lo)
+    act(["iw"], ["rr"], cyc(144), T.rr[:], T.iw[:, 0:144], COPY, scale=0.0)
+    act(["iw"], ["rr"], cyc(9), T.rr[:, 0:144:16], T.iw[:, 0:9], IDENT, scale=0.0, bias=BIG)
     act(["iw"], ["mxpad"], cyc(4), T.mx[:, 0:4], T.iw[:, 0:4], COPY)
-    act(["i8"], ["rs8"], cyc(320), T.rs8[:], T.i8[:], SIGN)
-    for t in range(2):
-        e, key = SPLIT[t] - 1, "p1%d" % t
-        act(["iw"], ["kb0%d" % t], cyc(6), T.kb[:, 16 * t:16 * t + e], T.iw[:, 0:16 * e:16], COPY, scale=-1.0)
-        act(["iw"], ["kb1%d" % t], cyc(10), T.kb[:, 16 * t + e:16 * t + 16], T.iw[:, 0:16 * (16 - e):16], COPY, scale=-1.0)
-        p1 = 240 * t
-        act(["iw"], [key], cyc(240), T.p1[:, p1:p1 + 240], T.iw[:, 0:240], IDENT, scale=0.0, bias=-1.0)
-        act(["iw"], [key], cyc(5), T.p1[:, p1 + 15:p1 + 16 * (e - 1):16], T.iw[:, 31:16 * e:16], COPY)
-        act(["iw"], [key], cyc(10), T.p1[:, p1 + 16 * e - 1:p1 + 240:16], T.iw[:, 15:16 * (16 - e):16], COPY)
-    for h, tb in ((1, T.tb1), (2, T.tb2)):
-        act(["iw"], ["tb%df" % h], cyc(BIAS), tb[:, 0:BIAS], T.iw[:, 0:BIAS], COPY, scale=0.0)
-        act(["iw"], ["tb%dg" % h], cyc(BIAS), tb[:, BIAS:2 * BIAS], T.iw[:, 0:BIAS], COPY, scale=0.0)
+    act(["i8"], ["rs8"], cyc(288), T.rs[:], T.ie[:], SIGN)
+    act(["iw"], ["kb0"], cyc(6), T.kb[:, 0:6], T.iw[:, 0:96:16], COPY, scale=-1.0)
+    act(["iw"], ["kb1"], cyc(10), T.kb[:, 6:16], T.iw[:, 0:160:16], COPY, scale=-1.0)
+    act(["iw"], ["p1"], cyc(240), T.pa[:], T.iw[:, 0:240], IDENT, scale=0.0, bias=-1.0)
+    act(["iw"], ["p1"], cyc(5), T.pa[:, 15:80:16], T.iw[:, 31:96:16], COPY)
+    act(["iw"], ["p1"], cyc(10), T.pa[:, 95:240:16], T.iw[:, 15:160:16], COPY)
+    for h, tb in ((1, T.tb), (2, T.tc)):
+        for x in range(3):
+            act(["iw"], ["tb%d%d" % (h, x)], cyc(BIAS), tb[:, BIAS * x:BIAS * x + BIAS], T.iw[:, 0:BIAS], COPY, scale=0.0)
     for tile, key, c in ((T.za, "zApad", NA), (T.ha, "hApad", NA), (T.zb, "zBpad", NB), (T.hb, "hBpad", NB)):
         fill(key, 256 - 2 * c, tile[:, 4 * c:512], 0.0)
 
-    cp(["sti"], ["stu"], cyc(2), T.stu[:], T.sti[:])
+    cp(["sti"], ["stu"], cyc(2), T.su[:], T.si[:])
     ts(["iw", "c_rho"], ["c_q"], 4, T.cx[:, 8:12], T.iw[:, 0:16:4], c_rho, None, ADD)
-    cp(["iw", "stu"], ["bf"], gat(32), T.bf[:], T.iw[:].indirect(T.stu[:]))
+    cp(["iw", "stu"], ["bf"], gat(32), T.bf[:], T.iw[:].indirect(T.su[:]))
     ts(["iw", "c_sig"], ["c_2"], 2, T.cx[:, 12:14], T.iw[:, 1:14:12], c_sig, c_sig, ADD, ADD)
     tt(["bf"], ["nd"], cyc(62), T.nd[:, 0:31], T.bf[:, 1:32], T.bf[:, 0:31], SUB)
     for q in range(2):
-        ts(["bf", "c_2"], ["o2%d" % q], 32, T.o2[:, q:64:2], T.bf[:], 2.0, T.cx[:, 12 + q:13 + q], MUL, ADD)
+        ts(["bf", "c_2"], ["o2%d" % q], 32, T.ot[:, q:64:2], T.bf[:], 2.0, T.cx[:, 12 + q:13 + q], MUL, ADD)
     ts(["nd", "cf"], ["ne"], 31, T.ne[:, 0:31], T.nd[:, 0:31], c_r, 0.0, ADD, MAX)
     for q in range(4):
-        ts(["bf", "c_q"], ["oc%d" % q], 32, T.ocd[:, q:128:4], T.bf[:], T.cx[:, 8 + q:9 + q], 2.0, ADD, MUL)
+        ts(["bf", "c_q"], ["oc%d" % q], 32, T.od[:, q:128:4], T.bf[:], T.cx[:, 8 + q:9 + q], 2.0, ADD, MUL)
     ts(["ne"], ["oe"], 31, T.oe[:, 0:31], T.ne[:, 0:31], 28.0, None, MIN)
-    ts(["iw", "cr"], ["win"], 32, T.win[:], T.iw[:, 0:32], T.cr[:, 12:13], EXCL, EQ, MUL)
-    ts(["i8", "cf"], ["m2"], 320, T.m2[:], T.i8[:], c_m8, None, EQ)
-    ts(["i40", "c_8m4"], ["ob"], 40, T.ob[:], T.i40[:], c_8m4, None, ADD)
-    KB = ["kb00", "kb10", "kb01", "kb11"]
-    ts(KB + ["c_bias"], KB, 16, T.kb[:, 0:32:2], T.kb[:, 0:32:2], c_bias, None, SUB)
+    ts(["iw", "cr"], ["win"], 32, T.wn[:], T.iw[:, 0:32], T.cr[:, 12:13], EXCL, EQ, MUL)
+    ts(["i8", "cf"], ["m2"], 288, T.mk[:], T.ie[:], c_m8, None, EQ)
+    ts(["i36", "c_8m4"], ["ob"], 36, T.ob[:], T.ib[:], c_8m4, None, ADD)
+    KB = ["kb0", "kb1"]
+    ts(KB + ["c_bias"], KB, 4, T.kb[:, 0:7:2], T.kb[:, 0:7:2], c_bias, None, SUB)
+    ts(KB + ["c_bias"], KB, 3, T.kb[:, 9:16:3], T.kb[:, 9:16:3], c_bias, None, SUB)
     cp(["c_bias"], ["ch0"], cyc(1), T.ch[:, 0:1], c_bias)
     for m in range(3):
         ts(["bf", "cr"], ["oz%d" % m], 2, T.oz[:, m:8:4], T.bf[:, 0:32:16], 4.0, T.cr[:, 16 * m:16 * m + 1], MUL, ADD)
-    tt(["bf"] + KB, ["kk"], cyc(64), T.kk[:], T.bf[:], T.kb[:], ADD)
+    for t in range(2):
+        tt(["bf"] + KB, ["kk%d" % t], cyc(32), T.kk[:, 16 * t:16 * t + 16], T.bf[:, 16 * t:16 * t + 16], T.kb[:], ADD)
 
     piece = {"A": (0, NA, 0, 0), "B": (NA, NB, 128, 0), "H": (NA + NB, NH, 208, 48)}
 
     def scores(t, k, bank):
         keys = ["qvB%d" % t, "halo%d" % t] if k == "H" else ["qv%s%d" % (k, t)]
-        mm(UR + keys, bank, T.urq, T.urs, 0, qv[t], sv[t], piece[k][2], 128)
+        mm(UR + keys, bank, T.ur, T.ux, 0, qv[t], sv[t], piece[k][2], 128)
 
     def plain(k, bank, group):
         j0, c, _, r0 = piece[k]
         c = min(c, 262 - j0)
-        move("s", group, ["ps%d" % bank], ["n" + k], cyc(c), T.i1[:, 2 * j0:2 * (j0 + c):2], ps[bank][:, r0:r0 + c])
+        move("s", group, ["ps%d" % bank], ["n" + k], cyc(c), T.ia[:, 2 * j0:2 * (j0 + c):2], ps[bank][:, r0:r0 + c])
 
     def masked(k, bank, q, group):
         j0, c, _, r0 = piece[k]
         a, b = max(j0, 8), min(j0 + c, 270)
-        move(q, group, ["cf", "ps%d" % bank], ["m" + k], cyc(b - a), T.i1[:, 2 * (a - 8) + 1:2 * (b - 8):2],
+        move(q, group, ["cf", "ps%d" % bank], ["m" + k], cyc(b - a), T.ia[:, 2 * (a - 8) + 1:2 * (b - 8):2],
              ps[bank][:, r0 + a - j0:r0 + b - j0], scale=c_hi)
 
     def shift(a, b, reads, key):
-        scan(reads + ["d1e", "d1o"], [key], 2 * (b - a), T.t1[:, 2 * a:2 * b], T.d1[:, 0:2 * (b - a)], T.i1[:, 2 * a:2 * b], MUL, ADD)
+        scan(reads + ["d1e", "d1o"], [key], 2 * (b - a), T.ta[:, 2 * a:2 * b], T.dd[:, 0:2 * (b - a)], T.ia[:, 2 * a:2 * b], MUL, ADD)
 
     def decode(t, reads, ra, cols, parts):
         for b in range(4):
@@ -487,69 +458,60 @@ def rank_program(g, core, T, topo):
         return ["%s%d" % (name, i) for i in range(a, b)]
 
     def search(t, h):
-        e = SPLIT[t] - 1
-        a, b = (0, e) if h == 1 else (e, 15)
+        a, b = (0, 6) if h == 1 else (6, 15)
         c0, k, name = 64 * t + 4, b - a, "%d%d" % (t, h)
-        move("s", "ex" + name, ["win", "oe"], span("ex", a, b), gat(16 * k), T.ex[:, 64 * a + 1:64 * b:4],
-             T.win[:].indirect(T.oe[:, 16 * t + a:16 * t + b]))
-        tt(T1 + ["o20", "o21", "m2"], span("g2", a, b), gat(32 * k), T.g2[:, 32 * a:32 * b],
-           T.t1[:, 24:524].indirect(T.o2[:, 32 * t + 2 * a:32 * t + 2 * b]), T.m2[:, 0:32 * k], MUL)
-        scan(span("g2", a, b) + ["rs8"], span("tt", a, b), 32 * k, T.tt[:, 32 * a:32 * b], T.rs8[:, 0:32 * k], T.g2[:, 32 * a:32 * b], MUL, ADD)
-        parts = -(-k // 3)
-        for x in range(parts):
-            i, j = a + k * x // parts, a + k * (x + 1) // parts
-            c = 64 * (j - i)
-            move("s", "cc%s%d" % (name, x), I1 + span("oc", 0, 4), span("cc", i, j), gat(c), T.cc[:, 64 * i:64 * j],
-                 T.i1[:].indirect(T.ocd[:, c0 + 4 * i:c0 + 4 * j]))
-            tt(span("tt", a, b) + ["ob"] + span("cc", i, j), span("df", i, j), gat(c), T.df[:, 64 * i:64 * j],
+        move("s", "ex" + name, ["win", "oe"], ["ex%d" % h], gat(16 * k), T.ex[:, 64 * a + 1:64 * b:4],
+             T.wn[:].indirect(T.oe[:, 16 * t + a:16 * t + b]))
+        tt(T1 + ["o20", "o21", "m2"], ["g2%d" % h], gat(32 * k), T.gg[:, 32 * a:32 * b],
+           T.ta[:, 24:524].indirect(T.ot[:, 32 * t + 2 * a:32 * t + 2 * b]), T.mk[:, 0:32 * k], MUL)
+        scan(["g2%d" % h, "rs8"], ["tt%d" % h], 32 * k, T.tt[:, 32 * a:32 * b], T.rs[:, 0:32 * k], T.gg[:, 32 * a:32 * b], MUL, ADD)
+        for i in range(a, b, 3):
+            j = i + 3
+            move("s", "cc%d%d" % (t, i), I1 + span("oc", 0, 4), ["cc%d" % i], gat(192), T.cc[:, 64 * i:64 * j],
+                 T.ia[:].indirect(T.od[:, c0 + 4 * i:c0 + 4 * j]))
+            tt(["tt%d" % h, "ob", "cc%d" % i], ["df%d" % i], gat(192), T.df[:, 64 * i:64 * j],
                T.tt[:, 32 * a:32 * b].indirect(T.ob[:, 4 * (i - a):4 * (j - a)]), T.cc[:, 64 * i:64 * j], SUB)
-            act(span("df", i, j), span("ab", i, j), cyc(c), T.ab[:, 64 * i:64 * j], T.df[:, 64 * i:64 * j], ABS)
-            scan(span("ab", i, j) + span("ex", i, j) + ["exa", "exc", "exd"], span("mx", i, j), c,
+            act(["df%d" % i], ["ab%d" % i], cyc(192), T.ab[:, 64 * i:64 * j], T.df[:, 64 * i:64 * j], ABS)
+            scan(["ab%d" % i, "ex%d" % h, "exa", "exc", "exd"], ["mx%d" % i], 192,
                  T.mx[:, 4 + 64 * i:4 + 64 * j], T.ex[:, 64 * i:64 * j], T.ab[:, 64 * i:64 * j], ADD, MAX)
-        scan(["mxpad", "rr"] + span("mx", max(a - 1, 0), b), span("mm", a, b), 16 * k, T.mm[:, 16 * a:16 * b],
-             T.mx[:, 3 + 64 * a:64 * b:4], T.rr[:, 0:16 * k], MIN, MAX)
-        tt(span("mx", a, b) + span("mm", a, b), span("nn", a, b), cyc(32 * k), T.nn[:, 16 * a:16 * b], T.mx[:, 7 + 64 * a:4 + 64 * b:4],
+        MX = ["mx%d" % i for i in range(a, b, 3)]
+        scan(["mxpad", "rr", "mx3"] + MX, ["mm%d" % h], 16 * k, T.mm[:, 16 * a:16 * b], T.mx[:, 3 + 64 * a:64 * b:4], T.rr[:, 0:16 * k], MIN, MAX)
+        tt(MX + ["mm%d" % h], ["nn%d" % h], cyc(32 * k), T.nn[:, 16 * a:16 * b], T.mx[:, 7 + 64 * a:4 + 64 * b:4],
            T.mm[:, 16 * a:16 * b], AluOpType.is_ge)
-        p1 = 240 * t
-        scan(span("nn", a, b) + ["p1%d" % t], span("pt", a, b), 16 * k, T.pt[:, 16 * a:16 * b], T.nn[:, 16 * a:16 * b],
-             T.p1[:, p1 + 16 * a:p1 + 16 * b], MUL, ADD)
-        cp(span("pt", a, b), span("op", a, b), cyc(k), T.op[:, a:b], T.pt[:, 16 * a + 15:16 * b:16])
-        tb, c = (T.tb1, T.tb2)[h - 1], 16 * k
-        move("s", "tf" + name, ["iw"] + span("op", a, b), ["tb%df" % h], gat(c), tb[:, 0:c], T.iw[:].indirect(T.op[:, a:b]))
-        move("s", "tg" + name, ["tb%df" % h, "c_bias"] + span("op", a, b), ["tb%dg" % h], gat(c - 16), tb[:, BIAS:BIAS + c - 16],
-             tb[:, 0:c].indirect(T.op[:, a:b - 1]), bias=c_bias)
-        for s in range(a // 2, (b + 1) // 2):
-            cp(["tb%df" % h, "tb%dg" % h, "ch0", "ch"], ["ch"], gat(16), T.ch[:, 4 * s + 2:4 * s + 34:2], tb[:].indirect(T.ch[:, 4 * s:4 * s + 1]))
-        a, b = (0, e + 1) if h == 1 else (e + 1, 16)
-        c = 3 * a + (h - 1)
-        cp(["ch", "ch0"], span("pf", a, b), cyc(9), T.pf[:, a:b], T.ch[:, 2 * a:2 * b:2])
-        tt(span("pf", a, b) + ["kk"], ["pp" + name], cyc(22), T.pp[:, 16 * t + a:16 * t + b], T.pf[:, a:b], T.kk[:, 16 * t + a:16 * t + b], ADD)
+        scan(["nn%d" % h, "p1"], ["pt%d" % h], 16 * k, T.pt[:, 16 * a:16 * b], T.nn[:, 16 * a:16 * b], T.pa[:, 16 * a:16 * b], MUL, ADD)
+        cp(["pt%d" % h], ["op%d" % h], cyc(k), T.op[:, a:b], T.pt[:, 16 * a + 15:16 * b:16])
+        tb, src, key = (T.tb, T.tc)[h - 1], T.iw[:], "iw"
+        for x in range(h + 1):
+            c = 16 * (k - x)
+            out = tb[:, BIAS * x:BIAS * x + c]
+            move("s", "tf%s%d" % (name, x), [key, "c_bias", "op%d" % h], ["tb%d%d" % (h, x)], gat(c), out,
+                 src.indirect(T.op[:, a:b - x]), bias=c_bias if x == h else None)
+            src, key = out, "tb%d%d" % (h, x)
+        for s in range(a, b, h + 1):
+            cp(span("tb%d" % h, 0, 3) + ["ch0", "ch"], ["ch", "ch%d" % h] + ["ch2"] * (s == 0), gat(16),
+               T.ch[:, 2 * s + 2:2 * s + 34:2], tb[:].indirect(T.ch[:, 2 * s:2 * s + 1]))
+        a, b, c = (0, 7, 0) if h == 1 else (7, 16, 22)
+        cp(["ch%d" % h, "ch0"], ["pf%d" % h], cyc(9), T.pf[:, a:b], T.ch[:, 2 * a:2 * b:2])
+        tt(["pf%d" % h, "kk%d" % t], ["pp" + name], cyc(18), T.pp[:, 16 * t + a:16 * t + b], T.pf[:, a:b], T.kk[:, 16 * t + a:16 * t + b], ADD)
         for m in range(3):
-            ts(["pp" + name, "cr"], span("og%d_" % m, a, b + 1) if h == 1 else span("og%d_" % m, a + 1, 17), 9,
-               T.og[:, c + m:c + 3 * (b - a):3], T.pp[:, 16 * t + a:16 * t + b], 4.0, T.cr[:, 16 * m:16 * m + 1], MUL, ADD)
+            ts(["pp" + name, "cr"], ["og%d%d" % (h, m)], 9, T.og[:, c + m:c + 3 * (b - a):3], T.pp[:, 16 * t + a:16 * t + b],
+               4.0, T.cr[:, 16 * m:16 * m + 1], MUL, ADD)
 
     def overlap(t, h):
-        s = SPLIT[t]
-        og = [x for m in range(3) for x in (span("og%d_" % m, 0, s + 1) if h == 1 else span("og%d_" % m, s + 1, 17))]
+        og = span("og%d" % h, 0, 3)
         if h == 1:
             move("s", "tz%d" % t, DV + span("oz", 0, 3), span("tn", 0, 3), gat(48), T.tn[:, 0:48], T.dv[:].indirect(T.oz[:, 4 * t:4 * t + 3]))
-            o0, u0, cols, ncols = 0, 0, 3 * s, 3 * s
-        else:
-            o0, u0, cols, ncols = 3 * s + 1, 3 * s, 48 - 3 * s, 45 - 3 * s
+        o0, u0, cols, ncols = ((0, 0, 21, 21), (22, 21, 27, 24))[h - 1]
         z, k = ((T.za, "A"), (T.zb, "B"))[h - 1]
         m = ncols // 4 * 2
         for i, (a, b) in enumerate(((0, m), (m, ncols))):
             move("s", "tn%d%d%d" % (t, h, i), DV + og, span("tn", u0 + 3 + a, u0 + 3 + b), gat(16 * (b - a)),
                  T.tn[:, 16 * (u0 + 3 + a):16 * (u0 + 3 + b)], T.dv[:, 48:1088].indirect(T.og[:, o0 + a:o0 + b]))
         for i, (a, b) in enumerate(((0, m + 2), (m + 2, cols))):
-            tt(DV + og + span("tn", u0 + a, u0 + b), ["z%s%d" % (k, i)] + ["z%spad" % k] * (t * i), gat(16 * (b - a)), z[:, 16 * a:16 * b],
+            tt(DV + og + span("tn", u0 + a, u0 + b), ["z%s%d" % (k, i)], gat(16 * (b - a)), z[:, 16 * a:16 * b],
                T.dv[:].indirect(T.og[:, o0 + a:o0 + b]), T.tn[:, 16 * (u0 + a):16 * (u0 + b)], ADD)
 
     tiles = {"A": (T.za, T.ha, T.xa), "B": (T.zb, T.hb, T.xb)}
-
-    def made(t, k):
-        c = 12 * SPLIT[t] if k == "A" else 192 - 12 * SPLIT[t]
-        return c, max(c, 128), (0 if k == "A" else ZB)
 
     def unload(tile, key, t, c, bank0, scale):
         for b in range(4):
@@ -558,38 +520,36 @@ def rank_program(g, core, T, topo):
 
     def layer(t, k):
         z, h, _ = tiles[k]
-        c, w, a = made(t, k)
-        quant(["z%s0" % k, "z%s1" % k, "z%spad" % k], ["qz" + k], T.qz, T.sz, a, z[:, 0:4 * w], w)
+        _, c, a, _ = piece[k]
+        quant(["z%s0" % k, "z%s1" % k, "z%spad" % k], ["qz" + k], T.qz, T.sz, a, z[:])
         for b in range(4):
-            mm(["qz" + k, "w%d" % t], b, wc[t], wsc[t], 128 * b, T.qz, T.sz, a, w)
+            mm(["qz" + k, "w%d" % t], b, wc[t], wsc[t], 128 * b, T.qz, T.sz, a, 128)
         for b in range(4):
-            mm(["qz" + k, "eq%d" % b], 4 + b, T.eq, T.es, 128 * b, T.qz, T.sz, a, w, True, False)
+            mm(["qz" + k, "eq%d" % b], 4 + b, T.eq, T.es, 128 * b, T.qz, T.sz, a, 128, True, False)
         unload(h, "h" + k, t, c, 0, 0.03125)
-        quant(span("h" + k, 0, 4) + ["h%spad" % k], ["qh" + k], T.qh, T.sh, a, h[:, 0:4 * w], w)
+        quant(span("h" + k, 0, 4) + ["h%spad" % k], ["qh" + k], T.qh, T.sh, a, h[:])
 
     def new_state(t, k):
         x = tiles[k][2]
-        c, w, a = made(t, k)
+        _, c, a, _ = piece[k]
         for b in range(4):
-            mm(["qh" + k, "eq%d" % b], 4 + b, T.eq, T.es, 128 * b, T.qh, T.sh, a, w, False, True)
+            mm(["qh" + k, "eq%d" % b], 4 + b, T.eq, T.es, 128 * b, T.qh, T.sh, a, 128, False, True)
         name = "x" + k.lower()
         keys = span(name, 0, 4)
         if t == 0:
             for key in keys:
                 readers[key] = list(readers[name])
-            a = piece[k][2]
         unload(x, name, t, c, 4, None)
-        quant(keys + [name + "pad"], ["qv%s%d" % (k, t + 1)], qv[t + 1], sv[t + 1], a, x[:, 0:4 * w], w)
+        quant(keys + [name + "pad"], ["qv%s%d" % (k, t + 1)], qv[t + 1], sv[t + 1], a, x[:])
 
     def store(k, sem, queues):
-        c, w, a = made(1, k)
-        j0 = 0 if k == "A" else 192 - c
+        j0, c, a, _ = piece[k]
         key = ["qv%s2" % k]
-        mm(key + ["vq"], 0, T.vq, T.vs, 0, T.qv2, T.sv2, a, w)
-        dma(queues[0], sem[0], key, [], T.oc[:, 4 * j0:4 * (j0 + c)], bytes_of(T.qv2[:, a:a + c]), STORE)
+        mm(key + ["vq"], 0, T.vq, T.vs, 0, T.qc, T.sc, a, 128)
+        dma(queues[0], sem[0], key, [], T.oc[:, 4 * j0:4 * (j0 + c)], bytes_of(T.qc[:, a:a + c]), STORE)
         for i in range(4):
             j = i // 2
-            dma(queues[j], sem[j], key, [], T.osc[4 * i:4 * i + 4, j0:j0 + c], T.sv2[32 * i:32 * i + 4, a:a + c], STORE)
+            dma(queues[j], sem[j], key, [], T.osc[4 * i:4 * i + 4, j0:j0 + c], T.sc[32 * i:32 * i + 4, a:a + c], STORE)
         move("s" if k == "A" else "v", "y" + k, ["ps0"], ["y" + k], cyc(c), T.yb[:, j0:j0 + c], ps[0][:, 0:c])
         dma(queues[1], sem[1], ["y" + k], [], T.y[:, j0:j0 + c], T.yb[:, j0:j0 + c], STORE)
 

@@ -5,25 +5,41 @@ F32, BF, I32, U16, CODE, U8 = "float32", "bfloat16", "int32", "uint16", "float8_
 NA, NB, NH = 84, 108, 80
 BIG = 5.0e29
 EXCL = 1.0e29
-BIAS = 160
+PAD = 48
 HC = 128
 WS0 = 128
-PLANS = ({"cyc": 0.00095, "gat": 0.00125, "wake": 0.18, "halo0": 6.0, "halo1": 4.2, "w0": 15.0, "w1": 24.0},
-         {"cyc": 0.00085, "gat": 0.00100, "wake": 0.11, "halo0": 4.8, "halo1": 3.4, "w0": 12.0, "w1": 20.0},
-         {"cyc": 0.00115, "gat": 0.00155, "wake": 0.27, "halo0": 7.5, "halo1": 5.2, "w0": 18.7, "w1": 28.0})
+ROUNDS = (({"segs": (0, 7), "chase": (1, 2, 3), "dist": (3, 3), "lap": ((0, 7, 2),), "banks": (0, 0)},
+           {"segs": (7, 16), "chase": (1, 2, 3, 3), "dist": (3, 3, 3), "lap": ((7, 16, 2),), "banks": (4, 4)}),
+          ({"segs": (0, 7), "chase": (1, 2, 3), "dist": (3, 3), "lap": ((0, 7, 2),), "banks": (0, 0)},
+           {"segs": (7, 16), "chase": (1, 2, 3, 3), "dist": (3, 3, 3), "lap": ((7, 16, 2),), "banks": (4, 4)}))
+PLANS = ({"cyc": 0.00095, "gat": 0.00125, "wake": 0.18, "x": 1.8, "halo0": 5.0, "halo1": 3.6, "w0": 13.0, "w1": 24.0},
+         {"cyc": 0.00085, "gat": 0.00100, "wake": 0.11, "x": 1.5, "halo0": 4.0, "halo1": 2.6, "w0": 11.0, "w1": 20.0},
+         {"cyc": 0.00115, "gat": 0.00155, "wake": 0.27, "x": 2.6, "halo0": 7.0, "halo1": 5.0, "w0": 17.0, "w1": 28.0})
 TRIES = 10000
 STORE = 2.4
 
+
+def steps_of(part):
+    return max(part["segs"][0] - 1, 0), part["segs"][1] - 1
+
+
+PARTS = [p for r in ROUNDS for p in r]
+MOST = max(steps_of(p)[1] - steps_of(p)[0] for p in PARTS)
+DEEP = max(max(p["chase"]) for p in PARTS)
+TW = 16 * MOST
+
 SCRATCH = {}
-for _dt, _list in ((BF, "xa512 xb512 za512 zb512 ha512 hb512 ut512 vt512 et516 ex960 dv1088 tn768"),
+for _dt, _list in ((BF, "xa768 xb512 za768 zb512 ha768 hb512 ut512 vt512 et516 ex960 dv1136 tn832 nn240 pt240 pa240"),
                    (CODE, "eq512 uq128 ur128 vq128 qa336 qb336 qc256 qz256 qh256 wl512 wh256 wa512 wb512"),
                    (U8, "es512 us128 ux128 vs128 sa336 sb336 sc256 sz256 sh256 ls512 hs256 sx512 sy512"),
                    (I32, "si2 pi1 ci8"),
-                   (U16, "su2 ou8 ob36 od128 ot64 oe32 oz8 op16 ch64 og50"),
-                   (F32, "cf8 cx16 cr48 iw256 ie288 ib36 mk288 rs288 dd344 rr144 pa240 wn32 kb16 kk32 bf32 nd32 ne32 ia524 ta524 "
-                         "gg480 tt480 cc960 df960 ab960 mx964 mm240 nn240 pt240 tb480 tc480 pf16 pp32 yb192")):
+                   (U16, "su2 ou8 ob60 od128 ot64 oe32 ow32 op32 ca50 cb50 ga52 gb52 gd52 ge52"),
+                   (F32, "cf8 cx24 iw256 ie480 ib60 mk480 rs480 dd344 rr240 wn32 bf32 nd32 ne32 ia524 ta524 "
+                         "gg480 tt480 cc960 df960 ab960 mx968 mm240 pw512 na256 nb256 pp32 yb192")):
     for _n in _list.split():
         SCRATCH[_n[:2]] = ("sbuf", [128, int(_n[2:])], _dt)
+for _n in ("tb", "tc"):
+    SCRATCH[_n] = ("sbuf", [128, 2 * DEEP * TW], F32)
 for _b in range(8):
     SCRATCH["ps%d" % _b] = ("psum", [128, 512], F32)
 
@@ -89,6 +105,21 @@ def spare_engines(T, topo, r):
     return [e for e in topo.engines(c, helpers_of(T, topo, r)[0]) if e not in off]
 
 
+def tables_of(part):
+    need, s = {}, steps_of(part)[0]
+    for x in part["chase"]:
+        for j in range(1, x + 1):
+            need.setdefault((j, 0), set()).add(s)
+        if s + x < 15:
+            need.setdefault((x, 1), set()).add(s)
+        s += x
+    for x in range(max(part["chase"]), 1, -1):
+        for kind in range(2):
+            for i in need.get((x, kind), ()):
+                need.setdefault((x - 1, kind), set()).add(i + 1)
+    return {k: (min(v), max(v) + 1) for k, v in need.items()}
+
+
 def cyc(c):
     return (0.0, max(64, c), 0)
 
@@ -108,43 +139,57 @@ def priced(nodes, plan):
 
 def replay(nodes, queue, seq, price):
     cost, lat, wake = price
-    issued, end, free = {}, {}, {}
+    issued, end, free = [0.0] * len(nodes), [0.0] * len(nodes), {q: 0.0 for q in set(queue)}
     for i in seq:
-        t = free.get(queue[i], 0.0)
+        q = queue[i]
+        t = free[q]
         for j in nodes[i]["hard"]:
-            t = max(t, end[j] + wake)
+            if end[j] > t:
+                t = end[j]
         for j in nodes[i]["soft"]:
-            t = max(t, issued[j])
-        issued[i] = t + cost[i]
-        end[i] = issued[i] + lat[i]
-        if queue[i]:
-            free[queue[i]] = issued[i]
-    return max(end.values())
+            if issued[j] > t:
+                t = issued[j]
+        t += cost[i]
+        issued[i] = t
+        end[i] = t + lat[i] + wake
+        if q:
+            free[q] = t
+    return max(end) - wake
 
 
 def lay_out(nodes, after, queue, rank, look, price):
     cost, lat, wake = price
     left = [len(nd["hard"]) + len(nd["soft"]) for nd in nodes]
     avail = [0.0] * len(nodes)
-    ready = [i for i in range(len(nodes)) if left[i] == 0]
-    free, seq = {q: 0.0 for q in queue}, []
-    while ready:
-        first = min(ready, key=lambda i: max(avail[i], free[queue[i]]))
-        q = queue[first]
+    ready = {q: [] for q in set(queue)}
+    for i in range(len(nodes)):
+        if left[i] == 0:
+            ready[queue[i]].append(i)
+    free, seq = {q: 0.0 for q in ready}, []
+    for _ in nodes:
+        start, q, first = 1e9, None, None
+        for k in ready:
+            if ready[k]:
+                i = min(ready[k], key=lambda x: avail[x])
+                s = max(avail[i], free[k])
+                if s < start:
+                    start, q, first = s, k, i
         i = first
-        if q:
-            limit = max(avail[first], free[q]) + look * cost[first]
-            i = max([k for k in ready if queue[k] == q and avail[k] <= limit], key=lambda k: rank[k])
+        if q and len(ready[q]) > 1:
+            limit = start + look * cost[first]
+            i = max([k for k in ready[q] if avail[k] <= limit], key=lambda x: rank[x])
         t = max(avail[i], free[q]) + cost[i]
         if q:
             free[q] = t
         seq.append(i)
-        ready.remove(i)
+        ready[q].remove(i)
         for j, hard in after[i]:
-            avail[j] = max(avail[j], t + lat[i] + wake if hard else t)
+            e = t + lat[i] + wake if hard else t
+            if e > avail[j]:
+                avail[j] = e
             left[j] -= 1
             if left[j] == 0:
-                ready.append(j)
+                ready[queue[j]].append(j)
     return seq
 
 
@@ -222,7 +267,7 @@ def rank_program(g, core, T, topo):
                 soft.add(wrote[k])
         i = len(nodes)
         nodes.append({"q": q, "hard": sorted(hard), "soft": sorted(soft - hard), "call": call, "cost": cost, "lat": lat,
-                      "sem": sem, "inc": inc, "group": group})
+                      "sem": sem, "inc": inc, "group": group, "name": (list(writes) + list(reads))[0]})
         for k in reads:
             readers.setdefault(k, []).append(i)
         for k in list(writes) + list(behind):
@@ -253,6 +298,7 @@ def rank_program(g, core, T, topo):
     ps = [T["ps%d" % b] for b in range(8)]
     qv, sv = [T.qa, T.qb, T.qc], [T.sa, T.sb, T.sc]
     wc, wsc = [T.wa, T.wb], [T.sx, T.sy]
+    ch, nw, og = [T.ca, T.cb], [T.na, T.nb], [[T.ga, T.gb], [T.gd, T.ge]]
     e1 = len(topo.engines(nxt, core))
     arrives("w0", 2 * e1 + sum(len(topo.engines(h, core)) for h in helpers_of(T, topo, (rank + 1) % n)))
     arrives("w1", 4 * sum(len(topo.engines(h, core)) for h in helpers_of(T, topo, (rank + 2) % n)))
@@ -293,8 +339,8 @@ def rank_program(g, core, T, topo):
             return S.activation(out, src, COPY)
         node(q, reads, writes, call, cost, sem="own", group=group)
 
-    def quant(reads, writes, q, s, a, tile):
-        op("v", reads, writes, lambda: V.quantize_mx(q[:, a:a + 128], s[:, a:a + 128], tile), fixed(0.125))
+    def quant(reads, writes, q, s, a, tile, cols=128):
+        op("v", reads, writes, lambda: V.quantize_mx(q[:, a:a + cols], s[:, a:a + cols], tile), fixed(0.012 + 0.00088 * cols))
 
     def mm(reads, bank, lq, ls, la, rq, rs, ra, cols, start=True, stop=True):
         key = "ps%d" % bank
@@ -318,12 +364,16 @@ def rank_program(g, core, T, topo):
         node("g", reads, [], lambda _q: g.remote_dma_fused(trs, local_sem=T.sem.sent), fixed(0.3), behind=["g"])
         sent[0] += 2 * half
 
-    def iota(key, out, pattern, base, cost):
-        op("g", [], [key], lambda: g.iota(out, pattern, base, 0, allow_small_or_imprecise_dtypes=True), fixed(cost), behind=["g"])
+    def iota(key, out, pattern, base, c):
+        op("g", [], [key], lambda: g.iota(out, pattern, base, 0, allow_small_or_imprecise_dtypes=True),
+           fixed(0.13 + 0.002 * c), behind=["g"])
+
+    def span(name, a, b):
+        return ["%s%d" % (name, i) for i in range(a, b)]
 
     WD = 512 - 2 * HC
-    dma("s", "lws0", [], ["ws0"], T.ls[:, 0:WS0], T.ws[:, 0:WS0], 1.9)
-    dma("y", "lxa", [], ["xa"], T.xa[:, 0:4 * NA], T.x[:, 0:4 * NA], 2.6)
+    dma("y", "lxa", [], ["xa"], T.xa[:, 0:4 * NA], T.x[:, 0:4 * NA], "x")
+    dma("s", "lws0", [], ["ws0"], T.ls[:, 0:WS0], T.ws[:, 0:WS0], "x")
     dma("s", "lst", [], ["sti"], T.si[:], T.st[:], 2.9)
     dma("y", "lwh", [], ["wlh"], bytes_of(T.wl[:, WD:512]), T.wc[:, 4 * WD:2048], 3.7)
     dma("y", "lu", [], ["ut"], T.ut[:], T.u[:], 4.6)
@@ -334,36 +384,33 @@ def rank_program(g, core, T, topo):
     EQ = AluOpType.is_equal
     s0 = WS0 // 2
     op("g", [], ["pi"], lambda: g.iota(T.pi[:], [[0, 1]], 0, 1), fixed(0.13), behind=["g"])
-    iota("iw", T.iw[:], [[1, 256]], 0, 0.66)
-    iota("i8", T.ie[:], [[0, 36], [1, 8]], 0, 0.73)
+    iota("iw", T.iw[:], [[1, 256]], 0, 256)
     to_helpers(["ws0"], [T.ls[:, 0:s0], T.ls[:, s0:WS0]], T.hs[:, 0:s0], T.sem.hp0)
-    iota("i36", T.ib[:], [[32, 9], [0, 4]], 7, 0.2)
     fill("xapad", 88, T.xa[:, 4 * NA:512], 0.0)
+    quant(["xa", "xapad"], ["qvA0"], T.qa, T.sa, 0, T.xa[:, 0:512])
+    send_halo(0)
+    iota("i8", T.ie[:, 0:32 * MOST], [[0, 4 * MOST], [1, 8]], 0, 32 * MOST)
+    iota("i36", T.ib[:, 0:4 * MOST], [[32, MOST], [0, 4]], 7, 4 * MOST)
     fill("xbpad", 40, T.xb[:, 4 * NB:512], 0.0)
     fill("et", 258, T.et[:], 0.0)
     SHR, AND = AluOpType.logical_shift_right, AluOpType.bitwise_and
-    ts(["pi"], ["ci0"], 1, T.ci[:, 0:1], T.pi[:], 15, None, AND)
-    ts(["pi"], ["ci1"], 1, T.ci[:, 1:2], T.pi[:], 2, 3, SHR, AND)
-    ts(["pi"], ["ci2"], 1, T.ci[:, 2:3], T.pi[:], 3, None, AND)
-    ts(["pi"], ["ci3"], 1, T.ci[:, 3:4], T.pi[:], 3, 1, SHR, AND)
-    ts(["pi"], ["ci4"], 1, T.ci[:, 4:5], T.pi[:], 7, None, AND)
-    ts(["pi"], ["ci5"], 1, T.ci[:, 5:6], T.pi[:], 127, None, AND)
+    for i, (sh, low) in enumerate(((0, 15), (2, 3), (0, 3), (3, 1), (0, 7), (0, 127), (0, 1))):
+        ts(["pi"], ["ci%d" % i], 1, T.ci[:, i:i + 1], T.pi[:], sh, low, SHR, AND)
     fill("exa", 120, T.ex[:, 0:960:4], -BIG)
-    cp(["ci0", "ci1", "ci2", "ci3", "ci4", "ci5"], ["cf"], cyc(6), T.cf[:, 0:6], T.ci[:, 0:6])
+    cp(span("ci", 0, 7), ["cf"], cyc(7), T.cf[:, 0:7], T.ci[:, 0:7])
     fill("exc", 120, T.ex[:, 2:960:4], 0.0)
     fill("exd", 120, T.ex[:, 3:960:4], 0.0)
-    c_r, c_r4, c_m4, c_hi, c_m8, c_p = [T.cf[:, i:i + 1] for i in range(6)]
-    c_lo, c_8m4, c_rho, c_sig, c_bias = [T.cx[:, i:i + 1] for i in range(5)]
+    fill("dvpad", 24, T.dv[:, 0:PAD], 0.0)
+    c_r, c_r4, c_m4, c_hi, c_m8, c_p, c_m2 = [T.cf[:, i:i + 1] for i in range(7)]
+    c_lo, c_8m4, c_rho, c_sig, c_r12, c_rp, c_x1 = [T.cx[:, i:i + 1] for i in range(7)]
+    c_bias = {x: T.cx[:, 15 + x:16 + x] for x in range(1, DEEP + 1)}
     cp(["iw"], ["ou"], cyc(8), T.ou[:], T.iw[:, 0:128:16])
     ts(["iw", "cf"], ["et"], 128, T.et[:, 3:515:4], T.iw[:, 0:128], c_p, None, EQ)
     ts(["cf"], ["c_rho"], 1, c_rho, c_m4, 3.0, c_r4, MUL, ADD)
     ts(["cf"], ["c_sig"], 1, c_sig, c_hi, 3.0, c_m8, MUL, ADD)
-    ts(["cf"], ["c_bias"], 1, c_bias, c_r, 2.0, float(BIAS), MIN, MUL)
     for b in range(4):
         quant(["et"], ["eq%d" % b], T.eq, T.es, 128 * b, T.et[:, 3 - b:515 - b])
 
-    quant(["xa", "xapad"], ["qvA0"], T.qa, T.sa, 0, T.xa[:])
-    send_halo(0)
     quant(["ut"], ["uq"], T.uq, T.us, 0, T.ut[:])
     quant(["xb", "xbpad"], ["qvB0"], T.qa, T.sa, 128, T.xb[:])
     cp(["uq", "ou"], ["urq"], gat(128), T.ur[:].bitcast(dt.uint32), T.uq[:].bitcast(dt.uint32).indirect(T.ou[:]))
@@ -379,25 +426,49 @@ def rank_program(g, core, T, topo):
     to_helpers(["wls"], [T.ls[:, WS0:256 + s0], T.ls[:, 256 + s0:512]], T.hs[:, s0:256], T.sem.hp3)
     quant(["vt"], ["vq"], T.vq, T.vs, 0, T.vt[:])
 
+    def flat(key, out, c, value, reads=()):
+        act(["iw"] + list(reads), [key], cyc(c), out, T.iw[:, 0:c], IDENT, scale=0.0, bias=value)
+
     act(["cf"], ["c_lo"], cyc(1), c_lo, c_hi, IDENT, scale=-1.0, bias=1.0)
     act(["cf"], ["c_8m4"], cyc(1), c_8m4, c_m4, COPY, scale=8.0)
-    act(["cf", "iw"], ["cr"], cyc(48), T.cr[:], T.iw[:, 0:48], IDENT, bias=c_r)
-    act(["iw"], ["d1e"], cyc(172), T.dd[:, 0:344:2], T.iw[:, 0:172], COPY, scale=0.0)
-    act(["iw", "c_lo"], ["d1o"], cyc(172), T.dd[:, 1:344:2], T.iw[:, 0:172], IDENT, scale=0.0, bias=c_lo)
-    act(["iw"], ["rr"], cyc(144), T.rr[:], T.iw[:, 0:144], COPY, scale=0.0)
-    act(["iw"], ["rr"], cyc(9), T.rr[:, 0:144:16], T.iw[:, 0:9], IDENT, scale=0.0, bias=BIG)
-    act(["iw"], ["mxpad"], cyc(4), T.mx[:, 0:4], T.iw[:, 0:4], COPY)
-    act(["i8"], ["rs8"], cyc(288), T.rs[:], T.ie[:], SIGN)
-    act(["iw"], ["kb0"], cyc(6), T.kb[:, 0:6], T.iw[:, 0:96:16], COPY, scale=-1.0)
-    act(["iw"], ["kb1"], cyc(10), T.kb[:, 6:16], T.iw[:, 0:160:16], COPY, scale=-1.0)
-    act(["iw"], ["p1"], cyc(240), T.pa[:], T.iw[:, 0:240], IDENT, scale=0.0, bias=-1.0)
-    act(["iw"], ["p1"], cyc(5), T.pa[:, 15:80:16], T.iw[:, 31:96:16], COPY)
-    act(["iw"], ["p1"], cyc(10), T.pa[:, 95:240:16], T.iw[:, 15:160:16], COPY)
-    for h, tb in ((1, T.tb), (2, T.tc)):
-        for x in range(3):
-            act(["iw"], ["tb%d%d" % (h, x)], cyc(BIAS), tb[:, BIAS * x:BIAS * x + BIAS], T.iw[:, 0:BIAS], COPY, scale=0.0)
-    for tile, key, c in ((T.za, "zApad", NA), (T.ha, "hApad", NA), (T.zb, "zBpad", NB), (T.hb, "hBpad", NB)):
-        fill(key, 256 - 2 * c, tile[:, 4 * c:512], 0.0)
+    act(["cf"], ["c_r12"], cyc(1), c_r12, c_r, IDENT, bias=12.0)
+    act(["cf"], ["c_rp"], cyc(1), c_rp, c_r, IDENT, bias=float(PAD))
+    act(["cf"], ["c_x1"], cyc(1), c_x1, c_m2, IDENT, scale=-2.0, bias=c_r)
+    flat("d1e", T.dd[:, 0:344:2], 172, 0.0)
+    flat("d1o", T.dd[:, 1:344:2], 172, c_lo, ["c_lo"])
+    flat("rr", T.rr[:, 0:TW], TW, 0.0)
+    flat("rr", T.rr[:, 0:TW:16], MOST, BIG)
+    act(["i8"], ["rs8"], cyc(32 * MOST), T.rs[:, 0:32 * MOST], T.ie[:, 0:32 * MOST], SIGN)
+    flat("p1", T.pa[:, 0:TW], TW, -1.0)
+    act(["iw"], ["p1"], cyc(MOST), T.pa[:, 15:TW:16], T.iw[:, 31:TW + 16:16], COPY)
+    for h, tb in enumerate((T.tb, T.tc)[:max(len(r) for r in ROUNDS)]):
+        deep = max(max(r[h]["chase"]) for r in ROUNDS if len(r) > h)
+        for x in range(2 * deep):
+            flat("tb%d%d" % (h, x), tb[:, TW * x:TW * x + TW], TW, 0.0)
+    for t in range(2):
+        for h, part in enumerate(ROUNDS[t]):
+            a = 64 * steps_of(part)[0] + 4 * h
+            if t == 0 or steps_of(part)[0] != steps_of(ROUNDS[0][h])[0]:
+                flat("mxpad%d" % a, T.mx[:, a:a + 4], 4, 0.0)
+    for h, tiles_h in enumerate(((T.za, T.ha), (T.zb, T.hb))):
+        c = min(12 * (r[h]["segs"][1] - r[h]["segs"][0]) for r in ROUNDS if len(r) > h)
+        for tile, key in zip(tiles_h, "zh"):
+            fill("%s%spad" % (key, "AB"[h]), 256 - 2 * c, tile[:, 4 * c:512], 0.0)
+    for x in sorted(set(x for p in PARTS for x in p["chase"])):
+        ts(["c_x1"], ["c_t%d" % x], 1, c_bias[x], c_x1, float(2 * x - 2), 1.0, MIN, ADD)
+        ts(["c_t%d" % x], ["c_t%d" % x], 1, c_bias[x], c_bias[x], float(TW), None, MUL)
+    same = [p["chase"] for p in ROUNDS[0]] == [p["chase"] for p in ROUNDS[1]]
+    if same:
+        nw[1] = nw[0]
+    for t in range(1 if same else 2):
+        flat("nw%d" % t, nw[t][:], 256, 0.0)
+        for part in ROUNDS[t]:
+            s = a = steps_of(part)[0]
+            for x in part["chase"]:
+                if s > 0:
+                    act(["iw", "c_t%d" % x], ["nw%d" % t], cyc(16), nw[t][:, 16 * s:16 * s + 16],
+                        T.iw[:, 16 * (s - a):16 * (s - a) + 16], IDENT, bias=c_bias[x])
+                s += x
 
     cp(["sti"], ["stu"], cyc(2), T.su[:], T.si[:])
     ts(["iw", "c_rho"], ["c_q"], 4, T.cx[:, 8:12], T.iw[:, 0:16:4], c_rho, None, ADD)
@@ -410,23 +481,23 @@ def rank_program(g, core, T, topo):
     for q in range(4):
         ts(["bf", "c_q"], ["oc%d" % q], 32, T.od[:, q:128:4], T.bf[:], T.cx[:, 8 + q:9 + q], 2.0, ADD, MUL)
     ts(["ne"], ["oe"], 31, T.oe[:, 0:31], T.ne[:, 0:31], 28.0, None, MIN)
-    ts(["iw", "cr"], ["win"], 32, T.wn[:], T.iw[:, 0:32], T.cr[:, 12:13], EXCL, EQ, MUL)
-    ts(["i8", "cf"], ["m2"], 288, T.mk[:], T.ie[:], c_m8, None, EQ)
-    ts(["i36", "c_8m4"], ["ob"], 36, T.ob[:], T.ib[:], c_8m4, None, ADD)
-    KB = ["kb0", "kb1"]
-    ts(KB + ["c_bias"], KB, 4, T.kb[:, 0:7:2], T.kb[:, 0:7:2], c_bias, None, SUB)
-    ts(KB + ["c_bias"], KB, 3, T.kb[:, 9:16:3], T.kb[:, 9:16:3], c_bias, None, SUB)
-    cp(["c_bias"], ["ch0"], cyc(1), T.ch[:, 0:1], c_bias)
-    for m in range(3):
-        ts(["bf", "cr"], ["oz%d" % m], 2, T.oz[:, m:8:4], T.bf[:, 0:32:16], 4.0, T.cr[:, 16 * m:16 * m + 1], MUL, ADD)
+    ts(["iw", "c_r12"], ["win"], 32, T.wn[:], T.iw[:, 0:32], c_r12, EXCL, EQ, MUL)
+    ts(["i8", "cf"], ["m2"], 32 * MOST, T.mk[:, 0:32 * MOST], T.ie[:, 0:32 * MOST], c_m8, None, EQ)
+    ts(["i36", "c_8m4"], ["ob"], 4 * MOST, T.ob[:, 0:4 * MOST], T.ib[:, 0:4 * MOST], c_8m4, None, ADD)
+    ts(["bf", "cf"], ["ow"], 32, T.ow[:], T.bf[:], c_r, None, ADD)
     for t in range(2):
-        tt(["bf"] + KB, ["kk%d" % t], cyc(32), T.kk[:, 16 * t:16 * t + 16], T.bf[:, 16 * t:16 * t + 16], T.kb[:], ADD)
+        act(["iw", "ow", "c_rp"], ["pw%d" % t], gat(256), T.pw[:, 256 * t:256 * t + 256],
+            T.iw[:].indirect(T.ow[:, 16 * t:16 * t + 16]), IDENT, scale=4.0, bias=c_rp)
+        first = T.pw[:, 256 * t:256 * t + 1]
+        x = ROUNDS[t][0]["chase"][0]
+        cp(["c_t%d" % x], ["ch%d" % t], cyc(1), ch[t][:, 0:1], c_bias[x])
+        cp(["pw%d" % t], ["seg%d_0" % t], cyc(1), ch[t][:, 1:2], first)
+        ts(["iw", "pw%d" % t], ["oz%d" % t], 4, og[t][0][:, 0:4], T.iw[:, 0:64:16], first, -16.0 - PAD, ADD, ADD)
 
     piece = {"A": (0, NA, 0, 0), "B": (NA, NB, 128, 0), "H": (NA + NB, NH, 208, 48)}
 
-    def scores(t, k, bank):
-        keys = ["qvB%d" % t, "halo%d" % t] if k == "H" else ["qv%s%d" % (k, t)]
-        mm(UR + keys, bank, T.ur, T.ux, 0, qv[t], sv[t], piece[k][2], 128)
+    def window_keys(t, k):
+        return ["qvB%d" % t, "halo%d" % t] if k == "H" else ["qv%s%d" % (k, t)]
 
     def plain(k, bank, group):
         j0, c, _, r0 = piece[k]
@@ -439,162 +510,181 @@ def rank_program(g, core, T, topo):
         move(q, group, ["cf", "ps%d" % bank], ["m" + k], cyc(b - a), T.ia[:, 2 * (a - 8) + 1:2 * (b - 8):2],
              ps[bank][:, r0 + a - j0:r0 + b - j0], scale=c_hi)
 
+    def scores(t, k, banks):
+        for bank in sorted(set(banks)):
+            mm(UR + window_keys(t, k), bank, T.ur, T.ux, 0, qv[t], sv[t], piece[k][2], 128)
+        plain(k, banks[0], "e%d%s%d" % (t, k, banks[0]))
+        masked(k, banks[1], "s" if banks[0] == banks[1] else "v", "e%d%s%d" % (t, k, banks[1]))
+
     def shift(a, b, reads, key):
         scan(reads + ["d1e", "d1o"], [key], 2 * (b - a), T.ta[:, 2 * a:2 * b], T.dd[:, 0:2 * (b - a)], T.ia[:, 2 * a:2 * b], MUL, ADD)
 
-    def decode(t, reads, ra, cols, parts):
+    def decode(t, k, banks):
+        j0, c, ra, r0 = piece[k]
         for b in range(4):
-            mm(["eq%d" % b] + reads, 4 + b, T.eq, T.es, 128 * b, qv[t], sv[t], ra, cols)
-            for k, r0 in parts:
-                j0, c = piece[k][0], piece[k][1]
-                move("s", "dv%d%d%d" % (t, ra, b), ["ps%d" % (4 + b)], ["dv%s%d" % (k, b)], cyc(c),
-                     T.dv[:, 4 * j0 + b:4 * (j0 + c):4], ps[4 + b][:, r0:r0 + c], scale=0.5)
+            mm(["eq%d" % b] + window_keys(t, k), banks[b], T.eq, T.es, 128 * b, qv[t], sv[t], ra, 128)
+            move("s", "dv%d%s%d" % (t, k, b), ["ps%d" % banks[b]], ["dv%s%d" % (k, b)], cyc(c),
+                 T.dv[:, PAD + 4 * j0 + b:PAD + 4 * (j0 + c):4], ps[banks[b]][:, r0:r0 + c], scale=0.5)
 
-    DV = ["dv%s%d" % (k, b) for k in "ABH" for b in range(4)]
+    DV = ["dvpad"] + ["dv%s%d" % (k, b) for k in "ABH" for b in range(4)]
     I1 = ["nA", "nB", "nH", "mA", "mB", "mH"]
     T1 = ["t1a", "t1b", "t1c"]
 
-    def span(name, a, b):
-        return ["%s%d" % (name, i) for i in range(a, b)]
-
     def search(t, h):
-        a, b = (0, 6) if h == 1 else (6, 15)
+        part = ROUNDS[t][h]
+        a, b = steps_of(part)
         c0, k, name = 64 * t + 4, b - a, "%d%d" % (t, h)
-        move("s", "ex" + name, ["win", "oe"], ["ex%d" % h], gat(16 * k), T.ex[:, 64 * a + 1:64 * b:4],
-             T.wn[:].indirect(T.oe[:, 16 * t + a:16 * t + b]))
-        tt(T1 + ["o20", "o21", "m2"], ["g2%d" % h], gat(32 * k), T.gg[:, 32 * a:32 * b],
+        m0 = 64 * a + 4 * h
+        e0 = a - a % 2
+        move("s", "ex" + name, ["win", "oe"], span("ex", e0, b), gat(16 * (b - e0)), T.ex[:, 64 * e0 + 1:64 * b:4],
+             T.wn[:].indirect(T.oe[:, 16 * t + e0:16 * t + b]))
+        tt(T1 + ["o20", "o21", "m2"], span("g2", a, b), gat(32 * k), T.gg[:, 32 * a:32 * b],
            T.ta[:, 24:524].indirect(T.ot[:, 32 * t + 2 * a:32 * t + 2 * b]), T.mk[:, 0:32 * k], MUL)
-        scan(["g2%d" % h, "rs8"], ["tt%d" % h], 32 * k, T.tt[:, 32 * a:32 * b], T.rs[:, 0:32 * k], T.gg[:, 32 * a:32 * b], MUL, ADD)
-        for i in range(a, b, 3):
-            j = i + 3
-            move("s", "cc%d%d" % (t, i), I1 + span("oc", 0, 4), ["cc%d" % i], gat(192), T.cc[:, 64 * i:64 * j],
+        scan(span("g2", a, b) + ["rs8"], span("tt", a, b), 32 * k, T.tt[:, 32 * a:32 * b], T.rs[:, 0:32 * k], T.gg[:, 32 * a:32 * b], MUL, ADD)
+        i, pads = a, [key for key in wrote if key.startswith("mxpad")]
+        for d in part["dist"]:
+            j = i + d
+            move("s", "cc%d%d" % (t, i), I1 + span("oc", 0, 4), span("cc", i, j), gat(64 * d), T.cc[:, 64 * i:64 * j],
                  T.ia[:].indirect(T.od[:, c0 + 4 * i:c0 + 4 * j]))
-            tt(["tt%d" % h, "ob", "cc%d" % i], ["df%d" % i], gat(192), T.df[:, 64 * i:64 * j],
+            tt(span("tt", a, b) + ["ob"] + span("cc", i, j), span("df", i, j), gat(64 * d), T.df[:, 64 * i:64 * j],
                T.tt[:, 32 * a:32 * b].indirect(T.ob[:, 4 * (i - a):4 * (j - a)]), T.cc[:, 64 * i:64 * j], SUB)
-            act(["df%d" % i], ["ab%d" % i], cyc(192), T.ab[:, 64 * i:64 * j], T.df[:, 64 * i:64 * j], ABS)
-            scan(["ab%d" % i, "ex%d" % h, "exa", "exc", "exd"], ["mx%d" % i], 192,
-                 T.mx[:, 4 + 64 * i:4 + 64 * j], T.ex[:, 64 * i:64 * j], T.ab[:, 64 * i:64 * j], ADD, MAX)
-        MX = ["mx%d" % i for i in range(a, b, 3)]
-        scan(["mxpad", "rr", "mx3"] + MX, ["mm%d" % h], 16 * k, T.mm[:, 16 * a:16 * b], T.mx[:, 3 + 64 * a:64 * b:4], T.rr[:, 0:16 * k], MIN, MAX)
-        tt(MX + ["mm%d" % h], ["nn%d" % h], cyc(32 * k), T.nn[:, 16 * a:16 * b], T.mx[:, 7 + 64 * a:4 + 64 * b:4],
+            act(span("df", i, j), span("ab", i, j), cyc(64 * d), T.ab[:, 64 * i:64 * j], T.df[:, 64 * i:64 * j], ABS)
+            scan(span("ab", i, j) + span("ex", i, j) + ["exa", "exc", "exd"] + pads, span("mx", i, j), 64 * d,
+                 T.mx[:, m0 + 4 + 64 * (i - a):m0 + 4 + 64 * (j - a)], T.ex[:, 64 * i:64 * j], T.ab[:, 64 * i:64 * j], ADD, MAX)
+            i = j
+        MX = span("mx", a, b)
+        scan(["rr"] + MX, span("mm", a, b), 16 * k, T.mm[:, 16 * a:16 * b], T.mx[:, m0 + 3:m0 + 64 * k:4], T.rr[:, 0:16 * k], MIN, MAX)
+        tt(MX + span("mm", a, b), span("nn", a, b), cyc(32 * k), T.nn[:, 16 * a:16 * b], T.mx[:, m0 + 7:m0 + 4 + 64 * k:4],
            T.mm[:, 16 * a:16 * b], AluOpType.is_ge)
-        scan(["nn%d" % h, "p1"], ["pt%d" % h], 16 * k, T.pt[:, 16 * a:16 * b], T.nn[:, 16 * a:16 * b], T.pa[:, 16 * a:16 * b], MUL, ADD)
-        cp(["pt%d" % h], ["op%d" % h], cyc(k), T.op[:, a:b], T.pt[:, 16 * a + 15:16 * b:16])
-        tb, src, key = (T.tb, T.tc)[h - 1], T.iw[:], "iw"
-        for x in range(h + 1):
-            c = 16 * (k - x)
-            out = tb[:, BIAS * x:BIAS * x + c]
-            move("s", "tf%s%d" % (name, x), [key, "c_bias", "op%d" % h], ["tb%d%d" % (h, x)], gat(c), out,
-                 src.indirect(T.op[:, a:b - x]), bias=c_bias if x == h else None)
-            src, key = out, "tb%d%d" % (h, x)
-        for s in range(a, b, h + 1):
-            cp(span("tb%d" % h, 0, 3) + ["ch0", "ch"], ["ch", "ch%d" % h] + ["ch2"] * (s == 0), gat(16),
-               T.ch[:, 2 * s + 2:2 * s + 34:2], tb[:].indirect(T.ch[:, 2 * s:2 * s + 1]))
-        a, b, c = (0, 7, 0) if h == 1 else (7, 16, 22)
-        cp(["ch%d" % h, "ch0"], ["pf%d" % h], cyc(9), T.pf[:, a:b], T.ch[:, 2 * a:2 * b:2])
-        tt(["pf%d" % h, "kk%d" % t], ["pp" + name], cyc(18), T.pp[:, 16 * t + a:16 * t + b], T.pf[:, a:b], T.kk[:, 16 * t + a:16 * t + b], ADD)
-        for m in range(3):
-            ts(["pp" + name, "cr"], ["og%d%d" % (h, m)], 9, T.og[:, c + m:c + 3 * (b - a):3], T.pp[:, 16 * t + a:16 * t + b],
-               4.0, T.cr[:, 16 * m:16 * m + 1], MUL, ADD)
+        scan(span("nn", a, b) + ["p1"], span("pt", a, b), 8 * k, T.pt[:, 16 * a:16 * b], T.nn[:, 16 * a:16 * b], T.pa[:, 0:16 * k], MUL, ADD)
+        ob = 16 * h
+        cp(span("pt", a, b), ["op%d" % h], cyc(k), T.op[:, ob:ob + k], T.pt[:, 16 * a + 15:16 * b:16])
+        tb, need = (T.tb, T.tc)[h], tables_of(part)
+        for x, kind in sorted(need):
+            i, j = need[(x, kind)]
+            i -= (i - a) % 2
+            at = TW * (2 * x - 2 + kind)
+            if x == 1:
+                src, key = ((T.pw[:, 256 * t + 16 * a:256 * t + 16 * b + 16], "pw%d" % t),
+                            (nw[t][:, 16 * a:16 * b + 16], "nw%d" % (0 if same else t)))[kind]
+            else:
+                src, key = tb[:, at - 2 * TW:at - TW], "tb%d%d" % (h, 2 * x - 4 + kind)
+            move("sv"[kind], "tf%s%d%d" % (name, x, kind), [key, "op%d" % h], ["tb%d%d" % (h, 2 * x - 2 + kind)], gat(16 * (j - i)),
+                 tb[:, at + 16 * (i - a):at + 16 * (j - a)], src.indirect(T.op[:, ob + i - a:ob + j - a]))
+        s = a
+        for x in part["chase"]:
+            cp(span("tb%d" % h, 0, 2 * x) + ["ch%d" % t], ["ch%d" % t] + span("seg%d_" % t, s + 1, s + x + 1), gat(16),
+               ch[t][:, 2 * s + 2:2 * s + 18], tb[:, 0:2 * x * TW].indirect(ch[t][:, 2 * s:2 * s + 1]))
+            s += x
+        if b == 15:
+            ts(span("seg%d_" % t, 0, 16), ["pp%d" % t], 16, T.pp[:, 16 * t:16 * t + 16], ch[t][:, 1:32:2], -float(PAD), 0.25, ADD, MUL)
+
+    def cuts(a, b, parts, more):
+        marks = [a] + [min(b, a + ((b - a) * i // parts // 2) * 2 + more) for i in range(1, parts)] + [b]
+        return [(u, v) for u, v in zip(marks, marks[1:]) if v > u]
 
     def overlap(t, h):
-        og = span("og%d" % h, 0, 3)
-        if h == 1:
-            move("s", "tz%d" % t, DV + span("oz", 0, 3), span("tn", 0, 3), gat(48), T.tn[:, 0:48], T.dv[:].indirect(T.oz[:, 4 * t:4 * t + 3]))
-        o0, u0, cols, ncols = ((0, 0, 21, 21), (22, 21, 27, 24))[h - 1]
-        z, k = ((T.za, "A"), (T.zb, "B"))[h - 1]
-        m = ncols // 4 * 2
-        for i, (a, b) in enumerate(((0, m), (m, ncols))):
-            move("s", "tn%d%d%d" % (t, h, i), DV + og, span("tn", u0 + 3 + a, u0 + 3 + b), gat(16 * (b - a)),
-                 T.tn[:, 16 * (u0 + 3 + a):16 * (u0 + 3 + b)], T.dv[:, 48:1088].indirect(T.og[:, o0 + a:o0 + b]))
-        for i, (a, b) in enumerate(((0, m + 2), (m + 2, cols))):
-            tt(DV + og + span("tn", u0 + a, u0 + b), ["z%s%d" % (k, i)], gat(16 * (b - a)), z[:, 16 * a:16 * b],
-               T.dv[:].indirect(T.og[:, o0 + a:o0 + b]), T.tn[:, 16 * (u0 + a):16 * (u0 + b)], ADD)
+        s0, s1 = ROUNDS[t][h]["segs"]
+        o, z, k = og[t][h], (T.za, T.zb)[h], "AB"[h]
+        lead = 4 if h == 0 else 0
+        j0 = 3 * s0 + 4 - lead
+        keys = []
+        for sa, sb, calls in ROUNDS[t][h]["lap"]:
+            u, v = lead + 3 * (sa - s0), lead + 3 * (sb - s0)
+            made = span("og%d%d%d_" % (t, h, sa), 0, 3)
+            for m in range(3):
+                ts(span("seg%d_" % t, sa, sb), [made[m]], sb - sa, o[:, u + m:v:3], ch[t][:, 2 * sa + 1:2 * sb:2], 16.0 * m, None, ADD)
+            first = 0 if sa == 0 else u
+            for a, b in cuts(first, v - 3 * (sb == 16), calls, 0):
+                move("s", "tn%d%d%d" % (t, h, a), DV + made + ["oz%d" % t], span("tn", j0 + a, j0 + b), gat(16 * (b - a)),
+                     T.tn[:, 16 * (j0 + a):16 * (j0 + b)], T.dv[:, PAD:].indirect(o[:, a:b]))
+            for a, b in cuts(u, v, calls, 0 if sa == 0 else 2):
+                keys.append("z%s%d" % (k, len(keys)))
+                tt(DV + made + span("tn", j0 + a - 3, j0 + b - 3), keys[-1:], gat(16 * (b - a)),
+                   z[:, 16 * (a - lead):16 * (b - lead)], T.dv[:].indirect(o[:, a:b]), T.tn[:, 16 * (j0 + a - 3):16 * (j0 + b - 3)], ADD)
+        return keys
 
-    tiles = {"A": (T.za, T.ha, T.xa), "B": (T.zb, T.hb, T.xb)}
+    tiles = ((T.za, T.ha, T.xa), (T.zb, T.hb, T.xb))
 
     def unload(tile, key, t, c, bank0, scale):
         for b in range(4):
             move("sv"[b % 2], "%s%d%d" % (key, t, b), ["ps%d" % (bank0 + b)], ["%s%d" % (key, b)], cyc(c),
                  tile[:, b:4 * c:4], ps[bank0 + b][:, 0:c], scale=scale)
 
-    def layer(t, k):
-        z, h, _ = tiles[k]
-        _, c, a, _ = piece[k]
-        quant(["z%s0" % k, "z%s1" % k, "z%spad" % k], ["qz" + k], T.qz, T.sz, a, z[:])
-        for b in range(4):
-            mm(["qz" + k, "w%d" % t], b, wc[t], wsc[t], 128 * b, T.qz, T.sz, a, 128)
-        for b in range(4):
-            mm(["qz" + k, "eq%d" % b], 4 + b, T.eq, T.es, 128 * b, T.qz, T.sz, a, 128, True, False)
-        unload(h, "h" + k, t, c, 0, 0.03125)
-        quant(span("h" + k, 0, 4) + ["h%spad" % k], ["qh" + k], T.qh, T.sh, a, h[:])
+    def columns(t, h):
+        s0, s1 = ROUNDS[t][h]["segs"]
+        return 12 * s0, 12 * (s1 - s0), max(128, 12 * (s1 - s0))
 
-    def new_state(t, k):
-        x = tiles[k][2]
-        _, c, a, _ = piece[k]
+    def layer(t, h, zs):
+        z, hh, x = tiles[h]
+        k, a = "AB"[h], 128 * h
+        _, c, w = columns(t, h)
+        r0, x0 = ROUNDS[t][h]["banks"]
+        quant(zs + ["z%spad" % k], ["qz" + k], T.qz, T.sz, a, z[:, 0:4 * w], w)
         for b in range(4):
-            mm(["qh" + k, "eq%d" % b], 4 + b, T.eq, T.es, 128 * b, T.qh, T.sh, a, 128, False, True)
+            mm(["qz" + k, "w%d" % t], r0 + b, wc[t], wsc[t], 128 * b, T.qz, T.sz, a, w)
+        if r0 == x0:
+            unload(hh, "h" + k, t, c, r0, 0.03125)
+        for b in range(4):
+            mm(["qz" + k, "eq%d" % b], x0 + b, T.eq, T.es, 128 * b, T.qz, T.sz, a, w, True, False)
+        if r0 != x0:
+            unload(hh, "h" + k, t, c, r0, 0.03125)
+        quant(span("h" + k, 0, 4) + ["h%spad" % k], ["qh" + k], T.qh, T.sh, a, hh[:, 0:4 * w], w)
+        for b in range(4):
+            mm(["qh" + k, "eq%d" % b], x0 + b, T.eq, T.es, 128 * b, T.qh, T.sh, a, w, False, True)
         name = "x" + k.lower()
         keys = span(name, 0, 4)
         if t == 0:
             for key in keys:
                 readers[key] = list(readers[name])
-        unload(x, name, t, c, 4, None)
-        quant(keys + [name + "pad"], ["qv%s%d" % (k, t + 1)], qv[t + 1], sv[t + 1], a, x[:])
+        unload(x, name, t, c, x0, None)
+        quant(keys + [name + "pad"], ["qv%s%d" % (k, t + 1)], qv[t + 1], sv[t + 1], a, x[:, 0:4 * w], w)
 
-    def store(k, sem, queues):
-        j0, c, a, _ = piece[k]
+    def store(h, sem, queues):
+        j0, c, w = columns(1, h)
+        k, a, bank = "AB"[h], 128 * h, ROUNDS[1][h]["banks"][0]
         key = ["qv%s2" % k]
-        mm(key + ["vq"], 0, T.vq, T.vs, 0, T.qc, T.sc, a, 128)
+        mm(key + ["vq"], bank, T.vq, T.vs, 0, T.qc, T.sc, a, w)
         dma(queues[0], sem[0], key, [], T.oc[:, 4 * j0:4 * (j0 + c)], bytes_of(T.qc[:, a:a + c]), STORE)
         for i in range(4):
             j = i // 2
             dma(queues[j], sem[j], key, [], T.osc[4 * i:4 * i + 4, j0:j0 + c], T.sc[32 * i:32 * i + 4, a:a + c], STORE)
-        move("s" if k == "A" else "v", "y" + k, ["ps0"], ["y" + k], cyc(c), T.yb[:, j0:j0 + c], ps[0][:, 0:c])
+        move("sv"[h], "y" + k, ["ps%d" % bank], ["y" + k], cyc(c), T.yb[:, j0:j0 + c], ps[bank][:, 0:c])
         dma(queues[1], sem[1], ["y" + k], [], T.y[:, j0:j0 + c], T.yb[:, j0:j0 + c], STORE)
 
-    def early(t, k, bank):
-        scores(t, k, bank)
-        plain(k, bank, "e%d%s" % (t, k))
-        masked(k, bank, "s", "e%d%s" % (t, k))
-
-    def late(t, k):
-        scores(t, k, 2)
-        scores(t, k, 3)
-        plain(k, 2, "n%d%s" % (t, k))
-        masked(k, 3, "v", "m%d%s" % (t, k))
-
-    early(0, "A", 0)
-    early(0, "B", 1)
+    scores(0, "A", (0, 0))
+    scores(0, "B", (1, 1))
     shift(12, 184, ["nA", "nB", "mA", "mB"], "t1a")
-    decode(0, ["qvA0", "qvB0"], 0, 256, (("A", 0), ("B", 128)))
-    late(0, "H")
+    decode(0, "A", (4, 5, 6, 7))
+    decode(0, "B", (4, 5, 6, 7))
+    scores(0, "H", (2, 3))
     shift(184, 262, ["nB", "nH", "mH"], "t1b")
-    decode(0, ["qvB0", "halo0"], 208, 128, (("H", 48),))
-    for t in range(2):
-        search(t, 1)
-        overlap(t, 1)
-        layer(t, "A")
-        new_state(t, "A")
-        if t == 0:
-            send_halo(1)
-        search(t, 2)
-        overlap(t, 2)
-        if t == 1:
-            store("A", ("sta", "sta"), ("y", "y"))
-            dma("y", "sta", ["pp01", "pp02", "pp11", "pp12"], [], T.ol[:], T.pp[0:128:16, :], STORE)
-        layer(t, "B")
-        if t == 0:
-            early(1, "A", 0)
-            shift(12, 76, ["nA", "mA"], "t1a")
-        new_state(t, "B")
-        if t == 0:
-            early(1, "H", 1)
-            late(1, "B")
-            shift(192, 262, ["nH", "mH"], "t1c")
-            shift(76, 192, ["nA", "nB", "mB", "mH"], "t1b")
-            decode(1, ["qvA1", "qvB1", "halo1"], 0, 336, (("A", 0), ("B", 128), ("H", 256)))
-    store("B", ("stb", "stc"), ("y", "s"))
+    decode(0, "H", (4, 5, 6, 7))
+    search(0, 0)
+    layer(0, 0, overlap(0, 0))
+    send_halo(1)
+    search(0, 1)
+    zs = overlap(0, 1)
+    scores(1, "A", (0, 0))
+    shift(12, 76, ["nA", "mA"], "t1a")
+    decode(1, "A", (1, 2, 3, 0))
+    layer(0, 1, zs)
+    scores(1, "B", (4, 5))
+    shift(76, 184, ["nA", "nB", "mB"], "t1c")
+    scores(1, "H", (0, 1))
+    shift(184, 262, ["nB", "nH", "mH"], "t1b")
+    decode(1, "B", (6, 7, 4, 5))
+    decode(1, "H", (2, 3, 0, 1))
+    last = len(ROUNDS[1]) - 1
+    for h in range(last + 1):
+        search(1, h)
+        zs = overlap(1, h)
+        if h == last:
+            dma("y", "sta", ["pp0", "pp1"], [], T.ol[:], T.pp[0:128:16, :], STORE)
+        layer(1, h, zs)
+        if h < last:
+            store(h, ("sta", "sta"), ("y", "y"))
+    store(last, ("stb", "stc"), ("y", "s"))
 
     if "plan" not in PLANNED:
         PLANNED["plan"] = schedule(nodes)

@@ -3,48 +3,55 @@ from concourse.mybir import dt, AluOpType, ActivationFunctionType
 
 F32, BF, I32, U16, CODE, U8 = "float32", "bfloat16", "int32", "uint16", "float8_e4m3fn_x4", "uint8"
 NA, NB, NH = 84, 108, 80
+QB = 4 * NH
 BIG = 5.0e29
 EXCL = 1.0e29
 PAD = 48
 HC = 128
 WS0 = 128
-ROUNDS = (({"segs": (0, 7), "chase": (1, 2, 3), "dist": (3, 3), "lap": ((0, 7, 2),), "banks": (0, 0)},
-           {"segs": (7, 16), "chase": (1, 2, 3, 3), "dist": (3, 3, 3), "lap": ((7, 16, 2),), "banks": (4, 4)}),
-          ({"segs": (0, 7), "chase": (1, 2, 3), "dist": (3, 3), "lap": ((0, 7, 2),), "banks": (0, 0)},
-           {"segs": (7, 16), "chase": (1, 2, 3, 3), "dist": (3, 3, 3), "lap": ((7, 16, 2),), "banks": (4, 4)}))
-PLANS = ({"cyc": 0.00095, "gat": 0.00125, "wake": 0.18, "x": 1.8, "halo0": 5.0, "halo1": 3.6, "w0": 13.0, "w1": 24.0},
-         {"cyc": 0.00085, "gat": 0.00100, "wake": 0.11, "x": 1.5, "halo0": 4.0, "halo1": 2.6, "w0": 11.0, "w1": 20.0},
-         {"cyc": 0.00115, "gat": 0.00155, "wake": 0.27, "x": 2.6, "halo0": 7.0, "halo1": 5.0, "w0": 17.0, "w1": 28.0})
-TRIES = 10000
+ROUNDS = ({"temp": (3, 3, 9), "dist": (3, 3, 3, 3, 3), "alone": 12, "find": ((1, 2, 3), (1, 2, 3), (1, 2)),
+           "pieces": (((0, 7), ((0, 4, 1), (4, 7, 1)), (0, 0)), ((7, 16), ((7, 13, 1), (13, 16, 1)), (4, 4)))},
+          {"temp": (3, 3, 9), "dist": (3, 3, 3, 3, 3), "alone": 12, "find": ((1, 2, 3), (1, 2, 3), (1, 2)),
+           "pieces": (((0, 7), ((0, 4, 1), (4, 7, 1)), (0, 0)), ((7, 16), ((7, 13, 1), (13, 16, 1)), (4, 4)))})
+PLANS = ({"cyc": 0.00095, "gat": 0.00125, "wake": 0.18, "x": 1.6, "u": 2.8, "xb": 3.4, "st": 2.0,
+          "halo0": 3.9, "halo1": 3.5, "w0": 5.0, "w1": 24.0},
+         {"cyc": 0.00085, "gat": 0.00100, "wake": 0.11, "x": 1.6, "u": 2.4, "xb": 2.9, "st": 1.8,
+          "halo0": 3.0, "halo1": 2.6, "w0": 4.0, "w1": 20.0},
+         {"cyc": 0.00115, "gat": 0.00155, "wake": 0.27, "x": 2.4, "u": 3.9, "xb": 4.7, "st": 2.9,
+          "halo0": 5.5, "halo1": 5.0, "w0": 7.0, "w1": 28.0})
+TRIES = 45000
+SLACK = 0.3
+SEED = 1
 STORE = 2.4
 
 
-def steps_of(part):
-    return max(part["segs"][0] - 1, 0), part["segs"][1] - 1
+def runs(sizes):
+    return [(sum(sizes[:i]), sum(sizes[:i + 1])) for i in range(len(sizes))]
 
 
-PARTS = [p for r in ROUNDS for p in r]
-MOST = max(steps_of(p)[1] - steps_of(p)[0] for p in PARTS)
-DEEP = max(max(p["chase"]) for p in PARTS)
-TW = 16 * MOST
+PARTS = [p for r in ROUNDS for p in r["find"]]
+MOST = max(max(r["temp"]) for r in ROUNDS)
+LONG = max(sum(p) for p in PARTS)
+DEEP = max(max(p) for p in PARTS)
+TW = 16 * LONG
+NP = max(len(r["find"]) for r in ROUNDS)
 
 SCRATCH = {}
 for _dt, _list in ((BF, "xa768 xb512 za768 zb512 ha768 hb512 ut512 vt512 et516 ex960 dv1136 tn832 nn240 pt240 pa240"),
-                   (CODE, "eq512 uq128 ur128 vq128 qa336 qb336 qc256 qz256 qh256 wl512 wh256 wa512 wb512"),
-                   (U8, "es512 us128 ux128 vs128 sa336 sb336 sc256 sz256 sh256 ls512 hs256 sx512 sy512"),
+                   (CODE, "eq512 uq128 ur128 vq128 qa448 qb448 la208 lb208 qc256 qz256 qh256 wl512 wh256 wa512 wb512"),
+                   (U8, "es512 us128 ux128 vs128 sa448 sb448 ma448 mb448 sc256 sz256 sh256 ls512 hs256 sx512 sy512"),
                    (I32, "si2 pi1 ci8"),
-                   (U16, "su2 ou8 ob60 od128 ot64 oe32 ow32 op32 ca50 cb50 ga52 gb52 gd52 ge52"),
+                   (U16, "su2 ou8 ob60 od128 ot64 oe32 ow32 of256 op32 ca50 cb50 ga52 gb52 gd52 ge52"),
                    (F32, "cf8 cx24 iw256 ie480 ib60 mk480 rs480 dd344 rr240 wn32 bf32 nd32 ne32 ia524 ta524 "
                          "gg480 tt480 cc960 df960 ab960 mx968 mm240 pw512 na256 nb256 pp32 yb192")):
     for _n in _list.split():
         SCRATCH[_n[:2]] = ("sbuf", [128, int(_n[2:])], _dt)
-for _n in ("tb", "tc"):
-    SCRATCH[_n] = ("sbuf", [128, 2 * DEEP * TW], F32)
+SCRATCH["tb"] = ("sbuf", [128, NP * 2 * DEEP * TW], F32)
 for _b in range(8):
     SCRATCH["ps%d" % _b] = ("psum", [128, 512], F32)
 
 SEMAPHORES = ["cv", "cs", "cp", "cg", "sent", "halo0", "halo1", "w0", "w1", "hp0", "hp1", "hp2", "hp3",
-              "lxa", "lxb", "lst", "lu", "lv", "lwh", "lws0", "lws", "lwd", "sta", "stb", "stc"]
+              "lxa", "lxb", "lst", "lu", "lv", "lwh", "lws0", "lws", "lwd", "sta", "stb"]
 
 ADD, SUB, MUL, MAX, MIN = AluOpType.add, AluOpType.subtract, AluOpType.mult, AluOpType.max, AluOpType.min
 COPY, IDENT, ABS = ActivationFunctionType.Copy, ActivationFunctionType.Identity, ActivationFunctionType.Abs
@@ -91,11 +98,11 @@ def helper_program(g, core, T, topo, r, i):
     send(T.sy[:, first * i:first * i + first], T.hs[:, 0:first], T.sem.w1, d2)
     g.wait_ge(T.sem.hp1, got)
     send(bytes_of(T.wa[:, a:a + c]), bytes_of(T.wh[:, 0:c]), T.sem.w0, d1)
-    send(bytes_of(T.wb[:, a:a + c]), bytes_of(T.wh[:, 0:c]), T.sem.w1, d2)
     g.wait_ge(T.sem.hp2, got)
-    send(bytes_of(T.wb[:, b:b + d]), bytes_of(T.wh[:, c:c + d]), T.sem.w1, d2)
     g.wait_ge(T.sem.hp3, got)
-    send(T.sy[:, WS0 + rest * i:WS0 + rest * i + rest], T.hs[:, first:256], T.sem.w1, d2)
+    send(bytes_of(T.wb[:, a:a + c]), bytes_of(T.wh[:, 0:c]), T.sem.w1, d2)
+    send(bytes_of(T.wb[:, b:b + d]), bytes_of(T.wh[:, c:c + d]), T.sem.w1, d2)
+    send(T.sy[:, WS0 + rest * i:WS0 + rest * i + rest], T.hs[:, first:first + rest], T.sem.w1, d2)
     g.wait_ge(T.sem.sent, total[0])
 
 
@@ -105,15 +112,15 @@ def spare_engines(T, topo, r):
     return [e for e in topo.engines(c, helpers_of(T, topo, r)[0]) if e not in off]
 
 
-def tables_of(part):
-    need, s = {}, steps_of(part)[0]
-    for x in part["chase"]:
+def tables_of(s, chase):
+    need = {}
+    for x in chase:
         for j in range(1, x + 1):
             need.setdefault((j, 0), set()).add(s)
         if s + x < 15:
             need.setdefault((x, 1), set()).add(s)
         s += x
-    for x in range(max(part["chase"]), 1, -1):
+    for x in range(max(chase), 1, -1):
         for kind in range(2):
             for i in need.get((x, kind), ()):
                 need.setdefault((x - 1, kind), set()).add(i + 1)
@@ -157,87 +164,115 @@ def replay(nodes, queue, seq, price):
     return max(end) - wake
 
 
-def lay_out(nodes, after, queue, rank, look, price):
-    cost, lat, wake = price
-    left = [len(nd["hard"]) + len(nd["soft"]) for nd in nodes]
-    avail = [0.0] * len(nodes)
-    ready = {q: [] for q in set(queue)}
-    for i in range(len(nodes)):
-        if left[i] == 0:
-            ready[queue[i]].append(i)
-    free, seq = {q: 0.0 for q in ready}, []
-    for _ in nodes:
-        start, q, first = 1e9, None, None
-        for k in ready:
-            if ready[k]:
-                i = min(ready[k], key=lambda x: avail[x])
-                s = max(avail[i], free[k])
-                if s < start:
-                    start, q, first = s, k, i
-        i = first
-        if q and len(ready[q]) > 1:
-            limit = start + look * cost[first]
-            i = max([k for k in ready[q] if avail[k] <= limit], key=lambda x: rank[x])
-        t = max(avail[i], free[q]) + cost[i]
+def lay_out(order, before, queue, cost):
+    start = [0.0] * len(order)
+    busy = {q: ([], []) for q in set(queue)}
+    for i in order:
+        t = 0.0
+        for j, gap in before[i]:
+            e = start[j] + gap
+            if e > t:
+                t = e
+        q, c = queue[i], cost[i]
         if q:
-            free[q] = t
-        seq.append(i)
-        ready[q].remove(i)
-        for j, hard in after[i]:
-            e = t + lat[i] + wake if hard else t
-            if e > avail[j]:
-                avail[j] = e
-            left[j] -= 1
-            if left[j] == 0:
-                ready[queue[j]].append(j)
-    return seq
+            a, b = busy[q]
+            k = len(a)
+            while k and b[k - 1] > t:
+                k -= 1
+            while k < len(a) and a[k] < t + c - 1e-9:
+                if b[k] > t:
+                    t = b[k]
+                k += 1
+            a.insert(k, t)
+            b.insert(k, t + c)
+        start[i] = t
+    return start
 
 
 def schedule(nodes):
-    after = [[] for _ in nodes]
-    for i, nd in enumerate(nodes):
-        for j in nd["hard"]:
-            after[j].append((i, True))
-        for j in nd["soft"]:
-            after[j].append((i, False))
+    n = len(nodes)
     prices = [priced(nodes, p) for p in PLANS]
     cost, lat, wake = prices[0]
-    rank = [0.0] * len(nodes)
-    for i in range(len(nodes) - 1, -1, -1):
-        rank[i] = cost[i] + max([lat[i]] + [rank[j] + (lat[i] + wake if hard else 0.0) for j, hard in after[i]])
+    fore, back = [[] for _ in nodes], [[] for _ in nodes]
+    lean, above = [], []
+    for nd in nodes:
+        implied = 0
+        for j in nd["hard"]:
+            implied |= above[j]
+        lean.append({"hard": [j for j in nd["hard"] if not implied >> j & 1], "soft": nd["soft"]})
+        for j in nd["hard"]:
+            implied |= 1 << j
+        above.append(implied)
+    for i, nd in enumerate(lean):
+        for j in nd["hard"]:
+            fore[i].append((j, cost[j] + lat[j] + wake))
+            back[j].append((i, cost[i] + lat[j] + wake))
+        for j in nd["soft"]:
+            fore[i].append((j, cost[j]))
+            back[j].append((i, cost[i]))
+    for i in range(n):
+        back[i].append((n, lat[i]))
     groups = {}
     for i, nd in enumerate(nodes):
         if nd["group"]:
             groups.setdefault(nd["group"], []).append(i)
     names = sorted(groups)
-    seed = [12345]
+    seed = [SEED]
 
     def rnd():
         seed[0] = (seed[0] * 1103515245 + 12345) % 2147483648
         return seed[0] / 2147483648.0
 
-    def attempt(queue, rank, look):
-        seq = lay_out(nodes, after, queue, rank, look, prices[0])
-        return (sum(replay(nodes, queue, seq, p) for p in prices), seq, queue, rank, look)
+    last = [i for i in range(n) if len(back[i]) == 1]
 
-    best = min([attempt([nd["q"] for nd in nodes], rank, look) for look in (0.0, 0.2, 0.4)], key=lambda b: b[0])
-    for _ in range(TRIES):
-        queue, rank, look = list(best[2]), list(best[3]), best[4]
-        kind = rnd()
-        if kind < 0.4:
-            for _k in range(1 + int(rnd() * 2)):
+    def attempt(queue, key, limit=1e9):
+        key = list(key)
+        for i in range(n):
+            for j, _ in fore[i]:
+                if key[j] >= key[i]:
+                    key[i] = key[j] + 1e-6
+        start = lay_out(sorted(range(n), key=lambda i: key[i]), fore, queue, cost)
+        first = max([start[i] + cost[i] + lat[i] for i in last])
+        if first > limit:
+            return (1e9,)
+        seq = sorted(range(n), key=lambda i: start[i])
+        return (first + sum(replay(lean, queue, seq, p) for p in prices[1:]), seq, queue, start, first)
+
+    def latest(queue, start):
+        order = [n] + sorted(range(n), key=lambda i: (-start[i] - cost[i], -i))
+        late = lay_out(order, back + [[]], queue + [None], cost + [0.0])
+        return [-late[i] - cost[i] for i in range(n)]
+
+    path = [0.0] * n
+    for i in range(n - 1, -1, -1):
+        path[i] = cost[i] + max([lat[i]] + [path[j] + gap - cost[j] for j, gap in back[i][:-1]])
+
+    def improve(best, tries):
+        now = best
+        for k in range(tries):
+            queue, key = list(now[2]), list(now[3])
+            kind = rnd()
+            if kind < 0.35:
                 for i in groups[names[int(rnd() * len(names))]]:
                     queue[i] = "s" if queue[i] == "v" else "v"
-        elif kind < 0.95:
-            a = int(rnd() * len(nodes))
-            d = (rnd() - 0.5) * 3.0
-            for i in range(a, min(len(nodes), a + 1 + int(rnd() * 14))):
-                rank[i] += d
-        else:
-            look = rnd() * 0.5
-        new = attempt(queue, rank, look)
-        if new[0] <= best[0]:
-            best = new
+            if kind > 0.9:
+                key = latest(queue, key)
+            elif kind > 0.25:
+                a, d = int(rnd() * n), (rnd() - 0.5) * 2.0
+                for i in range(a, min(n, a + 1 + int(rnd() * rnd() * 14))):
+                    key[i] += d
+            slack = SLACK * (1.0 - k / tries) * rnd()
+            new = attempt(queue, key, now[4] + 0.2 + slack / 2)
+            if new[0] <= now[0] + slack:
+                now = new
+                if new[0] < best[0]:
+                    best = new
+        return best
+
+    field = [attempt([nd["q"] for nd in nodes], [-r for r in path])] * 8
+    while len(field) > 1:
+        field = sorted([improve(b, TRIES // 3 // len(field)) for b in field], key=lambda b: b[0])[:len(field) // 2]
+    best = field[0]
     return best[1], best[2], best[0]
 
 
@@ -285,11 +320,13 @@ def rank_program(g, core, T, topo):
 
     sent = [0]
 
-    def send(reads, out, src, sem, dst, mark=()):
+    def send(reads, out, src, sem, dst, mark=(), local="sent", engines=None):
         rid, pid = topo.addr(dst, core)
-        node("g", reads, [], lambda _q: g.remote_dma(out, src, sem, T.sem.sent, pid, rid, topo.mask(core, dst)), fixed(0.3),
+        engines = engines or topo.engines(core, prev)
+        node("g", reads, [], lambda _q: g.remote_dma(out, src, sem, T.sem[local], pid, rid, mask_of(engines)), fixed(0.3),
              behind=["g"] + list(mark))
-        sent[0] += len(topo.engines(core, dst))
+        if local == "sent":
+            sent[0] += len(engines)
 
     V, S, P = g.vector, g.scalar, g.tensor
     prev, nxt = T.cores[(rank - 1) % n], T.cores[(rank + 1) % n]
@@ -299,8 +336,8 @@ def rank_program(g, core, T, topo):
     qv, sv = [T.qa, T.qb, T.qc], [T.sa, T.sb, T.sc]
     wc, wsc = [T.wa, T.wb], [T.sx, T.sy]
     ch, nw, og = [T.ca, T.cb], [T.na, T.nb], [[T.ga, T.gb], [T.gd, T.ge]]
+    lq, ls_ = [T.la, T.lb], [T.ma, T.mb]
     e1 = len(topo.engines(nxt, core))
-    arrives("w0", 2 * e1 + sum(len(topo.engines(h, core)) for h in helpers_of(T, topo, (rank + 1) % n)))
     arrives("w1", 4 * sum(len(topo.engines(h, core)) for h in helpers_of(T, topo, (rank + 2) % n)))
 
     def ts(reads, writes, c, out, in0, s1, s2, op0, op1=None):
@@ -350,48 +387,57 @@ def rank_program(g, core, T, topo):
 
     def send_halo(t):
         name = "halo%d" % t
-        send(["qvA%d" % t], bytes_of(qv[t][:, 256:336]), bytes_of(qv[t][:, 0:NH]), T.sem[name], prev)
-        send(["qvA%d" % t], sv[t][:, 256:336], sv[t][:, 0:NH], T.sem[name], prev, ["left" + name])
-        arrives(name, 2 * e1, ["left" + name])
+        rid, pid = topo.addr(prev, core)
+        off = topo.engines(core, prev)
+        half = len(off) // 2
+        pairs = ((bytes_of(qv[t][:, 0:NH]), bytes_of(lq[t][:, 128:128 + NH])), (sv[t][:, 0:QB], ls_[t][:, 128:128 + QB]))
+        trs = [RemoteDMATransfer(dst_ids=[DstId(rid=rid, pnc=pid)], dma_engine_mask=mask_of(off[half * i:half * i + half]),
+                                 remote_sem=T.sem[name], src=src, dst=dst) for i, (src, dst) in enumerate(pairs)]
+        node("g", ["qvA%d" % t, "rest%d" % t], [], lambda _q: g.remote_dma_fused(trs, local_sem=T.sem.sent), fixed(0.4),
+             behind=["g", "a" + name])
+        sent[0] += 2 * half
+        arrives(name, e1, ["a" + name])
 
-    def to_helpers(reads, srcs, dst, sem):
+    def to_helpers(reads, srcs, dst, sem, engines=spare):
         half = len(spare) // 2
         trs = []
         for i in range(2):
             rid, pid = topo.addr(hs[i], core)
-            trs.append(RemoteDMATransfer(dst_ids=[DstId(rid=rid, pnc=pid)], dma_engine_mask=mask_of(spare[half * i:half * i + half]),
+            trs.append(RemoteDMATransfer(dst_ids=[DstId(rid=rid, pnc=pid)], dma_engine_mask=mask_of(engines[half * i:half * i + half]),
                                          remote_sem=sem, src=srcs[i], dst=dst))
         node("g", reads, [], lambda _q: g.remote_dma_fused(trs, local_sem=T.sem.sent), fixed(0.3), behind=["g"])
         sent[0] += 2 * half
 
     def iota(key, out, pattern, base, c):
-        op("g", [], [key], lambda: g.iota(out, pattern, base, 0, allow_small_or_imprecise_dtypes=True),
-           fixed(0.13 + 0.002 * c), behind=["g"])
+        op("g", [], key if isinstance(key, list) else [key],
+           lambda: g.iota(out, pattern, base, 0, allow_small_or_imprecise_dtypes=True), fixed(0.13 + 0.0019 * c), behind=["g"])
 
     def span(name, a, b):
         return ["%s%d" % (name, i) for i in range(a, b)]
 
     WD = 512 - 2 * HC
-    dma("y", "lxa", [], ["xa"], T.xa[:, 0:4 * NA], T.x[:, 0:4 * NA], "x")
+    dma("y", "lxa", [], ["xa"], T.xa[:, 0:4 * NH], T.x[:, 0:4 * NH], "x")
     dma("s", "lws0", [], ["ws0"], T.ls[:, 0:WS0], T.ws[:, 0:WS0], "x")
-    dma("s", "lst", [], ["sti"], T.si[:], T.st[:], 2.9)
-    dma("y", "lwh", [], ["wlh"], bytes_of(T.wl[:, WD:512]), T.wc[:, 4 * WD:2048], 3.7)
-    dma("y", "lu", [], ["ut"], T.ut[:], T.u[:], 4.6)
-    dma("y", "lxb", [], ["xb"], T.xb[:, 0:4 * NB], T.x[:, 4 * NA:768], 5.4)
-    dma("y", "lws", ["ut"], ["wls"], T.ls[:, WS0:512], T.ws[:, WS0:512], 2.5)
-    dma("y", "lwd", [], ["wld"], bytes_of(T.wl[:, 0:WD]), T.wc[:, 0:4 * WD], 3.5)
+    dma("s", "lst", [], ["sti"], T.si[:], T.st[:], "st")
+    dma("y", "lu", [], ["ut"], T.ut[:], T.u[:], "u")
+    dma("y", "lxb", [], ["xb", "xbpad"], T.xb[:], T.x[:, 256:768], "xb")
+    dma("y", "lwh", [], ["wlh"], bytes_of(T.wl[:, WD:512]), T.wc[:, 4 * WD:2048], 4.4)
 
     EQ = AluOpType.is_equal
     s0 = WS0 // 2
     op("g", [], ["pi"], lambda: g.iota(T.pi[:], [[0, 1]], 0, 1), fixed(0.13), behind=["g"])
     iota("iw", T.iw[:], [[1, 256]], 0, 256)
-    to_helpers(["ws0"], [T.ls[:, 0:s0], T.ls[:, s0:WS0]], T.hs[:, 0:s0], T.sem.hp0)
-    fill("xapad", 88, T.xa[:, 4 * NA:512], 0.0)
+    to_helpers(["ws0"], [T.ls[:, 0:s0], T.ls[:, s0:WS0]], T.hs[:, 0:s0], T.sem.hp0, topo.engines(core, prev))
+    fill("zApad", 384, T.za[:], 0.0)
+    for t in range(2):
+        quant(["zApad"], ["rest%d" % t], qv[t], sv[t], 128, T.za[:], QB - 128)
+    fill("xapad", 96, T.xa[:, 4 * NH:512], 0.0)
     quant(["xa", "xapad"], ["qvA0"], T.qa, T.sa, 0, T.xa[:, 0:512])
     send_halo(0)
-    iota("i8", T.ie[:, 0:32 * MOST], [[0, 4 * MOST], [1, 8]], 0, 32 * MOST)
     iota("i36", T.ib[:, 0:4 * MOST], [[32, MOST], [0, 4]], 7, 4 * MOST)
-    fill("xbpad", 40, T.xb[:, 4 * NB:512], 0.0)
+    iota("i8", T.ie[:, 0:32 * MOST], [[0, 4 * MOST], [1, 8]], 0, 32 * MOST)
+    dma("y", "lwd", ["i36"], ["wld"], bytes_of(T.wl[:, 0:WD]), T.wc[:, 0:4 * WD], 2.6)
+    dma("y", "lws", [], ["wls"], T.ls[:, WS0:512], T.ws[:, WS0:512], 3.2)
     fill("et", 258, T.et[:], 0.0)
     SHR, AND = AluOpType.logical_shift_right, AluOpType.bitwise_and
     for i, (sh, low) in enumerate(((0, 15), (2, 3), (0, 3), (3, 1), (0, 7), (0, 127), (0, 1))):
@@ -412,19 +458,24 @@ def rank_program(g, core, T, topo):
         quant(["et"], ["eq%d" % b], T.eq, T.es, 128 * b, T.et[:, 3 - b:515 - b])
 
     quant(["ut"], ["uq"], T.uq, T.us, 0, T.ut[:])
-    quant(["xb", "xbpad"], ["qvB0"], T.qa, T.sa, 128, T.xb[:])
+    quant(["xb"], ["qvB0"], T.qa, T.sa, QB, T.xb[:])
+    for t in range(2):
+        quant(["xb"], ["ahead%d" % t], lq[t], ls_[t], 0, T.xb[:])
     cp(["uq", "ou"], ["urq"], gat(128), T.ur[:].bitcast(dt.uint32), T.uq[:].bitcast(dt.uint32).indirect(T.ou[:]))
     act(["uq", "ou"], ["urs"], gat(128), T.ux[:], T.us[:].indirect(T.ou[:]), COPY)
     UR = ["urq", "urs"]
-    dma("y", "lv", ["halo0"], ["vt"], T.vt[:], T.v[:], 3.0)
     (a0, c0), (b0, d0) = helper_columns(0)
     (a1, _), (b1, _) = helper_columns(1)
     to_helpers(["wlh"], [bytes_of(T.wl[:, a0:a0 + c0]), bytes_of(T.wl[:, a1:a1 + c0])], bytes_of(T.wh[:, 0:c0]), T.sem.hp1)
-    send(["ws0", "wls"], T.sx[:], T.ls[:], T.sem.w0, prev)
     send(["wld"], bytes_of(T.wa[:, 0:WD]), bytes_of(T.wl[:, 0:WD]), T.sem.w0, prev)
-    to_helpers(["wld"], [bytes_of(T.wl[:, b0:b0 + d0]), bytes_of(T.wl[:, b1:b1 + d0])], bytes_of(T.wh[:, c0:c0 + d0]), T.sem.hp2)
-    to_helpers(["wls"], [T.ls[:, WS0:256 + s0], T.ls[:, 256 + s0:512]], T.hs[:, s0:256], T.sem.hp3)
-    quant(["vt"], ["vq"], T.vq, T.vs, 0, T.vt[:])
+    send(["ws0", "wls"], T.sx[:], T.ls[:], T.sem.w0, prev, ["aw0"])
+    arrives("w0", 2 * e1 + sum(len(topo.engines(c, core)) for c in helpers_of(T, topo, (rank + 1) % n)), ["aw0"])
+    for h in range(NP):
+        deep = 2 * max(max(r["find"][h]) for r in ROUNDS if len(r["find"]) > h)
+        iota(span("tb%d" % h, 0, deep), T.tb[:, 2 * DEEP * TW * h:2 * DEEP * TW * h + deep * TW], [[0, deep * TW]], 0, deep * TW)
+        if h == 0:
+            to_helpers(["wld"], [bytes_of(T.wl[:, b0:b0 + d0]), bytes_of(T.wl[:, b1:b1 + d0])], bytes_of(T.wh[:, c0:c0 + d0]), T.sem.hp2)
+            to_helpers(["wls"], [T.ls[:, WS0:256 + s0], T.ls[:, 256 + s0:512]], T.hs[:, s0:256], T.sem.hp3)
 
     def flat(key, out, c, value, reads=()):
         act(["iw"] + list(reads), [key], cyc(c), out, T.iw[:, 0:c], IDENT, scale=0.0, bias=value)
@@ -437,34 +488,28 @@ def rank_program(g, core, T, topo):
     flat("d1e", T.dd[:, 0:344:2], 172, 0.0)
     flat("d1o", T.dd[:, 1:344:2], 172, c_lo, ["c_lo"])
     flat("rr", T.rr[:, 0:TW], TW, 0.0)
-    flat("rr", T.rr[:, 0:TW:16], MOST, BIG)
+    flat("rr", T.rr[:, 0:TW:16], LONG, BIG)
     act(["i8"], ["rs8"], cyc(32 * MOST), T.rs[:, 0:32 * MOST], T.ie[:, 0:32 * MOST], SIGN)
     flat("p1", T.pa[:, 0:TW], TW, -1.0)
-    act(["iw"], ["p1"], cyc(MOST), T.pa[:, 15:TW:16], T.iw[:, 31:TW + 16:16], COPY)
-    for h, tb in enumerate((T.tb, T.tc)[:max(len(r) for r in ROUNDS)]):
-        deep = max(max(r[h]["chase"]) for r in ROUNDS if len(r) > h)
-        for x in range(2 * deep):
-            flat("tb%d%d" % (h, x), tb[:, TW * x:TW * x + TW], TW, 0.0)
-    for t in range(2):
-        for h, part in enumerate(ROUNDS[t]):
-            a = 64 * steps_of(part)[0] + 4 * h
-            if t == 0 or steps_of(part)[0] != steps_of(ROUNDS[0][h])[0]:
-                flat("mxpad%d" % a, T.mx[:, a:a + 4], 4, 0.0)
+    act(["iw"], ["p1"], cyc(LONG), T.pa[:, 15:TW:16], T.iw[:, 31:TW + 16:16], COPY)
+    flat("mx-1", T.mx[:, 0:4], 4, 0.0)
     for h, tiles_h in enumerate(((T.za, T.ha), (T.zb, T.hb))):
-        c = min(12 * (r[h]["segs"][1] - r[h]["segs"][0]) for r in ROUNDS if len(r) > h)
+        c = min(12 * (r["pieces"][h][0][1] - r["pieces"][h][0][0]) for r in ROUNDS if len(r["pieces"]) > h)
         for tile, key in zip(tiles_h, "zh"):
-            fill("%s%spad" % (key, "AB"[h]), 256 - 2 * c, tile[:, 4 * c:512], 0.0)
-    for x in sorted(set(x for p in PARTS for x in p["chase"])):
+            if key + "AB"[h] != "zA":
+                fill("%s%spad" % (key, "AB"[h]), 256 - 2 * c, tile[:, 4 * c:512], 0.0)
+    for x in sorted(set(x for p in PARTS for x in p)):
         ts(["c_x1"], ["c_t%d" % x], 1, c_bias[x], c_x1, float(2 * x - 2), 1.0, MIN, ADD)
         ts(["c_t%d" % x], ["c_t%d" % x], 1, c_bias[x], c_bias[x], float(TW), None, MUL)
-    same = [p["chase"] for p in ROUNDS[0]] == [p["chase"] for p in ROUNDS[1]]
+    same = ROUNDS[0]["find"] == ROUNDS[1]["find"]
     if same:
         nw[1] = nw[0]
     for t in range(1 if same else 2):
         flat("nw%d" % t, nw[t][:], 256, 0.0)
-        for part in ROUNDS[t]:
-            s = a = steps_of(part)[0]
-            for x in part["chase"]:
+        s = 0
+        for part in ROUNDS[t]["find"]:
+            a = s
+            for x in part:
                 if s > 0:
                     act(["iw", "c_t%d" % x], ["nw%d" % t], cyc(16), nw[t][:, 16 * s:16 * s + 16],
                         T.iw[:, 16 * (s - a):16 * (s - a) + 16], IDENT, bias=c_bias[x])
@@ -485,85 +530,104 @@ def rank_program(g, core, T, topo):
     ts(["i8", "cf"], ["m2"], 32 * MOST, T.mk[:, 0:32 * MOST], T.ie[:, 0:32 * MOST], c_m8, None, EQ)
     ts(["i36", "c_8m4"], ["ob"], 4 * MOST, T.ob[:, 0:4 * MOST], T.ib[:, 0:4 * MOST], c_8m4, None, ADD)
     ts(["bf", "cf"], ["ow"], 32, T.ow[:], T.bf[:], c_r, None, ADD)
+    for e in range(4):
+        ts(["ow"], ["of%d" % e], 32, T.of[:, 2 * e:256:8], T.ow[:], 2.0, 6.0 * e, MUL, ADD)
     for t in range(2):
         act(["iw", "ow", "c_rp"], ["pw%d" % t], gat(256), T.pw[:, 256 * t:256 * t + 256],
             T.iw[:].indirect(T.ow[:, 16 * t:16 * t + 16]), IDENT, scale=4.0, bias=c_rp)
         first = T.pw[:, 256 * t:256 * t + 1]
-        x = ROUNDS[t][0]["chase"][0]
+        x = ROUNDS[t]["find"][0][0]
         cp(["c_t%d" % x], ["ch%d" % t], cyc(1), ch[t][:, 0:1], c_bias[x])
         cp(["pw%d" % t], ["seg%d_0" % t], cyc(1), ch[t][:, 1:2], first)
         ts(["iw", "pw%d" % t], ["oz%d" % t], 4, og[t][0][:, 0:4], T.iw[:, 0:64:16], first, -16.0 - PAD, ADD, ADD)
 
-    piece = {"A": (0, NA, 0, 0), "B": (NA, NB, 128, 0), "H": (NA + NB, NH, 208, 48)}
+    piece = [{"A": (0, NH, 0, 0), "B": (NH, 192 - NH, QB, NH - 64), "H": (NA + NB, NH, NH, 48)},
+             {"A": (0, NA, 0, 0), "B": (NA, NB, QB, 0), "H": (NA + NB, NH, NH, 48)}]
 
     def window_keys(t, k):
-        return ["qvB%d" % t, "halo%d" % t] if k == "H" else ["qv%s%d" % (k, t)]
+        return ["ahead%d" % t, "halo%d" % t] if k == "H" else ["qv%s%d" % (k, t)]
 
-    def plain(k, bank, group):
-        j0, c, _, r0 = piece[k]
+    def side(t, k):
+        return (lq[t], ls_[t]) if k == "H" else (qv[t], sv[t])
+
+    def plain(t, k, bank, group):
+        j0, c, _, r0 = piece[t][k]
         c = min(c, 262 - j0)
         move("s", group, ["ps%d" % bank], ["n" + k], cyc(c), T.ia[:, 2 * j0:2 * (j0 + c):2], ps[bank][:, r0:r0 + c])
 
-    def masked(k, bank, q, group):
-        j0, c, _, r0 = piece[k]
+    def masked(t, k, bank, q, group):
+        j0, c, _, r0 = piece[t][k]
         a, b = max(j0, 8), min(j0 + c, 270)
         move(q, group, ["cf", "ps%d" % bank], ["m" + k], cyc(b - a), T.ia[:, 2 * (a - 8) + 1:2 * (b - 8):2],
              ps[bank][:, r0 + a - j0:r0 + b - j0], scale=c_hi)
 
     def scores(t, k, banks):
         for bank in sorted(set(banks)):
-            mm(UR + window_keys(t, k), bank, T.ur, T.ux, 0, qv[t], sv[t], piece[k][2], 128)
-        plain(k, banks[0], "e%d%s%d" % (t, k, banks[0]))
-        masked(k, banks[1], "s" if banks[0] == banks[1] else "v", "e%d%s%d" % (t, k, banks[1]))
+            mm(UR + window_keys(t, k), bank, T.ur, T.ux, 0, side(t, k)[0], side(t, k)[1], piece[t][k][2], 128)
+        plain(t, k, banks[0], "e%d%s%d" % (t, k, banks[0]))
+        masked(t, k, banks[1], "s" if banks[0] == banks[1] else "v", "e%d%s%d" % (t, k, banks[1]))
 
     def shift(a, b, reads, key):
         scan(reads + ["d1e", "d1o"], [key], 2 * (b - a), T.ta[:, 2 * a:2 * b], T.dd[:, 0:2 * (b - a)], T.ia[:, 2 * a:2 * b], MUL, ADD)
 
     def decode(t, k, banks):
-        j0, c, ra, r0 = piece[k]
+        j0, c, ra, r0 = piece[t][k]
         for b in range(4):
-            mm(["eq%d" % b] + window_keys(t, k), banks[b], T.eq, T.es, 128 * b, qv[t], sv[t], ra, 128)
+            mm(["eq%d" % b] + window_keys(t, k), banks[b], T.eq, T.es, 128 * b, side(t, k)[0], side(t, k)[1], ra, 128)
             move("s", "dv%d%s%d" % (t, k, b), ["ps%d" % banks[b]], ["dv%s%d" % (k, b)], cyc(c),
                  T.dv[:, PAD + 4 * j0 + b:PAD + 4 * (j0 + c):4], ps[banks[b]][:, r0:r0 + c], scale=0.5)
 
     DV = ["dvpad"] + ["dv%s%d" % (k, b) for k in "ABH" for b in range(4)]
     I1 = ["nA", "nB", "nH", "mA", "mB", "mH"]
-    T1 = ["t1a", "t1b", "t1c"]
+    T1 = ["t1a", "t1b", "t1c", "rest1"]
 
-    def search(t, h):
-        part = ROUNDS[t][h]
-        a, b = steps_of(part)
-        c0, k, name = 64 * t + 4, b - a, "%d%d" % (t, h)
-        m0 = 64 * a + 4 * h
-        e0 = a - a % 2
-        move("s", "ex" + name, ["win", "oe"], span("ex", e0, b), gat(16 * (b - e0)), T.ex[:, 64 * e0 + 1:64 * b:4],
-             T.wn[:].indirect(T.oe[:, 16 * t + e0:16 * t + b]))
-        tt(T1 + ["o20", "o21", "m2"], span("g2", a, b), gat(32 * k), T.gg[:, 32 * a:32 * b],
-           T.ta[:, 24:524].indirect(T.ot[:, 32 * t + 2 * a:32 * t + 2 * b]), T.mk[:, 0:32 * k], MUL)
-        scan(span("g2", a, b) + ["rs8"], span("tt", a, b), 32 * k, T.tt[:, 32 * a:32 * b], T.rs[:, 0:32 * k], T.gg[:, 32 * a:32 * b], MUL, ADD)
-        i, pads = a, [key for key in wrote if key.startswith("mxpad")]
-        for d in part["dist"]:
-            j = i + d
+    def distances(t):
+        c0, held = 64 * t + 4, {}
+        move("s", "ex%d" % t, ["win", "oe"], ["exb"], gat(240), T.ex[:, 1:960:4], T.wn[:].indirect(T.oe[:, 16 * t:16 * t + 15]))
+        for i, j in runs(ROUNDS[t]["temp"]):
+            d = j - i
+            tt(T1 + ["o20", "o21", "m2"], span("g2", i, j), gat(32 * d), T.gg[:, 32 * i:32 * j],
+               T.ta[:, 24:524].indirect(T.ot[:, 32 * t + 2 * i:32 * t + 2 * j]), T.mk[:, 0:32 * d], MUL)
+            scan(span("g2", i, j) + ["rs8"], span("tt", i, j), 32 * d, T.tt[:, 32 * i:32 * j], T.rs[:, 0:32 * d], T.gg[:, 32 * i:32 * j], MUL, ADD)
+            held.update({s: (i, j) for s in range(i, j)})
+        for i, j in runs(ROUNDS[t]["dist"]):
+            d = j - i
+            u, v = held[i]
+            if i >= ROUNDS[t]["alone"]:
+                made = []
+                for s in range(i, j):
+                    for e in range(4):
+                        c = 128 * t + 8 * s + 8 + 2 * e
+                        made.append("ab%d_%d" % (s, e))
+                        act(I1 + ["of%d" % e, "tt%d" % s], made[-1:], gat(16), T.ab[:, 64 * s + e:64 * s + 64:4],
+                            T.ia[:].indirect(T.of[:, c:c + 1]), ABS, scale=-1.0, bias=T.tt[:, 32 * s + 8 * e + 7:32 * s + 8 * e + 8])
+                scan(made + ["exa", "exb", "exc", "exd"], span("mx", i, j), 64 * d,
+                     T.mx[:, 4 + 64 * i:4 + 64 * j], T.ex[:, 64 * i:64 * j], T.ab[:, 64 * i:64 * j], ADD, MAX)
+                continue
             move("s", "cc%d%d" % (t, i), I1 + span("oc", 0, 4), span("cc", i, j), gat(64 * d), T.cc[:, 64 * i:64 * j],
                  T.ia[:].indirect(T.od[:, c0 + 4 * i:c0 + 4 * j]))
-            tt(span("tt", a, b) + ["ob"] + span("cc", i, j), span("df", i, j), gat(64 * d), T.df[:, 64 * i:64 * j],
-               T.tt[:, 32 * a:32 * b].indirect(T.ob[:, 4 * (i - a):4 * (j - a)]), T.cc[:, 64 * i:64 * j], SUB)
+            tt(span("tt", u, v) + ["ob"] + span("cc", i, j), span("df", i, j), gat(64 * d), T.df[:, 64 * i:64 * j],
+               T.tt[:, 32 * u:32 * v].indirect(T.ob[:, 4 * (i - u):4 * (j - u)]), T.cc[:, 64 * i:64 * j], SUB)
             act(span("df", i, j), span("ab", i, j), cyc(64 * d), T.ab[:, 64 * i:64 * j], T.df[:, 64 * i:64 * j], ABS)
-            scan(span("ab", i, j) + span("ex", i, j) + ["exa", "exc", "exd"] + pads, span("mx", i, j), 64 * d,
-                 T.mx[:, m0 + 4 + 64 * (i - a):m0 + 4 + 64 * (j - a)], T.ex[:, 64 * i:64 * j], T.ab[:, 64 * i:64 * j], ADD, MAX)
-            i = j
-        MX = span("mx", a, b)
-        scan(["rr"] + MX, span("mm", a, b), 16 * k, T.mm[:, 16 * a:16 * b], T.mx[:, m0 + 3:m0 + 64 * k:4], T.rr[:, 0:16 * k], MIN, MAX)
-        tt(MX + span("mm", a, b), span("nn", a, b), cyc(32 * k), T.nn[:, 16 * a:16 * b], T.mx[:, m0 + 7:m0 + 4 + 64 * k:4],
+            scan(span("ab", i, j) + ["exa", "exb", "exc", "exd"], span("mx", i, j), 64 * d,
+                 T.mx[:, 4 + 64 * i:4 + 64 * j], T.ex[:, 64 * i:64 * j], T.ab[:, 64 * i:64 * j], ADD, MAX)
+
+    def search(t, h):
+        part = ROUNDS[t]["find"][h]
+        a, b = runs([sum(p) for p in ROUNDS[t]["find"]])[h]
+        k, name = b - a, "%d%d" % (t, h)
+        scan(["rr"] + span("mx", a - 1, b), span("mm", a, b), 16 * k, T.mm[:, 16 * a:16 * b], T.mx[:, 64 * a + 3:64 * b:4],
+             T.rr[:, 0:16 * k], MIN, MAX)
+        tt(span("mx", a, b) + span("mm", a, b), span("nn", a, b), cyc(32 * k), T.nn[:, 16 * a:16 * b], T.mx[:, 64 * a + 7:64 * b + 4:4],
            T.mm[:, 16 * a:16 * b], AluOpType.is_ge)
         scan(span("nn", a, b) + ["p1"], span("pt", a, b), 8 * k, T.pt[:, 16 * a:16 * b], T.nn[:, 16 * a:16 * b], T.pa[:, 0:16 * k], MUL, ADD)
-        ob = 16 * h
+        ob, t0 = 2 * a, 2 * DEEP * TW * h
         cp(span("pt", a, b), ["op%d" % h], cyc(k), T.op[:, ob:ob + k], T.pt[:, 16 * a + 15:16 * b:16])
-        tb, need = (T.tb, T.tc)[h], tables_of(part)
+        tb, need = T.tb, tables_of(a, part)
         for x, kind in sorted(need):
             i, j = need[(x, kind)]
             i -= (i - a) % 2
-            at = TW * (2 * x - 2 + kind)
+            at = t0 + TW * (2 * x - 2 + kind)
             if x == 1:
                 src, key = ((T.pw[:, 256 * t + 16 * a:256 * t + 16 * b + 16], "pw%d" % t),
                             (nw[t][:, 16 * a:16 * b + 16], "nw%d" % (0 if same else t)))[kind]
@@ -572,9 +636,9 @@ def rank_program(g, core, T, topo):
             move("sv"[kind], "tf%s%d%d" % (name, x, kind), [key, "op%d" % h], ["tb%d%d" % (h, 2 * x - 2 + kind)], gat(16 * (j - i)),
                  tb[:, at + 16 * (i - a):at + 16 * (j - a)], src.indirect(T.op[:, ob + i - a:ob + j - a]))
         s = a
-        for x in part["chase"]:
+        for x in part:
             cp(span("tb%d" % h, 0, 2 * x) + ["ch%d" % t], ["ch%d" % t] + span("seg%d_" % t, s + 1, s + x + 1), gat(16),
-               ch[t][:, 2 * s + 2:2 * s + 18], tb[:, 0:2 * x * TW].indirect(ch[t][:, 2 * s:2 * s + 1]))
+               ch[t][:, 2 * s + 2:2 * s + 18], tb[:, t0:t0 + 2 * x * TW].indirect(ch[t][:, 2 * s:2 * s + 1]))
             s += x
         if b == 15:
             ts(span("seg%d_" % t, 0, 16), ["pp%d" % t], 16, T.pp[:, 16 * t:16 * t + 16], ch[t][:, 1:32:2], -float(PAD), 0.25, ADD, MUL)
@@ -584,12 +648,12 @@ def rank_program(g, core, T, topo):
         return [(u, v) for u, v in zip(marks, marks[1:]) if v > u]
 
     def overlap(t, h):
-        s0, s1 = ROUNDS[t][h]["segs"]
+        (s0, s1), lap, _ = ROUNDS[t]["pieces"][h]
         o, z, k = og[t][h], (T.za, T.zb)[h], "AB"[h]
         lead = 4 if h == 0 else 0
         j0 = 3 * s0 + 4 - lead
         keys = []
-        for sa, sb, calls in ROUNDS[t][h]["lap"]:
+        for sa, sb, calls in lap:
             u, v = lead + 3 * (sa - s0), lead + 3 * (sb - s0)
             made = span("og%d%d%d_" % (t, h, sa), 0, 3)
             for m in range(3):
@@ -612,14 +676,14 @@ def rank_program(g, core, T, topo):
                  tile[:, b:4 * c:4], ps[bank0 + b][:, 0:c], scale=scale)
 
     def columns(t, h):
-        s0, s1 = ROUNDS[t][h]["segs"]
+        s0, s1 = ROUNDS[t]["pieces"][h][0]
         return 12 * s0, 12 * (s1 - s0), max(128, 12 * (s1 - s0))
 
     def layer(t, h, zs):
         z, hh, x = tiles[h]
         k, a = "AB"[h], 128 * h
-        _, c, w = columns(t, h)
-        r0, x0 = ROUNDS[t][h]["banks"]
+        j0, c, w = columns(t, h)
+        r0, x0 = ROUNDS[t]["pieces"][h][2]
         quant(zs + ["z%spad" % k], ["qz" + k], T.qz, T.sz, a, z[:, 0:4 * w], w)
         for b in range(4):
             mm(["qz" + k, "w%d" % t], r0 + b, wc[t], wsc[t], 128 * b, T.qz, T.sz, a, w)
@@ -636,21 +700,21 @@ def rank_program(g, core, T, topo):
         keys = span(name, 0, 4)
         if t == 0:
             for key in keys:
-                readers[key] = list(readers[name])
+                readers[key] = list(readers.get(name, []))
         unload(x, name, t, c, x0, None)
-        quant(keys + [name + "pad"], ["qv%s%d" % (k, t + 1)], qv[t + 1], sv[t + 1], a, x[:, 0:4 * w], w)
+        quant(keys + [name + "pad"], ["qv%s%d" % (k, t + 1)] + ["qc"] * t, qv[t + 1], sv[t + 1], j0 if t else QB * h, x[:, 0:4 * w], w)
 
-    def store(h, sem, queues):
+    def store(h, last):
         j0, c, w = columns(1, h)
-        k, a, bank = "AB"[h], 128 * h, ROUNDS[1][h]["banks"][0]
-        key = ["qv%s2" % k]
-        mm(key + ["vq"], bank, T.vq, T.vs, 0, T.qc, T.sc, a, w)
-        dma(queues[0], sem[0], key, [], T.oc[:, 4 * j0:4 * (j0 + c)], bytes_of(T.qc[:, a:a + c]), STORE)
-        for i in range(4):
-            j = i // 2
-            dma(queues[j], sem[j], key, [], T.osc[4 * i:4 * i + 4, j0:j0 + c], T.sc[32 * i:32 * i + 4, a:a + c], STORE)
+        k, bank = "AB"[h], ROUNDS[1]["pieces"][h][2][0]
+        key = ["qv%s2" % k, "qc"]
+        mm(key + ["vq"], bank, T.vq, T.vs, 0, T.qc, T.sc, j0, w)
+        dma("y", "sta", key[:1], [], T.oc[:, 4 * j0:4 * (j0 + c)], bytes_of(T.qc[:, j0:j0 + c]), STORE)
+        if last:
+            for i in range(4):
+                dma("y", "sta", key, [], T.osc[4 * i:4 * i + 4, :], T.sc[32 * i:32 * i + 4, 0:192], STORE)
         move("sv"[h], "y" + k, ["ps%d" % bank], ["y" + k], cyc(c), T.yb[:, j0:j0 + c], ps[bank][:, 0:c])
-        dma(queues[1], sem[1], ["y" + k], [], T.y[:, j0:j0 + c], T.yb[:, j0:j0 + c], STORE)
+        dma("s" if last else "y", "stb" if last else "sta", ["y" + k], [], T.y[:, j0:j0 + c], T.yb[:, j0:j0 + c], STORE)
 
     scores(0, "A", (0, 0))
     scores(0, "B", (1, 1))
@@ -660,10 +724,13 @@ def rank_program(g, core, T, topo):
     scores(0, "H", (2, 3))
     shift(184, 262, ["nB", "nH", "mH"], "t1b")
     decode(0, "H", (4, 5, 6, 7))
-    search(0, 0)
+    distances(0)
+    for h in range(len(ROUNDS[0]["find"])):
+        search(0, h)
     layer(0, 0, overlap(0, 0))
     send_halo(1)
-    search(0, 1)
+    dma("y", "lv", ["halo1"], ["vt"], T.vt[:], T.v[:], 2.5)
+    quant(["vt"], ["vq"], T.vq, T.vs, 0, T.vt[:])
     zs = overlap(0, 1)
     scores(1, "A", (0, 0))
     shift(12, 76, ["nA", "mA"], "t1a")
@@ -675,26 +742,29 @@ def rank_program(g, core, T, topo):
     shift(184, 262, ["nB", "nH", "mH"], "t1b")
     decode(1, "B", (6, 7, 4, 5))
     decode(1, "H", (2, 3, 0, 1))
-    last = len(ROUNDS[1]) - 1
-    for h in range(last + 1):
+    distances(1)
+    for h in range(len(ROUNDS[1]["find"])):
         search(1, h)
+    last = len(ROUNDS[1]["pieces"]) - 1
+    for h in range(last + 1):
         zs = overlap(1, h)
         if h == last:
             dma("y", "sta", ["pp0", "pp1"], [], T.ol[:], T.pp[0:128:16, :], STORE)
         layer(1, h, zs)
-        if h < last:
-            store(h, ("sta", "sta"), ("y", "y"))
-    store(last, ("stb", "stc"), ("y", "s"))
+        store(h, h == last)
 
     if "plan" not in PLANNED:
         PLANNED["plan"] = schedule(nodes)
     seq, queue, _ = PLANNED["plan"]
-    count, waited, token = {"sent": sent[0]}, {}, {}
+    count, token, place, behind = {"sent": sent[0]}, {}, {}, {}
+    known = {q: {} for q in Q}
 
     def need(q, s, c):
-        if waited.get((q, s), 0) < c:
+        if known[q].get(s, 0) < c:
             Q[q].wait_ge(T.sem[s], c)
-            waited[(q, s)] = c
+            known[q][s] = c
+            for k, v in behind.get((s, c), {}).items():
+                known[q][k] = max(known[q].get(k, 0), v)
 
     for i in seq:
         nd, q = nodes[i], queue[i]
@@ -703,7 +773,7 @@ def rank_program(g, core, T, topo):
             toks = {}
             for j in nd["hard"]:
                 toks[token[j][0]] = max(toks.get(token[j][0], 0), token[j][1])
-            for k in sorted(toks):
+            for k in sorted(toks, key=lambda k: -place[(k, toks[k])]):
                 need(q, k, toks[k])
             call = nd["call"](q)
             if s:
@@ -711,5 +781,8 @@ def rank_program(g, core, T, topo):
         if s:
             count[s] = count.get(s, 0) + nd["inc"]
             token[i] = (s, count[s])
+            place[token[i]] = len(place)
+            if nd["sem"] == "own":
+                behind[token[i]] = dict(known[q])
     for s in sorted(count):
         need("g", s, count[s])

from concourse.bass import DstId, RemoteDMATransfer
from concourse.mybir import dt, AluOpType, ActivationFunctionType

F32, BF, I32, U16, CODE, U8 = "float32", "bfloat16", "int32", "uint16", "float8_e4m3fn_x4", "uint8"
NA, NB, NH = 84, 108, 80
QB = 4 * NH
BIG = 5.0e29
EXCL = 1.0e29
PAD = 48
HC = 128
WS0 = 128
ROUNDS = ({"temp": (3, 3, 9), "dist": (3, 3, 3, 3, 3), "alone": 12, "find": ((1, 2, 3), (1, 2, 3), (1, 2)),
           "pieces": (((0, 7), ((0, 4, 1), (4, 7, 1)), (0, 0)), ((7, 16), ((7, 13, 1), (13, 16, 1)), (4, 4)))},
          {"temp": (3, 3, 9), "dist": (3, 3, 3, 3, 3), "alone": 12, "find": ((1, 2, 3), (1, 2, 3), (1, 2)),
           "pieces": (((0, 7), ((0, 4, 1), (4, 7, 1)), (0, 0)), ((7, 16), ((7, 13, 1), (13, 16, 1)), (4, 4)))})
PLANS = ({"cyc": 0.00095, "gat": 0.00125, "wake": 0.18, "x": 1.6, "u": 2.8, "xb": 3.4, "st": 2.0,
          "halo0": 3.9, "halo1": 3.5, "w0": 5.0, "w1": 24.0},
         {"cyc": 0.00085, "gat": 0.00100, "wake": 0.11, "x": 1.6, "u": 2.4, "xb": 2.9, "st": 1.8,
          "halo0": 3.0, "halo1": 2.6, "w0": 4.0, "w1": 20.0},
         {"cyc": 0.00115, "gat": 0.00155, "wake": 0.27, "x": 2.4, "u": 3.9, "xb": 4.7, "st": 2.9,
          "halo0": 5.5, "halo1": 5.0, "w0": 7.0, "w1": 28.0})
TRIES = 45000
SLACK = 0.3
SEED = 1
STORE = 2.4


def runs(sizes):
    return [(sum(sizes[:i]), sum(sizes[:i + 1])) for i in range(len(sizes))]


PARTS = [p for r in ROUNDS for p in r["find"]]
MOST = max(max(r["temp"]) for r in ROUNDS)
LONG = max(sum(p) for p in PARTS)
DEEP = max(max(p) for p in PARTS)
TW = 16 * LONG
NP = max(len(r["find"]) for r in ROUNDS)

SCRATCH = {}
for _dt, _list in ((BF, "xa768 xb512 za768 zb512 ha768 hb512 ut512 vt512 et516 ex960 dv1136 tn832 nn240 pt240 pa240"),
                   (CODE, "eq512 uq128 ur128 vq128 qa448 qb448 la208 lb208 qc256 qz256 qh256 wl512 wh256 wa512 wb512"),
                   (U8, "es512 us128 ux128 vs128 sa448 sb448 ma448 mb448 sc256 sz256 sh256 ls512 hs256 sx512 sy512"),
                   (I32, "si2 pi1 ci8"),
                   (U16, "su2 ou8 ob60 od128 ot64 oe32 ow32 of256 op32 ca50 cb50 ga52 gb52 gd52 ge52"),
                   (F32, "cf8 cx24 iw256 ie480 ib60 mk480 rs480 dd344 rr240 wn32 bf32 nd32 ne32 ia524 ta524 "
                         "gg480 tt480 cc960 df960 ab960 mx968 mm240 pw512 na256 nb256 pp32 yb192")):
    for _n in _list.split():
        SCRATCH[_n[:2]] = ("sbuf", [128, int(_n[2:])], _dt)
SCRATCH["tb"] = ("sbuf", [128, NP * 2 * DEEP * TW], F32)
for _b in range(8):
    SCRATCH["ps%d" % _b] = ("psum", [128, 512], F32)

SEMAPHORES = ["cv", "cs", "cp", "cg", "sent", "halo0", "halo1", "w0", "w1", "hp0", "hp1", "hp2", "hp3",
              "lxa", "lxb", "lst", "lu", "lv", "lwh", "lws0", "lws", "lwd", "sta", "stb"]

ADD, SUB, MUL, MAX, MIN = AluOpType.add, AluOpType.subtract, AluOpType.mult, AluOpType.max, AluOpType.min
COPY, IDENT, ABS = ActivationFunctionType.Copy, ActivationFunctionType.Identity, ActivationFunctionType.Abs
SIGN = ActivationFunctionType.Sign
PLANNED = {}


def mask_of(engines):
    m = 0
    for e in engines:
        m |= 1 << e
    return m


def helpers_of(T, topo, r):
    c, n = T.cores[r], len(T.cores)
    prev = T.cores[(r - 1) % n]
    return [h for h in topo.cores_of(c) if topo.die(h) != topo.die(c) and topo.may_write(h, prev) and T.rank_of(h) is None][:2]


def bytes_of(view):
    return view.bitcast(dt.uint8)


def helper_columns(i):
    rest = 256 - HC
    return (512 - 2 * HC + HC * i, HC), (rest * i, rest)


def helper_program(g, core, T, topo, r, i):
    n = len(T.cores)
    d1, d2 = T.cores[(r - 1) % n], T.cores[(r - 2) % n]
    total = [0]

    def send(out, src, sem, dst):
        rid, pid = topo.addr(dst, core)
        g.remote_dma(out, src, sem, T.sem.sent, pid, rid, topo.mask(core, dst))
        total[0] += len(topo.engines(core, dst))

    got = len(spare_engines(T, topo, r)) // 2
    (a, c), (b, d) = helper_columns(i)
    first, rest = WS0 // 2, 256 - WS0 // 2
    g.wait_ge(T.sem.hp0, got)
    send(T.sy[:, first * i:first * i + first], T.hs[:, 0:first], T.sem.w1, d2)
    g.wait_ge(T.sem.hp1, got)
    send(bytes_of(T.wa[:, a:a + c]), bytes_of(T.wh[:, 0:c]), T.sem.w0, d1)
    g.wait_ge(T.sem.hp2, got)
    g.wait_ge(T.sem.hp3, got)
    send(bytes_of(T.wb[:, a:a + c]), bytes_of(T.wh[:, 0:c]), T.sem.w1, d2)
    send(bytes_of(T.wb[:, b:b + d]), bytes_of(T.wh[:, c:c + d]), T.sem.w1, d2)
    send(T.sy[:, WS0 + rest * i:WS0 + rest * i + rest], T.hs[:, first:first + rest], T.sem.w1, d2)
    g.wait_ge(T.sem.sent, total[0])


def spare_engines(T, topo, r):
    c = T.cores[r]
    off = topo.engines(c, T.cores[(r - 1) % len(T.cores)])
    return [e for e in topo.engines(c, helpers_of(T, topo, r)[0]) if e not in off]


def tables_of(s, chase):
    need = {}
    for x in chase:
        for j in range(1, x + 1):
            need.setdefault((j, 0), set()).add(s)
        if s + x < 15:
            need.setdefault((x, 1), set()).add(s)
        s += x
    for x in range(max(chase), 1, -1):
        for kind in range(2):
            for i in need.get((x, kind), ()):
                need.setdefault((x - 1, kind), set()).add(i + 1)
    return {k: (min(v), max(v) + 1) for k, v in need.items()}


def cyc(c):
    return (0.0, max(64, c), 0)


def gat(c):
    return (0.06, 0, c)


def fixed(c):
    return (c, 0, 0)


def priced(nodes, plan):
    cost = [nd["cost"][0] + nd["cost"][1] * plan["cyc"] + nd["cost"][2] * plan["gat"] for nd in nodes]
    return cost, [plan.get(nd["lat"], nd["lat"]) for nd in nodes], plan["wake"]


def replay(nodes, queue, seq, price):
    cost, lat, wake = price
    issued, end, free = [0.0] * len(nodes), [0.0] * len(nodes), {q: 0.0 for q in set(queue)}
    for i in seq:
        q = queue[i]
        t = free[q]
        for j in nodes[i]["hard"]:
            if end[j] > t:
                t = end[j]
        for j in nodes[i]["soft"]:
            if issued[j] > t:
                t = issued[j]
        t += cost[i]
        issued[i] = t
        end[i] = t + lat[i] + wake
        if q:
            free[q] = t
    return max(end) - wake


def lay_out(order, before, queue, cost):
    start = [0.0] * len(order)
    busy = {q: ([], []) for q in set(queue)}
    for i in order:
        t = 0.0
        for j, gap in before[i]:
            e = start[j] + gap
            if e > t:
                t = e
        q, c = queue[i], cost[i]
        if q:
            a, b = busy[q]
            k = len(a)
            while k and b[k - 1] > t:
                k -= 1
            while k < len(a) and a[k] < t + c - 1e-9:
                if b[k] > t:
                    t = b[k]
                k += 1
            a.insert(k, t)
            b.insert(k, t + c)
        start[i] = t
    return start


def schedule(nodes):
    n = len(nodes)
    prices = [priced(nodes, p) for p in PLANS]
    cost, lat, wake = prices[0]
    fore, back = [[] for _ in nodes], [[] for _ in nodes]
    lean, above = [], []
    for nd in nodes:
        implied = 0
        for j in nd["hard"]:
            implied |= above[j]
        lean.append({"hard": [j for j in nd["hard"] if not implied >> j & 1], "soft": nd["soft"]})
        for j in nd["hard"]:
            implied |= 1 << j
        above.append(implied)
    for i, nd in enumerate(lean):
        for j in nd["hard"]:
            fore[i].append((j, cost[j] + lat[j] + wake))
            back[j].append((i, cost[i] + lat[j] + wake))
        for j in nd["soft"]:
            fore[i].append((j, cost[j]))
            back[j].append((i, cost[i]))
    for i in range(n):
        back[i].append((n, lat[i]))
    groups = {}
    for i, nd in enumerate(nodes):
        if nd["group"]:
            groups.setdefault(nd["group"], []).append(i)
    names = sorted(groups)
    seed = [SEED]

    def rnd():
        seed[0] = (seed[0] * 1103515245 + 12345) % 2147483648
        return seed[0] / 2147483648.0

    last = [i for i in range(n) if len(back[i]) == 1]

    def attempt(queue, key, limit=1e9):
        key = list(key)
        for i in range(n):
            for j, _ in fore[i]:
                if key[j] >= key[i]:
                    key[i] = key[j] + 1e-6
        start = lay_out(sorted(range(n), key=lambda i: key[i]), fore, queue, cost)
        first = max([start[i] + cost[i] + lat[i] for i in last])
        if first > limit:
            return (1e9,)
        seq = sorted(range(n), key=lambda i: start[i])
        return (first + sum(replay(lean, queue, seq, p) for p in prices[1:]), seq, queue, start, first)

    def latest(queue, start):
        order = [n] + sorted(range(n), key=lambda i: (-start[i] - cost[i], -i))
        late = lay_out(order, back + [[]], queue + [None], cost + [0.0])
        return [-late[i] - cost[i] for i in range(n)]

    path = [0.0] * n
    for i in range(n - 1, -1, -1):
        path[i] = cost[i] + max([lat[i]] + [path[j] + gap - cost[j] for j, gap in back[i][:-1]])

    def improve(best, tries):
        now = best
        for k in range(tries):
            queue, key = list(now[2]), list(now[3])
            kind = rnd()
            if kind < 0.35:
                for i in groups[names[int(rnd() * len(names))]]:
                    queue[i] = "s" if queue[i] == "v" else "v"
            if kind > 0.9:
                key = latest(queue, key)
            elif kind > 0.25:
                a, d = int(rnd() * n), (rnd() - 0.5) * 2.0
                for i in range(a, min(n, a + 1 + int(rnd() * rnd() * 14))):
                    key[i] += d
            slack = SLACK * (1.0 - k / tries) * rnd()
            new = attempt(queue, key, now[4] + 0.2 + slack / 2)
            if new[0] <= now[0] + slack:
                now = new
                if new[0] < best[0]:
                    best = new
        return best

    field = [attempt([nd["q"] for nd in nodes], [-r for r in path])] * 8
    while len(field) > 1:
        field = sorted([improve(b, TRIES // 3 // len(field)) for b in field], key=lambda b: b[0])[:len(field) // 2]
    best = field[0]
    return best[1], best[2], best[0]


def rank_program(g, core, T, topo):
    rank = T.rank_of(core)
    n = len(T.cores)
    if rank is None:
        for r in range(n):
            hs = helpers_of(T, topo, r)
            if core in hs:
                helper_program(g, core, T, topo, r, hs.index(core))
        return

    Q = {"v": g.vector, "s": g.scalar, "p": g.tensor, "g": g, "y": g.sync}
    own = {"v": "cv", "s": "cs", "p": "cp", "g": "cg"}
    nodes, wrote, readers = [], {}, {}

    def node(q, reads, writes, call, cost, lat=0.0, sem=None, inc=1, loose=(), behind=(), group=None):
        hard, soft = set(), set()
        for k in list(reads) + list(writes):
            if k in wrote:
                (soft if k in loose else hard).add(wrote[k])
            if k in writes:
                hard.update(readers.get(k, []))
        for k in behind:
            if k in wrote:
                soft.add(wrote[k])
        i = len(nodes)
        nodes.append({"q": q, "hard": sorted(hard), "soft": sorted(soft - hard), "call": call, "cost": cost, "lat": lat,
                      "sem": sem, "inc": inc, "group": group, "name": (list(writes) + list(reads))[0]})
        for k in reads:
            readers.setdefault(k, []).append(i)
        for k in list(writes) + list(behind):
            wrote[k] = i
            readers[k] = []

    def op(q, reads, writes, call, cost, loose=(), behind=()):
        node(q, reads, writes, lambda _q: call(), cost, sem="own", loose=loose, behind=behind)

    def dma(q, s, reads, writes, out, src, lat):
        node(q, reads, writes, lambda _q: Q[q].dma_start(out, src), fixed(0.06), lat, s, 16, behind=["dma" + q])

    def arrives(key, c, behind=()):
        node(None, [], [key], None, fixed(0.0), key, key, c, behind=behind)

    sent = [0]

    def send(reads, out, src, sem, dst, mark=(), local="sent", engines=None):
        rid, pid = topo.addr(dst, core)
        engines = engines or topo.engines(core, prev)
        node("g", reads, [], lambda _q: g.remote_dma(out, src, sem, T.sem[local], pid, rid, mask_of(engines)), fixed(0.3),
             behind=["g"] + list(mark))
        if local == "sent":
            sent[0] += len(engines)

    V, S, P = g.vector, g.scalar, g.tensor
    prev, nxt = T.cores[(rank - 1) % n], T.cores[(rank + 1) % n]
    hs = helpers_of(T, topo, rank)
    spare = spare_engines(T, topo, rank)
    ps = [T["ps%d" % b] for b in range(8)]
    qv, sv = [T.qa, T.qb, T.qc], [T.sa, T.sb, T.sc]
    wc, wsc = [T.wa, T.wb], [T.sx, T.sy]
    ch, nw, og = [T.ca, T.cb], [T.na, T.nb], [[T.ga, T.gb], [T.gd, T.ge]]
    lq, ls_ = [T.la, T.lb], [T.ma, T.mb]
    e1 = len(topo.engines(nxt, core))
    arrives("w1", 4 * sum(len(topo.engines(h, core)) for h in helpers_of(T, topo, (rank + 2) % n)))

    def ts(reads, writes, c, out, in0, s1, s2, op0, op1=None):
        if op1 is None:
            op("v", reads, writes, lambda: V.tensor_scalar(out, in0, s1, None, op0), cyc(c))
        else:
            op("v", reads, writes, lambda: V.tensor_scalar(out, in0, s1, s2, op0, op1), cyc(c))

    def cp(reads, writes, cost, out, src):
        op("v", reads, writes, lambda: V.tensor_copy(out, src), cost)

    def tt(reads, writes, cost, out, a, b, o):
        op("v", reads, writes, lambda: V.tensor_tensor(out, a, b, o), cost)

    def scan(reads, writes, c, out, d0, d1, o0, o1):
        op("v", reads, writes, lambda: V.tensor_tensor_scan(out, d0, d1, 0.0, o0, o1), cyc(c))

    def fill(key, c, out, value):
        op("v", [], [key], lambda: V.memset(out, value), cyc(c))

    def act(reads, writes, cost, out, src, func, **kw):
        op("s", reads, writes, lambda: S.activation(out, src, func, **kw), cost)

    def move(q, group, reads, writes, cost, out, src, scale=None, bias=None):
        def call(on):
            if on == "v":
                if scale is not None:
                    return V.tensor_scalar(out, src, scale, None, MUL)
                if bias is not None:
                    return V.tensor_scalar(out, src, bias, None, ADD)
                return V.tensor_copy(out, src)
            if scale is not None:
                return S.activation(out, src, IDENT, scale=scale)
            if bias is not None:
                return S.activation(out, src, IDENT, bias=bias)
            return S.activation(out, src, COPY)
        node(q, reads, writes, call, cost, sem="own", group=group)

    def quant(reads, writes, q, s, a, tile, cols=128):
        op("v", reads, writes, lambda: V.quantize_mx(q[:, a:a + cols], s[:, a:a + cols], tile), fixed(0.012 + 0.00088 * cols))

    def mm(reads, bank, lq, ls, la, rq, rs, ra, cols, start=True, stop=True):
        key = "ps%d" % bank
        op("p", reads, [key], lambda: P.matmul_mx(ps[bank][:, 0:cols], lq[:, la:la + 128], ls[:, la:la + 128],
                                                  rq[:, ra:ra + cols], rs[:, ra:ra + cols], start, stop),
           fixed((cols + 16) * 0.0006), loose=() if start else (key,))

    def send_halo(t):
        name = "halo%d" % t
        rid, pid = topo.addr(prev, core)
        off = topo.engines(core, prev)
        half = len(off) // 2
        pairs = ((bytes_of(qv[t][:, 0:NH]), bytes_of(lq[t][:, 128:128 + NH])), (sv[t][:, 0:QB], ls_[t][:, 128:128 + QB]))
        trs = [RemoteDMATransfer(dst_ids=[DstId(rid=rid, pnc=pid)], dma_engine_mask=mask_of(off[half * i:half * i + half]),
                                 remote_sem=T.sem[name], src=src, dst=dst) for i, (src, dst) in enumerate(pairs)]
        node("g", ["qvA%d" % t, "rest%d" % t], [], lambda _q: g.remote_dma_fused(trs, local_sem=T.sem.sent), fixed(0.4),
             behind=["g", "a" + name])
        sent[0] += 2 * half
        arrives(name, e1, ["a" + name])

    def to_helpers(reads, srcs, dst, sem, engines=spare):
        half = len(spare) // 2
        trs = []
        for i in range(2):
            rid, pid = topo.addr(hs[i], core)
            trs.append(RemoteDMATransfer(dst_ids=[DstId(rid=rid, pnc=pid)], dma_engine_mask=mask_of(engines[half * i:half * i + half]),
                                         remote_sem=sem, src=srcs[i], dst=dst))
        node("g", reads, [], lambda _q: g.remote_dma_fused(trs, local_sem=T.sem.sent), fixed(0.3), behind=["g"])
        sent[0] += 2 * half

    def iota(key, out, pattern, base, c):
        op("g", [], key if isinstance(key, list) else [key],
           lambda: g.iota(out, pattern, base, 0, allow_small_or_imprecise_dtypes=True), fixed(0.13 + 0.0019 * c), behind=["g"])

    def span(name, a, b):
        return ["%s%d" % (name, i) for i in range(a, b)]

    WD = 512 - 2 * HC
    dma("y", "lxa", [], ["xa"], T.xa[:, 0:4 * NH], T.x[:, 0:4 * NH], "x")
    dma("s", "lws0", [], ["ws0"], T.ls[:, 0:WS0], T.ws[:, 0:WS0], "x")
    dma("s", "lst", [], ["sti"], T.si[:], T.st[:], "st")
    dma("y", "lu", [], ["ut"], T.ut[:], T.u[:], "u")
    dma("y", "lxb", [], ["xb", "xbpad"], T.xb[:], T.x[:, 256:768], "xb")
    dma("y", "lwh", [], ["wlh"], bytes_of(T.wl[:, WD:512]), T.wc[:, 4 * WD:2048], 4.4)

    EQ = AluOpType.is_equal
    s0 = WS0 // 2
    op("g", [], ["pi"], lambda: g.iota(T.pi[:], [[0, 1]], 0, 1), fixed(0.13), behind=["g"])
    iota("iw", T.iw[:], [[1, 256]], 0, 256)
    to_helpers(["ws0"], [T.ls[:, 0:s0], T.ls[:, s0:WS0]], T.hs[:, 0:s0], T.sem.hp0, topo.engines(core, prev))
    fill("zApad", 384, T.za[:], 0.0)
    for t in range(2):
        quant(["zApad"], ["rest%d" % t], qv[t], sv[t], 128, T.za[:], QB - 128)
    fill("xapad", 96, T.xa[:, 4 * NH:512], 0.0)
    quant(["xa", "xapad"], ["qvA0"], T.qa, T.sa, 0, T.xa[:, 0:512])
    send_halo(0)
    iota("i36", T.ib[:, 0:4 * MOST], [[32, MOST], [0, 4]], 7, 4 * MOST)
    iota("i8", T.ie[:, 0:32 * MOST], [[0, 4 * MOST], [1, 8]], 0, 32 * MOST)
    dma("y", "lwd", ["i36"], ["wld"], bytes_of(T.wl[:, 0:WD]), T.wc[:, 0:4 * WD], 2.6)
    dma("y", "lws", [], ["wls"], T.ls[:, WS0:512], T.ws[:, WS0:512], 3.2)
    fill("et", 258, T.et[:], 0.0)
    SHR, AND = AluOpType.logical_shift_right, AluOpType.bitwise_and
    for i, (sh, low) in enumerate(((0, 15), (2, 3), (0, 3), (3, 1), (0, 7), (0, 127), (0, 1))):
        ts(["pi"], ["ci%d" % i], 1, T.ci[:, i:i + 1], T.pi[:], sh, low, SHR, AND)
    fill("exa", 120, T.ex[:, 0:960:4], -BIG)
    cp(span("ci", 0, 7), ["cf"], cyc(7), T.cf[:, 0:7], T.ci[:, 0:7])
    fill("exc", 120, T.ex[:, 2:960:4], 0.0)
    fill("exd", 120, T.ex[:, 3:960:4], 0.0)
    fill("dvpad", 24, T.dv[:, 0:PAD], 0.0)
    c_r, c_r4, c_m4, c_hi, c_m8, c_p, c_m2 = [T.cf[:, i:i + 1] for i in range(7)]
    c_lo, c_8m4, c_rho, c_sig, c_r12, c_rp, c_x1 = [T.cx[:, i:i + 1] for i in range(7)]
    c_bias = {x: T.cx[:, 15 + x:16 + x] for x in range(1, DEEP + 1)}
    cp(["iw"], ["ou"], cyc(8), T.ou[:], T.iw[:, 0:128:16])
    ts(["iw", "cf"], ["et"], 128, T.et[:, 3:515:4], T.iw[:, 0:128], c_p, None, EQ)
    ts(["cf"], ["c_rho"], 1, c_rho, c_m4, 3.0, c_r4, MUL, ADD)
    ts(["cf"], ["c_sig"], 1, c_sig, c_hi, 3.0, c_m8, MUL, ADD)
    for b in range(4):
        quant(["et"], ["eq%d" % b], T.eq, T.es, 128 * b, T.et[:, 3 - b:515 - b])

    quant(["ut"], ["uq"], T.uq, T.us, 0, T.ut[:])
    quant(["xb"], ["qvB0"], T.qa, T.sa, QB, T.xb[:])
    for t in range(2):
        quant(["xb"], ["ahead%d" % t], lq[t], ls_[t], 0, T.xb[:])
    cp(["uq", "ou"], ["urq"], gat(128), T.ur[:].bitcast(dt.uint32), T.uq[:].bitcast(dt.uint32).indirect(T.ou[:]))
    act(["uq", "ou"], ["urs"], gat(128), T.ux[:], T.us[:].indirect(T.ou[:]), COPY)
    UR = ["urq", "urs"]
    (a0, c0), (b0, d0) = helper_columns(0)
    (a1, _), (b1, _) = helper_columns(1)
    to_helpers(["wlh"], [bytes_of(T.wl[:, a0:a0 + c0]), bytes_of(T.wl[:, a1:a1 + c0])], bytes_of(T.wh[:, 0:c0]), T.sem.hp1)
    send(["wld"], bytes_of(T.wa[:, 0:WD]), bytes_of(T.wl[:, 0:WD]), T.sem.w0, prev)
    send(["ws0", "wls"], T.sx[:], T.ls[:], T.sem.w0, prev, ["aw0"])
    arrives("w0", 2 * e1 + sum(len(topo.engines(c, core)) for c in helpers_of(T, topo, (rank + 1) % n)), ["aw0"])
    for h in range(NP):
        deep = 2 * max(max(r["find"][h]) for r in ROUNDS if len(r["find"]) > h)
        iota(span("tb%d" % h, 0, deep), T.tb[:, 2 * DEEP * TW * h:2 * DEEP * TW * h + deep * TW], [[0, deep * TW]], 0, deep * TW)
        if h == 0:
            to_helpers(["wld"], [bytes_of(T.wl[:, b0:b0 + d0]), bytes_of(T.wl[:, b1:b1 + d0])], bytes_of(T.wh[:, c0:c0 + d0]), T.sem.hp2)
            to_helpers(["wls"], [T.ls[:, WS0:256 + s0], T.ls[:, 256 + s0:512]], T.hs[:, s0:256], T.sem.hp3)

    def flat(key, out, c, value, reads=()):
        act(["iw"] + list(reads), [key], cyc(c), out, T.iw[:, 0:c], IDENT, scale=0.0, bias=value)

    act(["cf"], ["c_lo"], cyc(1), c_lo, c_hi, IDENT, scale=-1.0, bias=1.0)
    act(["cf"], ["c_8m4"], cyc(1), c_8m4, c_m4, COPY, scale=8.0)
    act(["cf"], ["c_r12"], cyc(1), c_r12, c_r, IDENT, bias=12.0)
    act(["cf"], ["c_rp"], cyc(1), c_rp, c_r, IDENT, bias=float(PAD))
    act(["cf"], ["c_x1"], cyc(1), c_x1, c_m2, IDENT, scale=-2.0, bias=c_r)
    flat("d1e", T.dd[:, 0:344:2], 172, 0.0)
    flat("d1o", T.dd[:, 1:344:2], 172, c_lo, ["c_lo"])
    flat("rr", T.rr[:, 0:TW], TW, 0.0)
    flat("rr", T.rr[:, 0:TW:16], LONG, BIG)
    act(["i8"], ["rs8"], cyc(32 * MOST), T.rs[:, 0:32 * MOST], T.ie[:, 0:32 * MOST], SIGN)
    flat("p1", T.pa[:, 0:TW], TW, -1.0)
    act(["iw"], ["p1"], cyc(LONG), T.pa[:, 15:TW:16], T.iw[:, 31:TW + 16:16], COPY)
    flat("mx-1", T.mx[:, 0:4], 4, 0.0)
    for h, tiles_h in enumerate(((T.za, T.ha), (T.zb, T.hb))):
        c = min(12 * (r["pieces"][h][0][1] - r["pieces"][h][0][0]) for r in ROUNDS if len(r["pieces"]) > h)
        for tile, key in zip(tiles_h, "zh"):
            if key + "AB"[h] != "zA":
                fill("%s%spad" % (key, "AB"[h]), 256 - 2 * c, tile[:, 4 * c:512], 0.0)
    for x in sorted(set(x for p in PARTS for x in p)):
        ts(["c_x1"], ["c_t%d" % x], 1, c_bias[x], c_x1, float(2 * x - 2), 1.0, MIN, ADD)
        ts(["c_t%d" % x], ["c_t%d" % x], 1, c_bias[x], c_bias[x], float(TW), None, MUL)
    same = ROUNDS[0]["find"] == ROUNDS[1]["find"]
    if same:
        nw[1] = nw[0]
    for t in range(1 if same else 2):
        flat("nw%d" % t, nw[t][:], 256, 0.0)
        s = 0
        for part in ROUNDS[t]["find"]:
            a = s
            for x in part:
                if s > 0:
                    act(["iw", "c_t%d" % x], ["nw%d" % t], cyc(16), nw[t][:, 16 * s:16 * s + 16],
                        T.iw[:, 16 * (s - a):16 * (s - a) + 16], IDENT, bias=c_bias[x])
                s += x

    cp(["sti"], ["stu"], cyc(2), T.su[:], T.si[:])
    ts(["iw", "c_rho"], ["c_q"], 4, T.cx[:, 8:12], T.iw[:, 0:16:4], c_rho, None, ADD)
    cp(["iw", "stu"], ["bf"], gat(32), T.bf[:], T.iw[:].indirect(T.su[:]))
    ts(["iw", "c_sig"], ["c_2"], 2, T.cx[:, 12:14], T.iw[:, 1:14:12], c_sig, c_sig, ADD, ADD)
    tt(["bf"], ["nd"], cyc(62), T.nd[:, 0:31], T.bf[:, 1:32], T.bf[:, 0:31], SUB)
    for q in range(2):
        ts(["bf", "c_2"], ["o2%d" % q], 32, T.ot[:, q:64:2], T.bf[:], 2.0, T.cx[:, 12 + q:13 + q], MUL, ADD)
    ts(["nd", "cf"], ["ne"], 31, T.ne[:, 0:31], T.nd[:, 0:31], c_r, 0.0, ADD, MAX)
    for q in range(4):
        ts(["bf", "c_q"], ["oc%d" % q], 32, T.od[:, q:128:4], T.bf[:], T.cx[:, 8 + q:9 + q], 2.0, ADD, MUL)
    ts(["ne"], ["oe"], 31, T.oe[:, 0:31], T.ne[:, 0:31], 28.0, None, MIN)
    ts(["iw", "c_r12"], ["win"], 32, T.wn[:], T.iw[:, 0:32], c_r12, EXCL, EQ, MUL)
    ts(["i8", "cf"], ["m2"], 32 * MOST, T.mk[:, 0:32 * MOST], T.ie[:, 0:32 * MOST], c_m8, None, EQ)
    ts(["i36", "c_8m4"], ["ob"], 4 * MOST, T.ob[:, 0:4 * MOST], T.ib[:, 0:4 * MOST], c_8m4, None, ADD)
    ts(["bf", "cf"], ["ow"], 32, T.ow[:], T.bf[:], c_r, None, ADD)
    for e in range(4):
        ts(["ow"], ["of%d" % e], 32, T.of[:, 2 * e:256:8], T.ow[:], 2.0, 6.0 * e, MUL, ADD)
    for t in range(2):
        act(["iw", "ow", "c_rp"], ["pw%d" % t], gat(256), T.pw[:, 256 * t:256 * t + 256],
            T.iw[:].indirect(T.ow[:, 16 * t:16 * t + 16]), IDENT, scale=4.0, bias=c_rp)
        first = T.pw[:, 256 * t:256 * t + 1]
        x = ROUNDS[t]["find"][0][0]
        cp(["c_t%d" % x], ["ch%d" % t], cyc(1), ch[t][:, 0:1], c_bias[x])
        cp(["pw%d" % t], ["seg%d_0" % t], cyc(1), ch[t][:, 1:2], first)
        ts(["iw", "pw%d" % t], ["oz%d" % t], 4, og[t][0][:, 0:4], T.iw[:, 0:64:16], first, -16.0 - PAD, ADD, ADD)

    piece = [{"A": (0, NH, 0, 0), "B": (NH, 192 - NH, QB, NH - 64), "H": (NA + NB, NH, NH, 48)},
             {"A": (0, NA, 0, 0), "B": (NA, NB, QB, 0), "H": (NA + NB, NH, NH, 48)}]

    def window_keys(t, k):
        return ["ahead%d" % t, "halo%d" % t] if k == "H" else ["qv%s%d" % (k, t)]

    def side(t, k):
        return (lq[t], ls_[t]) if k == "H" else (qv[t], sv[t])

    def plain(t, k, bank, group):
        j0, c, _, r0 = piece[t][k]
        c = min(c, 262 - j0)
        move("s", group, ["ps%d" % bank], ["n" + k], cyc(c), T.ia[:, 2 * j0:2 * (j0 + c):2], ps[bank][:, r0:r0 + c])

    def masked(t, k, bank, q, group):
        j0, c, _, r0 = piece[t][k]
        a, b = max(j0, 8), min(j0 + c, 270)
        move(q, group, ["cf", "ps%d" % bank], ["m" + k], cyc(b - a), T.ia[:, 2 * (a - 8) + 1:2 * (b - 8):2],
             ps[bank][:, r0 + a - j0:r0 + b - j0], scale=c_hi)

    def scores(t, k, banks):
        for bank in sorted(set(banks)):
            mm(UR + window_keys(t, k), bank, T.ur, T.ux, 0, side(t, k)[0], side(t, k)[1], piece[t][k][2], 128)
        plain(t, k, banks[0], "e%d%s%d" % (t, k, banks[0]))
        masked(t, k, banks[1], "s" if banks[0] == banks[1] else "v", "e%d%s%d" % (t, k, banks[1]))

    def shift(a, b, reads, key):
        scan(reads + ["d1e", "d1o"], [key], 2 * (b - a), T.ta[:, 2 * a:2 * b], T.dd[:, 0:2 * (b - a)], T.ia[:, 2 * a:2 * b], MUL, ADD)

    def decode(t, k, banks):
        j0, c, ra, r0 = piece[t][k]
        for b in range(4):
            mm(["eq%d" % b] + window_keys(t, k), banks[b], T.eq, T.es, 128 * b, side(t, k)[0], side(t, k)[1], ra, 128)
            move("s", "dv%d%s%d" % (t, k, b), ["ps%d" % banks[b]], ["dv%s%d" % (k, b)], cyc(c),
                 T.dv[:, PAD + 4 * j0 + b:PAD + 4 * (j0 + c):4], ps[banks[b]][:, r0:r0 + c], scale=0.5)

    DV = ["dvpad"] + ["dv%s%d" % (k, b) for k in "ABH" for b in range(4)]
    I1 = ["nA", "nB", "nH", "mA", "mB", "mH"]
    T1 = ["t1a", "t1b", "t1c", "rest1"]

    def distances(t):
        c0, held = 64 * t + 4, {}
        move("s", "ex%d" % t, ["win", "oe"], ["exb"], gat(240), T.ex[:, 1:960:4], T.wn[:].indirect(T.oe[:, 16 * t:16 * t + 15]))
        for i, j in runs(ROUNDS[t]["temp"]):
            d = j - i
            tt(T1 + ["o20", "o21", "m2"], span("g2", i, j), gat(32 * d), T.gg[:, 32 * i:32 * j],
               T.ta[:, 24:524].indirect(T.ot[:, 32 * t + 2 * i:32 * t + 2 * j]), T.mk[:, 0:32 * d], MUL)
            scan(span("g2", i, j) + ["rs8"], span("tt", i, j), 32 * d, T.tt[:, 32 * i:32 * j], T.rs[:, 0:32 * d], T.gg[:, 32 * i:32 * j], MUL, ADD)
            held.update({s: (i, j) for s in range(i, j)})
        for i, j in runs(ROUNDS[t]["dist"]):
            d = j - i
            u, v = held[i]
            if i >= ROUNDS[t]["alone"]:
                made = []
                for s in range(i, j):
                    for e in range(4):
                        c = 128 * t + 8 * s + 8 + 2 * e
                        made.append("ab%d_%d" % (s, e))
                        act(I1 + ["of%d" % e, "tt%d" % s], made[-1:], gat(16), T.ab[:, 64 * s + e:64 * s + 64:4],
                            T.ia[:].indirect(T.of[:, c:c + 1]), ABS, scale=-1.0, bias=T.tt[:, 32 * s + 8 * e + 7:32 * s + 8 * e + 8])
                scan(made + ["exa", "exb", "exc", "exd"], span("mx", i, j), 64 * d,
                     T.mx[:, 4 + 64 * i:4 + 64 * j], T.ex[:, 64 * i:64 * j], T.ab[:, 64 * i:64 * j], ADD, MAX)
                continue
            move("s", "cc%d%d" % (t, i), I1 + span("oc", 0, 4), span("cc", i, j), gat(64 * d), T.cc[:, 64 * i:64 * j],
                 T.ia[:].indirect(T.od[:, c0 + 4 * i:c0 + 4 * j]))
            tt(span("tt", u, v) + ["ob"] + span("cc", i, j), span("df", i, j), gat(64 * d), T.df[:, 64 * i:64 * j],
               T.tt[:, 32 * u:32 * v].indirect(T.ob[:, 4 * (i - u):4 * (j - u)]), T.cc[:, 64 * i:64 * j], SUB)
            act(span("df", i, j), span("ab", i, j), cyc(64 * d), T.ab[:, 64 * i:64 * j], T.df[:, 64 * i:64 * j], ABS)
            scan(span("ab", i, j) + ["exa", "exb", "exc", "exd"], span("mx", i, j), 64 * d,
                 T.mx[:, 4 + 64 * i:4 + 64 * j], T.ex[:, 64 * i:64 * j], T.ab[:, 64 * i:64 * j], ADD, MAX)

    def search(t, h):
        part = ROUNDS[t]["find"][h]
        a, b = runs([sum(p) for p in ROUNDS[t]["find"]])[h]
        k, name = b - a, "%d%d" % (t, h)
        scan(["rr"] + span("mx", a - 1, b), span("mm", a, b), 16 * k, T.mm[:, 16 * a:16 * b], T.mx[:, 64 * a + 3:64 * b:4],
             T.rr[:, 0:16 * k], MIN, MAX)
        tt(span("mx", a, b) + span("mm", a, b), span("nn", a, b), cyc(32 * k), T.nn[:, 16 * a:16 * b], T.mx[:, 64 * a + 7:64 * b + 4:4],
           T.mm[:, 16 * a:16 * b], AluOpType.is_ge)
        scan(span("nn", a, b) + ["p1"], span("pt", a, b), 8 * k, T.pt[:, 16 * a:16 * b], T.nn[:, 16 * a:16 * b], T.pa[:, 0:16 * k], MUL, ADD)
        ob, t0 = 2 * a, 2 * DEEP * TW * h
        cp(span("pt", a, b), ["op%d" % h], cyc(k), T.op[:, ob:ob + k], T.pt[:, 16 * a + 15:16 * b:16])
        tb, need = T.tb, tables_of(a, part)
        for x, kind in sorted(need):
            i, j = need[(x, kind)]
            i -= (i - a) % 2
            at = t0 + TW * (2 * x - 2 + kind)
            if x == 1:
                src, key = ((T.pw[:, 256 * t + 16 * a:256 * t + 16 * b + 16], "pw%d" % t),
                            (nw[t][:, 16 * a:16 * b + 16], "nw%d" % (0 if same else t)))[kind]
            else:
                src, key = tb[:, at - 2 * TW:at - TW], "tb%d%d" % (h, 2 * x - 4 + kind)
            move("sv"[kind], "tf%s%d%d" % (name, x, kind), [key, "op%d" % h], ["tb%d%d" % (h, 2 * x - 2 + kind)], gat(16 * (j - i)),
                 tb[:, at + 16 * (i - a):at + 16 * (j - a)], src.indirect(T.op[:, ob + i - a:ob + j - a]))
        s = a
        for x in part:
            cp(span("tb%d" % h, 0, 2 * x) + ["ch%d" % t], ["ch%d" % t] + span("seg%d_" % t, s + 1, s + x + 1), gat(16),
               ch[t][:, 2 * s + 2:2 * s + 18], tb[:, t0:t0 + 2 * x * TW].indirect(ch[t][:, 2 * s:2 * s + 1]))
            s += x
        if b == 15:
            ts(span("seg%d_" % t, 0, 16), ["pp%d" % t], 16, T.pp[:, 16 * t:16 * t + 16], ch[t][:, 1:32:2], -float(PAD), 0.25, ADD, MUL)

    def cuts(a, b, parts, more):
        marks = [a] + [min(b, a + ((b - a) * i // parts // 2) * 2 + more) for i in range(1, parts)] + [b]
        return [(u, v) for u, v in zip(marks, marks[1:]) if v > u]

    def overlap(t, h):
        (s0, s1), lap, _ = ROUNDS[t]["pieces"][h]
        o, z, k = og[t][h], (T.za, T.zb)[h], "AB"[h]
        lead = 4 if h == 0 else 0
        j0 = 3 * s0 + 4 - lead
        keys = []
        for sa, sb, calls in lap:
            u, v = lead + 3 * (sa - s0), lead + 3 * (sb - s0)
            made = span("og%d%d%d_" % (t, h, sa), 0, 3)
            for m in range(3):
                ts(span("seg%d_" % t, sa, sb), [made[m]], sb - sa, o[:, u + m:v:3], ch[t][:, 2 * sa + 1:2 * sb:2], 16.0 * m, None, ADD)
            first = 0 if sa == 0 else u
            for a, b in cuts(first, v - 3 * (sb == 16), calls, 0):
                move("s", "tn%d%d%d" % (t, h, a), DV + made + ["oz%d" % t], span("tn", j0 + a, j0 + b), gat(16 * (b - a)),
                     T.tn[:, 16 * (j0 + a):16 * (j0 + b)], T.dv[:, PAD:].indirect(o[:, a:b]))
            for a, b in cuts(u, v, calls, 0 if sa == 0 else 2):
                keys.append("z%s%d" % (k, len(keys)))
                tt(DV + made + span("tn", j0 + a - 3, j0 + b - 3), keys[-1:], gat(16 * (b - a)),
                   z[:, 16 * (a - lead):16 * (b - lead)], T.dv[:].indirect(o[:, a:b]), T.tn[:, 16 * (j0 + a - 3):16 * (j0 + b - 3)], ADD)
        return keys

    tiles = ((T.za, T.ha, T.xa), (T.zb, T.hb, T.xb))

    def unload(tile, key, t, c, bank0, scale):
        for b in range(4):
            move("sv"[b % 2], "%s%d%d" % (key, t, b), ["ps%d" % (bank0 + b)], ["%s%d" % (key, b)], cyc(c),
                 tile[:, b:4 * c:4], ps[bank0 + b][:, 0:c], scale=scale)

    def columns(t, h):
        s0, s1 = ROUNDS[t]["pieces"][h][0]
        return 12 * s0, 12 * (s1 - s0), max(128, 12 * (s1 - s0))

    def layer(t, h, zs):
        z, hh, x = tiles[h]
        k, a = "AB"[h], 128 * h
        j0, c, w = columns(t, h)
        r0, x0 = ROUNDS[t]["pieces"][h][2]
        quant(zs + ["z%spad" % k], ["qz" + k], T.qz, T.sz, a, z[:, 0:4 * w], w)
        for b in range(4):
            mm(["qz" + k, "w%d" % t], r0 + b, wc[t], wsc[t], 128 * b, T.qz, T.sz, a, w)
        if r0 == x0:
            unload(hh, "h" + k, t, c, r0, 0.03125)
        for b in range(4):
            mm(["qz" + k, "eq%d" % b], x0 + b, T.eq, T.es, 128 * b, T.qz, T.sz, a, w, True, False)
        if r0 != x0:
            unload(hh, "h" + k, t, c, r0, 0.03125)
        quant(span("h" + k, 0, 4) + ["h%spad" % k], ["qh" + k], T.qh, T.sh, a, hh[:, 0:4 * w], w)
        for b in range(4):
            mm(["qh" + k, "eq%d" % b], x0 + b, T.eq, T.es, 128 * b, T.qh, T.sh, a, w, False, True)
        name = "x" + k.lower()
        keys = span(name, 0, 4)
        if t == 0:
            for key in keys:
                readers[key] = list(readers.get(name, []))
        unload(x, name, t, c, x0, None)
        quant(keys + [name + "pad"], ["qv%s%d" % (k, t + 1)] + ["qc"] * t, qv[t + 1], sv[t + 1], j0 if t else QB * h, x[:, 0:4 * w], w)

    def store(h, last):
        j0, c, w = columns(1, h)
        k, bank = "AB"[h], ROUNDS[1]["pieces"][h][2][0]
        key = ["qv%s2" % k, "qc"]
        mm(key + ["vq"], bank, T.vq, T.vs, 0, T.qc, T.sc, j0, w)
        dma("y", "sta", key[:1], [], T.oc[:, 4 * j0:4 * (j0 + c)], bytes_of(T.qc[:, j0:j0 + c]), STORE)
        if last:
            for i in range(4):
                dma("y", "sta", key, [], T.osc[4 * i:4 * i + 4, :], T.sc[32 * i:32 * i + 4, 0:192], STORE)
        move("sv"[h], "y" + k, ["ps%d" % bank], ["y" + k], cyc(c), T.yb[:, j0:j0 + c], ps[bank][:, 0:c])
        dma("s" if last else "y", "stb" if last else "sta", ["y" + k], [], T.y[:, j0:j0 + c], T.yb[:, j0:j0 + c], STORE)

    scores(0, "A", (0, 0))
    scores(0, "B", (1, 1))
    shift(12, 184, ["nA", "nB", "mA", "mB"], "t1a")
    decode(0, "A", (4, 5, 6, 7))
    decode(0, "B", (4, 5, 6, 7))
    scores(0, "H", (2, 3))
    shift(184, 262, ["nB", "nH", "mH"], "t1b")
    decode(0, "H", (4, 5, 6, 7))
    distances(0)
    for h in range(len(ROUNDS[0]["find"])):
        search(0, h)
    layer(0, 0, overlap(0, 0))
    send_halo(1)
    dma("y", "lv", ["halo1"], ["vt"], T.vt[:], T.v[:], 2.5)
    quant(["vt"], ["vq"], T.vq, T.vs, 0, T.vt[:])
    zs = overlap(0, 1)
    scores(1, "A", (0, 0))
    shift(12, 76, ["nA", "mA"], "t1a")
    decode(1, "A", (1, 2, 3, 0))
    layer(0, 1, zs)
    scores(1, "B", (4, 5))
    shift(76, 184, ["nA", "nB", "mB"], "t1c")
    scores(1, "H", (0, 1))
    shift(184, 262, ["nB", "nH", "mH"], "t1b")
    decode(1, "B", (6, 7, 4, 5))
    decode(1, "H", (2, 3, 0, 1))
    distances(1)
    for h in range(len(ROUNDS[1]["find"])):
        search(1, h)
    last = len(ROUNDS[1]["pieces"]) - 1
    for h in range(last + 1):
        zs = overlap(1, h)
        if h == last:
            dma("y", "sta", ["pp0", "pp1"], [], T.ol[:], T.pp[0:128:16, :], STORE)
        layer(1, h, zs)
        store(h, h == last)

    if "plan" not in PLANNED:
        PLANNED["plan"] = schedule(nodes)
    seq, queue, _ = PLANNED["plan"]
    count, token, place, behind = {"sent": sent[0]}, {}, {}, {}
    known = {q: {} for q in Q}

    def need(q, s, c):
        if known[q].get(s, 0) < c:
            Q[q].wait_ge(T.sem[s], c)
            known[q][s] = c
            for k, v in behind.get((s, c), {}).items():
                known[q][k] = max(known[q].get(k, 0), v)

    for i in seq:
        nd, q = nodes[i], queue[i]
        s = own[q] if nd["sem"] == "own" else nd["sem"]
        if q:
            toks = {}
            for j in nd["hard"]:
                toks[token[j][0]] = max(toks.get(token[j][0], 0), token[j][1])
            for k in sorted(toks, key=lambda k: -place[(k, toks[k])]):
                need(q, k, toks[k])
            call = nd["call"](q)
            if s:
                call.then_inc(T.sem[s], nd["inc"])
        if s:
            count[s] = count.get(s, 0) + nd["inc"]
            token[i] = (s, count[s])
            place[token[i]] = len(place)
            if nd["sem"] == "own":
                behind[token[i]] = dict(known[q])
    for s in sorted(count):
        need("g", s, count[s])
